import numpy as np, ml_dtypes
CORES = [40,64,80,88,96,104,120,144]
N = 8
BF = ml_dtypes.bfloat16
def gentries(a):
    return np.ascontiguousarray(a.reshape(8, 16, -1).transpose(0, 2, 1)).reshape(8, -1)
def gtable(e):
    e = np.asarray(e); return np.ascontiguousarray(e.reshape(8, -1, 16).transpose(0, 2, 1)).reshape(128, -1).astype(np.int32)
W, H, L, CAP, RO = 1280, 512, 256, 192, 3
def pick(t, e):
    return np.take_along_axis(t, e[:, None, :], 2)
def at(x, c):
    return pick(x, c.reshape(8, -1)).reshape(8, 16, 16, -1)
def moved(v, dl):
    return np.clip(v + dl[:, :, None, :], 0, 63)
def spot(u):
    return (((u * u) >> 5) + 37 * u) & (H - 1)
def parts(rng):
    x = rng.integers(0, 64, (N, 8, 16, W)); su = rng.integers(0, W, (N, 8, 16, W)); co = np.argsort(rng.random((N, 8, 16, W)), axis=-1)
    dl = rng.integers(-20, 21, (N, 8, 16, L)); la = rng.integers(0, W, (N, 8, L)); lb = rng.integers(0, W, (N, 8, L))
    wt = rng.integers(0, 256, (N, 8, 16)); th = 110 + 20 * np.argsort(rng.random((N, 8)), axis=-1) + rng.integers(0, 20, (N, 8))
    return x, su, co, dl, la, lb, wt, th
def pack(x, su, co, dl, la, lb, wt, th):
    fl = lambda a, n: np.ascontiguousarray(np.asarray(a).reshape(N, 128, n)).astype(np.float32).astype(BF)
    it = lambda a: np.ascontiguousarray(np.asarray(a).reshape(N, 128, W)).astype(np.int32)
    return {"x0": fl(x, W), "su": it(su), "co": it(co), "dl": fl(dl, L), "la": np.stack([gtable(a) for a in la]), "lb": np.stack([gtable(a) for a in lb]),
            "wt": fl(wt, 1), "th": np.asarray(th).reshape(N, 8, 1).astype(np.int32)}
def put(p, c, v):
    w = np.argmax(p == v[..., None], axis=-1); old = p[..., c].copy()
    np.put_along_axis(p, w[..., None], old[..., None], -1); p[..., c] = v
def two(rng, n):
    c = rng.integers(0, 3, (N, 8, 1, n)); return np.where(c < 2, c, rng.integers(0, 2, (N, 8, 16, n)))
def spots(dl, wt):
    return spot(np.sum(63 * wt[:, :, None] * (dl > 0), axis=1) & 4095)
def setup_inputs(rng):
    return pack(*parts(rng))
def setup_inputs_spread(rng):
    x, su, co, dl, la, lb, wt, th = parts(rng)
    p = np.exp2(rng.integers(-2, 3, (N, 8, 1, W))); x = np.minimum((64 * rng.random((N, 8, 16, W)) ** p).astype(np.int64), 63)
    p = np.exp2(rng.integers(-2, 3, (N, 8, 1, W))); su = np.minimum((W * rng.random((N, 8, 16, W)) ** p).astype(np.int64), W - 1)
    dl = np.rint((2 * rng.random((N, 8, 16, L)) - 1) * rng.choice(np.array([0, 1, 3, 9, 27, 63]), (N, 8, 1, L))).astype(np.int64)
    la = np.minimum((W * rng.random((N, 8, L)) ** 2).astype(np.int64), W - 1); lb = W - 1 - np.minimum((W * rng.random((N, 8, L)) ** 2).astype(np.int64), W - 1)
    wt = np.minimum(np.exp2(8 * rng.random((N, 8, 16))).astype(np.int64), 256) - 1
    th = np.where(rng.random((N, 8)) < 0.5, np.minimum(np.exp2(10 * rng.random((N, 8))).astype(np.int64), 1024) - 1, rng.integers(100, 300, (N, 8)))
    return pack(x, su, co, dl, la, lb, wt, th)
def setup_inputs_ends(rng):
    x, su, co, dl, la, lb, wt, th = parts(rng)
    x = 63 * two(rng, W); su = (W - 1) * two(rng, W); dl = 126 * two(rng, L) - 63
    la = (W - 1) * rng.integers(0, 2, (N, 8, L)); lb = (W - 1) * rng.integers(0, 2, (N, 8, L)); la[:, :, L - 1] = W - 1; lb[:, :, 0] = 0
    wt = 255 * rng.integers(0, 2, (N, 8, 16)); wt[:, 0] = 255 * (np.arange(16) & 1); wt[:, 7] = 255
    th = 1023 * rng.integers(0, 2, (N, 8)); th[:, 0] = 1023; th[:, 1] = 0; th[:, 7] = 0; th[0, 6] = 1023
    z = rng.integers(0, 2, (N, 8, 16)); z[:, :, 0] = 1; z[:, :, 15] = 0
    put(co, 0, (W - 1) * z); put(co, W - 1, (W - 1) * (1 - z))
    dl[:, 7] = np.where(rng.random((N, 1, L)) < 0.5, 63, -63); dl[:, 7, :, 0] = 63; dl[:, 7, :, 1] = -63; dl[:, 7, :, L - 1] = 63
    x[:, 7, :, 0] = 0; x[:, 7, :, W - 1] = 0; x[:, 7, :, spot((16 * 63 * 255) & 4095)] = 0
    x[:, 6, :, 0] = 63; x[:, 6, :, W - 1] = 63; dl[:, 6, :, 0] = -63; dl[:, 6, :, L - 1] = -63
    return pack(x, su, co, dl, la, lb, wt, th)
def setup_inputs_corners(rng):
    x, su, co, dl, la, lb, wt, th = parts(rng); th[:] = 0; dl = 126 * rng.integers(0, 2, (N, 8, 16, L)) - 63
    for r in range(N):
        own = spots(dl[r], wt[r]); come = spots(dl[r - 1], wt[r])
        for i in range(8):
            p = np.unique(own[i]); z = p[:0]
            if i % 2: z = p; p = np.setdiff1d(come[i], z)
            n = int(rng.choice(np.array([0, 1, CAP - 1, CAP, CAP + 1, W - H])))
            if r in (0, N - 1): n = (CAP, CAP, CAP + 1, CAP + 1, CAP - 1, CAP - 1, 0, 1)[i]
            if r == 1 and i in (2, 6): n = W - H
            n = min(n, 16 * len(p), W - H)
            a = np.concatenate([z, p]); s = np.stack([rng.permutation(H)[:len(a)] for k in range(16)])
            c = s[:, len(z):].copy().reshape(-1); c[rng.permutation(len(c))[:n]] = H + rng.permutation(W - H)[:n]
            s[:, len(z):] = c.reshape(16, -1)
            rest = np.ones(W, bool); rest[a] = False
            for k in range(16):
                free = np.ones(W, bool); free[s[k]] = False
                co[r, i, k, a] = s[k]; co[r, i, k, rest] = rng.permutation(np.flatnonzero(free))
    return pack(x, su, co, dl, la, lb, wt, th)
def setup_inputs_crowd(rng):
    x, su, co, dl, la, lb, wt, th = parts(rng)
    dl[:, :2] = 126 * rng.integers(0, 2, (N, 2, 16, L)) - 63
    for i in range(8):
        m = (1, 1, 2, 1, 4, 1, 2, 1)[i]; s = rng.integers(0, m, L); z = int(rng.integers(1, L - 1))
        if i % 2: s[z] = m
        la[:, i] = la[:, i][:, s]; lb[:, i] = lb[:, i][:, s]; dl[:, i] = dl[:, i][:, :, s]
    for r in range(N):
        n = spots(dl[r], wt[r])
        put(co[r, 0], int(n[0, 0]), np.full(16, W - 1)); put(co[r, 1], int(n[1, 0]), np.full(16, H))
        if r % 3 < 2: th[r] = 0
        if r % 3 == 0: dl[r, 5, :, L - 1] = 0; lb[r, 5, L - 1] = la[r, 5, L - 1]
        if r % 3 == 1: th[r, 3] = 1; dl[r, 3, :, L - 1] = 0; lb[r, 3, L - 1] = la[r, 3, L - 1]
    return pack(x, su, co, dl, la, lb, wt, th)
def setup_inputs_ties(rng):
    x, su, co, dl, la, lb, wt, th = parts(rng)
    x = 8 * (x >> 4); x[:, 1::2] = 63 - x[:, 1::2]; dl = 8 * rng.integers(-1, 2, (N, 8, 16, L))
    x[:, 3] = 63; x[:, 3, :7] = 62 + np.minimum(rng.integers(0, 4, (N, 7, W)), 1); dl[:, 3] = -63; dl[2, 3, :, 48:] = 0
    put(co[2, 3], 0, H + np.arange(16)); su[2, 3, :, H:H + 16] = H + ((np.arange(16) + 1) & 15)
    su[:, ::2, :, :W // 2] = su[:, ::2, :1, :W // 2].copy()
    la[:, :, 16:32] = la[:, :, :16].copy(); lb[:, :, 16:32] = lb[:, :, :16].copy(); dl[:, :, :, 16:32] = dl[:, :, :, :16].copy()
    lb[:, :, 32:48] = la[:, :, 32:48].copy(); dl[:, :, :, 32:48] = 0
    for r in range(N):
        dd = np.sum(np.abs(at(x[r], pick(co[r], lb[r])) - moved(at(x[r], pick(co[r], la[r])), dl[r])), axis=1)
        th[r] = np.sort(np.min(dd, axis=1), axis=1)[:, L // 2]; th[r, 4:] += rng.integers(0, 2, 4)
        if r == 2: th[r] = 1023; th[r, 3] = np.min(dd[3, :, :32])
    return pack(x, su, co, dl, la, lb, wt, th)
def check_inputs(d):
    bad = []
    for k, lo, hi in (("x0", 0, 63), ("su", 0, W - 1), ("co", 0, W - 1), ("dl", -63, 63), ("la", 0, W - 1), ("lb", 0, W - 1), ("wt", 0, 255), ("th", 0, 1023)):
        a = np.asarray(d[k]).astype(np.float64)
        if not (np.min(a) >= lo and np.max(a) <= hi): bad.append("range of " + k)
        if np.any(a != np.floor(a)): bad.append("whole numbers of " + k)
    if np.any(np.sort(np.asarray(d["co"]), axis=-1) != np.arange(W)): bad.append("a row of co holds every node once")
    return bad
def reference(x0, su, co, dl, la, lb, wt, th):
    x = x0.astype(np.float32).astype(np.int32).reshape(N, 8, 16, W); s = su.astype(np.int64).reshape(N, 8, 16, W); c = co.astype(np.int64).reshape(N, 8, 16, W)
    sh = dl.astype(np.float32).astype(np.int32).reshape(N, 8, 16, L); w = wt.astype(np.float32).astype(np.int32).reshape(N, 8, 16, 1, 1); lim = th.astype(np.int64).reshape(N, 8, 1)
    a = np.stack([gentries(v) for v in la]).astype(np.int64); b = np.stack([gentries(v) for v in lb]).astype(np.int64)
    flag = np.zeros((N, 8, W), bool); last = np.zeros(N, np.int64)
    for t in range(RO):
        for r in range(N):
            q = (r - t) % N
            d = pick(c[r], a[q]); f = pick(c[r], b[q])
            dist = np.sum(np.abs(at(x[r], f) - moved(at(x[r], d), sh[q])), axis=1)
            k = np.argmin(dist, axis=1)[:, None, :]
            dk = np.take_along_axis(d, k, 1)[:, 0]; fk = np.take_along_axis(f, k, 1)[:, 0]
            same = np.take_along_axis(dist, k, 1)[:, 0] < lim[r] + (last[r] & 63)
            e = moved(at(x[r], pick(s[r], dk)), sh[q])
            n = spot(np.sum(w[r] * e, axis=1).astype(np.int64) & 4095)
            j = np.argmax(np.sum(np.abs(at(x[r], n) - e), axis=1), axis=1)[:, None, :]
            nj = np.take_along_axis(n, j, 1)[:, 0]; ej = np.take_along_axis(e, j[:, None], 2)[:, :, 0]
            for i in range(8):
                lane = np.flatnonzero(~same[i]); place, first = np.unique(nj[i, lane], return_index=True)
                x[r, i][:, place] = ej[i][:, lane[first]]
                flag[r, i, c[r, i][:, place].reshape(-1)] = True; flag[r, i, :H] = False
                v = np.flatnonzero(flag[r, i])[:CAP]
                z = x[r, i][:, s[r, i][:, v]]
                x[r, i][:, v] = (np.max(z, axis=1) + np.min(z, axis=1)) >> 1
                flag[r, i, v] = False
            last[r] = np.sum(~same)
            a[q] = np.where(same, dk, a[q]); b[q] = np.where(same, fk, b[q])
    return {"yx": x.reshape(N, 128, W).astype(np.float32).astype(BF), "ya": np.stack([gtable(a[(r - RO + 1) % N]) for r in range(N)]).astype(np.float32),
            "yb": np.stack([gtable(b[(r - RO + 1) % N]) for r in range(N)]).astype(np.float32)}

@@ -1,0 +1,632 @@
+from concourse.mybir import dt, AluOpType, AxisListType, ActivationFunctionType
+A = AluOpType
+F = ActivationFunctionType
+B2, F4, I4, U2, H2 = "bfloat16", "float32", "int32", "uint16", "float16"
+SB = lambda w, d: ("sbuf", [128] + w, d)
+CH = [(0, 8), (8, 8)]
+NC = len(CH)
+QM = max(q for _, q in CH)
+VFUSED = ((1, 1, 0), (1, 1, 1), (2, 0, 0), (2, 1, 0))
+VFLAG = (2, 8)
+VREP = (6, 0, 4)
+VREN = 1
+SCRATCH = {}
+
+
+def declare(d, **kw):
+    for names, w in kw.items():
+        for n in names.split("_"):
+            SCRATCH[n] = SB(list(w), d)
+
+
+declare(B2, xw=[1536], wtb=[1], dl0_dl1_dl2_rdl=[256], rep0_rep1_rep2=[4096], blk_rge_tri_trx_idb_idn_oneb_kc2_kc3=[128],
+        lr_ww=[16, 128], rx_rn_fsb=[768], t0_t1_mb0_mb1_g0_g1=[1024], e=[4096], upb=[48], fv=[1536], gr_mx_mn=[3072])
+declare(I4, coe_sue=[1536], lai=[32], thi_pi=[1], pr=[3], di_dm2=[32], ai=[2], ui_ua_ub_uc_un=[16 * QM], i2=[3 * QM], si=[192])
+declare(U2, ab0_ab1_ab2_rab1_rab2_abo1_abo2=[32], df=[512], dlist_ne16_nw16_eo16=[16], c16=[16 * QM], pos=[48], vl=[12], sv=[192])
+declare(F4, abf_abn_abd_df32_al=[32], pf=[4], opar_thf_thq_thr_asum_tha=[1], rowg_dif_e8_onef=[128], rowr_kc1_dT=[512], it=[1536],
+        rmin_rmax=[32 * QM], q16_lcol_dump_ebase_ald_nef=[16], v48_dv_dv1_z48_up0_fl_r0_r1_r2_r3_r4=[48], dm_sm_cmm_cms_sm2=[192], kd_kk_kk2_zf=[32 * QM],
+        sma=[3 * QM], smb=[QM], fs0_fs1=[1536], cmp=[960])
+declare(H2, m00_m01_m10_m11=[128], dfh_ta=[16, 2, 16], nh_na=[QM // 2, 2, 16], nr=[16 * QM])
+for _c, (_q0, _q) in enumerate(CH):
+    SCRATCH["a%d" % _c] = SB([_q, 16, 16], B2)
+    for _n in ("s16%d", "n16%d"):
+        SCRATCH[_n % _c] = SB([16 * _q], U2)
+    SCRATCH["ct%d" % _c] = SB([16, _q], U2)
+    SCRATCH["ew%d" % _c] = SB([16 * _q], B2)
+    SCRATCH["eq%d" % _c] = SB([_q * (16 * _q + 2)], B2)
+    SCRATCH["cwi%d" % _q] = SB([_q * (16 * _q + 2)], F4)
+    SCRATCH["cw%d" % _q] = SB([_q * (16 * _q + 2)], B2)
+SCRATCH["we"] = SB([QM * (16 * QM + 2)], B2)
+for _n in ("py0", "py1"):
+    SCRATCH[_n] = ("psum", [128, 32, 2, 16], F4)
+for _n in ("kp0", "kp1", "ps0", "ps1"):
+    SCRATCH[_n] = ("psum", [128, 512], F4)
+
+PACK = {}
+
+
+def pack(buf, d, names):
+    n = 0
+    for x in names.split():
+        w = SCRATCH.pop(x)[1][1]
+        PACK[x] = (buf, n, w)
+        n += w + w % 2
+    SCRATCH[buf] = SB([n], d)
+
+
+pack("pkf", F4, "pf opar thf thq thr asum tha q16 lcol dump ebase ald nef v48 dv dv1 z48 up0 fl r0 r1 r2 r3 r4 sma smb abf abd df32 al")
+pack("pki", I4, "pi pr di dm2 ai i2")
+pack("pku", U2, "dlist ne16 nw16 eo16 pos vl")
+SEMAPHORES = ["cv", "cs", "ct", "cg", "ls", "rdl", "rab1", "rab2", "adl1", "adl2", "aab1", "aab2", "ox"] + ["ld%d" % n for n in range(16)] + ["o%d" % n for n in range(8)]
+SIZE = {B2: 2, F4: 4, I4: 4, U2: 2, H2: 2}
+INFO = {}
+
+
+def relay_of(src, dst, topo):
+    if topo.may_write(src, dst):
+        return None
+    c = [x for x in topo.cores_of(src) if x != src and topo.may_write(x, dst)]
+    c.sort(key=lambda x: (topo.die(x) != topo.die(src), x))
+    return c[0]
+
+
+def send(g, T, topo, src, dst, out, in_, rsem):
+    rid, pid = topo.addr(dst, src)
+    g.remote_dma(out, in_, T.sem[rsem], T.sem.ls, pid, rid, topo.mask(src, dst))
+    return len(topo.engines(src, dst))
+
+
+def relay_program(g, core, T, topo, src):
+    i = T.rank_of(src)
+    d1, d2 = T.cores[(i + 1) % 8], T.cores[(i + 2) % 8]
+    n1 = relay_of(src, d1, topo) == core
+    n2 = relay_of(src, d2, topo) == core
+    k = len(topo.engines(src, core))
+    n = 0
+    g.wait_ge(T.sem.rdl, k)
+    if n1:
+        n += send(g, T, topo, core, d1, T.dl1[:], T.rdl[:], "adl1")
+    if n2:
+        n += send(g, T, topo, core, d2, T.dl2[:], T.rdl[:], "adl2")
+    if n1:
+        for t in (1, 2):
+            g.wait_ge(T.sem["rab%d" % t], k)
+            n += send(g, T, topo, core, d1, T["ab%d" % t][:], T["rab%d" % t][:], "aab%d" % t)
+    g.wait_ge(T.sem.ls, n)
+
+
+def s_(a, b, c=None):
+    return slice(a, b, c)
+
+
+def rank_program(g, core, T, topo):
+    rank = T.rank_of(core)
+    if rank is None:
+        for src in T.cores:
+            if core in topo.cores_of(src):
+                i = T.rank_of(src)
+                if core in [relay_of(src, T.cores[(i + s) % 8], topo) for s in (1, 2)]:
+                    relay_program(g, core, T, topo, src)
+        return
+    ops = []
+    acc = {}
+
+    def ap(name, *ix, p=None):
+        if name in PACK:
+            name, o, w = PACK[name]
+            r = range(*(ix[0] if ix else slice(None)).indices(w))
+            ix = (slice(o + r[0], o + r[-1] + 1, r.step),)
+        sh = SCRATCH[name][1][1:]
+        ix = list(ix) + [slice(None)] * (len(sh) - len(ix))
+        st, lo, hi, n = 1, 0, 0, 1
+        for d in range(len(sh) - 1, -1, -1):
+            x = ix[d]
+            if isinstance(x, slice):
+                r = range(*x.indices(sh[d]))
+                lo, hi, n = lo + r[0] * st, hi + r[-1] * st, n * len(r)
+            else:
+                lo, hi = lo + x * st, hi + x * st
+            st *= sh[d]
+        ps = SCRATCH[name][0] == "psum"
+        if ps:
+            lo, hi = 0, st
+        return {"ap": T[name][tuple([slice(None) if p is None else slice(0, p)] + ix)], "k": [(name, lo, hi + 1)], "n": n,
+                "b": SIZE[SCRATCH[name][2]], "ps": ps, "ind": False}
+
+    def ind(w, o):
+        r = dict(w)
+        r.update({"ap": w["ap"].indirect(o["ap"]), "k": w["k"] + o["k"], "n": 16 * o["n"], "ind": True})
+        return r
+
+    def op(eng, cost, outs, ins, fn, sem=None, val=1, lat=0.0):
+        i = len(ops)
+        wait, order = set(), set()
+        rk = [k for o in ins for k in o["k"]] + [k for o in outs for k in o["k"][1:]]
+        wk = [o["k"][0] for o in outs]
+        for kind, keys in (("r", rk), ("w", wk)):
+            for name, lo, hi in keys:
+                psum = SCRATCH[name][0] == "psum"
+                for (l2, h2, j, k2) in acc.get(name, []):
+                    if j == i or l2 >= hi or h2 <= lo:
+                        continue
+                    if kind == "r" and k2 == "r" and not (psum and ops[j]["eng"] != eng):
+                        continue
+                    if psum and eng == "T" and ops[j]["eng"] == "T":
+                        order.add(j)
+                    else:
+                        wait.add(j)
+        for kind, keys in (("r", rk), ("w", wk)):
+            for name, lo, hi in keys:
+                lst = acc.setdefault(name, [])
+                if kind == "w":
+                    lst[:] = [x for x in lst if not (lo <= x[0] and x[1] <= hi)]
+                lst.append((lo, hi, i, kind))
+        ops.append({"eng": eng, "cost": cost, "fn": fn, "wait": wait, "order": order - wait, "sem": sem, "val": val, "lat": lat})
+        return i
+
+    def vcost(o, ins, tt=False):
+        for x in [o] + ins:
+            if x["ind"]:
+                return 60 + x["n"] * (3.8 if x is o else 1.56)
+        if tt:
+            return 60 + max(64, o["n"] * (1 if any(x["ps"] for x in ins) else 2))
+        return 60 + max(64, o["n"] * (0.5 if all(x["b"] == 2 for x in [o] + ins) else 1))
+
+    def cp(o, i):
+        op("V", vcost(o, [i]), [o], [i], lambda q: q.tensor_copy(o["ap"], i["ap"]))
+
+    def tt(o, a, b, f):
+        op("V", vcost(o, [a, b], True), [o], [a, b], lambda q: q.tensor_tensor(o["ap"], a["ap"], b["ap"], f))
+
+    def ts(o, a, s1, f1, s2=None, f2=None):
+        sc = [x for x in (s1, s2) if isinstance(x, dict)]
+        v = [x["ap"] if isinstance(x, dict) else x for x in (s1, s2)]
+        if f2 is None:
+            op("V", vcost(o, [a]), [o], [a] + sc, lambda q: q.tensor_scalar(o["ap"], a["ap"], v[0], None, f1))
+        else:
+            op("V", vcost(o, [a]), [o], [a] + sc, lambda q: q.tensor_scalar(o["ap"], a["ap"], v[0], v[1], f1, f2))
+
+    def scan(o, a, b, init, f1, f2):
+        op("V", vcost(o, [a, b]), [o], [a, b], lambda q: q.tensor_tensor_scan(o["ap"], a["ap"], b["ap"], init, f1, f2))
+
+    def trans(o, i):
+        op("V", vcost(o, [i]), [o], [i], lambda q: q.transpose(o["ap"], i["ap"]))
+
+    def fill(o, c):
+        op("V", vcost(o, []), [o], [], lambda q: q.memset(o["ap"], c))
+
+    def act(o, i, f, scale=None):
+        n = i["n"] if i["ind"] else o["n"] if o["ind"] else i["n"]
+        cost = 80 + (n * 1.56 if i["ind"] else n * 3.8 if o["ind"] else max(64, n))
+        if scale is None:
+            op("S", cost, [o], [i], lambda q: q.activation(o["ap"], i["ap"], f))
+        else:
+            op("S", cost, [o], [i], lambda q: q.activation(o["ap"], i["ap"], f, 0.0, scale))
+
+    def mms(lst):
+        cost = 60 + sum(max(64, x[2]["n"]) * (4 if x[2]["b"] == 4 else 1) for x in lst)
+
+        def fn(q):
+            for o, l, r, a, z in lst:
+                m = q.matmul(o["ap"], l["ap"], r["ap"], a, z)
+            return m
+        op("T", cost, [x[0] for x in lst], [y for x in lst for y in x[1:3]], fn)
+
+    def load(eng, buf, src, n):
+        q = {"Y": g.sync, "S": g.scalar}[eng]
+        op(eng, 100, [buf], [], lambda _q: q.dma_start(buf["ap"], src), sem="ld%d" % n, val=16, lat=2500)
+
+    def store(dst, buf, sem):
+        op("Y", 100, [], [buf], lambda _q: g.sync.dma_start(dst, buf["ap"]), sem=sem, val=16, lat=2500)
+
+    def iota(o, pat, base, mult):
+        if o["k"][0][0] in ("coe", "pki", "sue"):
+            op("G", 130 + 2 * o["n"], [o], [], lambda q: q.iota(o["ap"], pat, base, mult))
+        else:
+            op("G", 130 + 2 * o["n"], [o], [], lambda q: q.iota(o["ap"], pat, base, mult, allow_small_or_imprecise_dtypes=True))
+
+    loc = [0]
+
+    def remote(stage, hops):
+        for dst, land, rsem in hops:
+            def fn(q, dst=dst, land=land, rsem=rsem):
+                loc[0] += send(g, T, topo, core, dst, T[land][:], stage["ap"], rsem)
+            i = op("G", 500, [], [stage], fn, sem="ls", val=0)
+        return i
+
+    def arrive(land, rsem, src, after, lat):
+        rl = relay_of(src, core, topo)
+        n = len(topo.engines(src if rl is None else rl, core))
+        i = op("N", 0, [ap(land)], [], lambda q: None, sem=rsem, val=n, lat=lat)
+        ops[i]["wait"].add(after)
+
+    nxt, nx2, prv, pr2 = [T.cores[(rank + s) % 8] for s in (1, 2, -1, -2)]
+    r1, r2 = relay_of(core, nxt, topo), relay_of(core, nx2, topo)
+    a_ = s_(None, None)
+    rcol = lambda: ap("pf", s_(0, 1))
+    flipm = [["m00", "m01"], ["m10", "m11"]]
+
+    def inputs():
+        n = 0
+        for c, (q0, q) in enumerate(CH):
+            load("Y", ap("lai", s_(2 * q0, 2 * q0 + q)), T.la[:, q0:q0 + q], n)
+            load("S", ap("lai", s_(2 * q0 + q, 2 * q0 + 2 * q)), T.lb[:, q0:q0 + q], n + 1)
+            n += 2
+        load("Y", ap("coe", s_(0, 1280)), T.co[:], n)
+        load("S", ap("dl0"), T.dl[:], n + 1)
+        load("Y", ap("xw", s_(0, 1280)), T.x0[:], n + 2)
+        load("S", ap("thi", p=8), T.th[:], n + 3)
+        load("S", ap("wtb"), T.wt[:], n + 4)
+        load("Y", ap("sue", s_(0, 1280)), T.su[:], n + 5)
+
+    def consts_a():
+        iota(ap("pi"), [[0, 1]], 0, 1)
+        iota(ap("dif"), [[1, 128]], 0, -1)
+        iota(ap("rowg"), [[1, 8], [0, 16]], 0, 0)
+        iota(ap("rowr"), [[0, 32], [1, 16]], 0, 0)
+        ts(ap("pr", s_(0, 1)), ap("pi"), 15, A.bitwise_and)
+        ts(ap("pr", s_(1, 2)), ap("pi"), 4, A.arith_shift_right)
+        ts(ap("pr", s_(2, 3)), ap("pi"), 4, A.arith_shift_right, 1, A.bitwise_and)
+        cp(ap("pf", s_(0, 3)), ap("pr"))
+        cp(ap("pf", s_(3, 4)), ap("pi"))
+        par = ap("pf", s_(2, 3))
+        ts(ap("opar"), par, -1.0, A.mult, 1.0, A.add)
+        ts(ap("idb"), ap("dif"), 0.0, A.is_equal)
+        ts(ap("idn"), ap("dif"), 0.0, A.is_equal, -1.0, A.mult)
+        ts(ap("m00"), ap("dif"), 0.0, A.is_equal, ap("opar"), A.mult)
+        ts(ap("m11"), ap("dif"), 0.0, A.is_equal, par, A.mult)
+        ts(ap("m01"), ap("dif"), 16.0, A.is_equal, ap("opar"), A.mult)
+        ts(ap("m10"), ap("dif"), -16.0, A.is_equal, par, A.mult)
+        ts(ap("blk"), ap("rowg"), ap("pf", s_(1, 2)), A.is_equal)
+        ts(ap("kc1"), ap("rowr"), 2048.0, A.mult, -16777216.0, A.add)
+        fill(ap("lr"), 0.0)
+        for r in range(16):
+            act(ap("lr", r, s_(r, 128, 16)), ap("blk", s_(r, 128, 16)), F.Copy, 32768.0)
+
+    def consts_b():
+        w = 32 * QM
+        ts(ap("rmin"), ap("rowr", s_(0, w)), 0.0, A.is_equal, 268435456.0, A.mult)
+        ts(ap("rmin"), ap("rmin"), -134217728.0, A.add)
+        ts(ap("rmax"), ap("rmin"), -1.0, A.mult)
+        ts(ap("kc2"), ap("rowr", s_(0, 128)), -512.0, A.mult, 7680.0, A.add)
+        fill(ap("kc3"), -16777216.0)
+        cp(ap("thf", p=8), ap("thi", p=8))
+        ts(ap("e8", p=8), ap("rowg", p=8), ap("pf", s_(3, 4), p=8), A.is_equal)
+        mms([(ap("ps0", s_(0, 1)), ap("e8", p=8), ap("thf", p=8), True, True)])
+        cp(ap("thq"), ap("ps0", s_(0, 1)))
+        ts(ap("thr"), ap("thq"), 32768.0, A.mult, -16777216.0, A.add)
+        fill(ap("ww"), 0.0)
+        for j in range(16):
+            ts(ap("ww", j, s_(j, 128, 16)), ap("blk", s_(j, 128, 16)), ap("wtb"), A.mult)
+        iota(ap("q16"), [[16, 16]], 0, 0)
+        ts(ap("lcol"), ap("q16"), rcol(), A.add)
+        ts(ap("dump"), ap("lcol"), 1280.0, A.add)
+        iota(ap("it"), [[1, 1536]], 0, 0)
+        for c, (q0, q) in enumerate(CH):
+            iota(ap("eq%d" % c), [[0, q * (16 * q + 2)]], 0, 0)
+            ts(ap("ebase", s_(q0, q0 + q)), ap("lcol", s_(0, q)), 16.0, A.mult, 15.0, A.add)
+        iota(ap("coe", s_(1280, 1536)), [[1, 256]], 1280, 0)
+        for q in sorted({q for _, q in CH}):
+            w, n = 16 * q + 2, q * (16 * q + 2)
+            iota(ap("cwi%d" % q), [[-16, q], [1, w]], -2, 0)
+            ts(ap("cwi%d" % q), ap("cwi%d" % q), rcol(), A.is_equal, 1023.0, A.mult)
+            ts(ap("cw%d" % q), ap("cwi%d" % q), 1.0, A.add)
+            fill(ap("cw%d" % q, s_(0, n, w)), 0.0)
+            fill(ap("cw%d" % q, s_(1, n, w)), 0.0)
+
+    def consts_c():
+        fill(ap("oneb"), 1.0)
+        fill(ap("onef"), 1.0)
+        fill(ap("zf"), 0.0)
+        fill(ap("z48"), 0.0)
+        fill(ap("fl"), 0.0)
+        iota(ap("xw", s_(1280, 1536)), [[0, 256]], 0, 0)
+        iota(ap("sue", s_(1280, 1536)), [[0, 256]], 0, 0)
+        iota(ap("v48"), [[16, 48]], 192, 0)
+        ts(ap("rge"), ap("rowr", s_(0, 128)), rcol(), A.is_ge)
+        tt(ap("tri"), ap("rge"), ap("blk"), A.mult)
+        tt(ap("trx"), ap("tri"), ap("blk"), A.subtract)
+        ts(ap("dv"), ap("v48"), rcol(), A.add)
+        ts(ap("dv1"), ap("dv"), 1.0, A.add)
+        ts(ap("dm"), ap("rowr", s_(0, 192)), rcol(), A.is_equal)
+        ts(ap("sm"), ap("rowr", s_(0, 192)), 0.0, A.is_gt)
+        for h in range(2):
+            ts(ap("rx", s_(384 * h, 384 * h + 384)), ap("rowr", s_(0, 384)), 0.0, A.is_gt)
+            ts(ap("rn", s_(384 * h, 384 * h + 384)), ap("rowr", s_(0, 384)), 0.0, A.is_equal, 64.0, A.mult)
+
+    def reps(t):
+        for k in range(16):
+            if k < VREP[t]:
+                cp(ap("rep%d" % t, s_(k, 4096, 16)), ap("dl%d" % t))
+            else:
+                act(ap("rep%d" % t, s_(k, 4096, 16)), ap("dl%d" % t), F.Copy)
+
+    def rnd(t):
+        rep, ab, last = "rep%d" % t, "ab%d" % t, t == 2
+        xall, base = ap("xw", s_(0, 1280)), ap("xw", s_(0, 512))
+        if t == 0:
+            cp(ap("ab0"), ap("lai"))
+        cp(ap("df"), ind(ap("coe", s_(0, 1280)), ap(ab)))
+        cp(ap("abf"), ap(ab))
+        cp(ap("dfh"), ap("df"))
+        trans(ap("ta"), ap("dfh"))
+        mms([(ap("py1", s_(0, 16), c1), ap(flipm[c1][gp]), ap("ta", a_, gp), gp == 0, gp == 1) for c1 in (0, 1) for gp in (0, 1)])
+        tt(ap("dT"), ap("py1", s_(0, 16)), ap("kc1"), A.add)
+        fs, fv = "fs%d" % (t % 2), "fv"
+        iota(ap(fs, s_(512, 1280)), [[0, 768]], 0, 0)
+        iota(ap(fv, s_(512, 1280)), [[0, 768]], 0, 0)
+
+        def second(c, h, w, off, m, fused):
+            dst = ap("a%d" % c, s_(4 * h, 4 * h + 4))
+            z = h % 2
+            if fused:
+                tt(ap("g%d" % z), ind(w, off), m, A.subtract)
+                act(dst, ap("g%d" % z), F.Abs)
+            else:
+                act(ap("g%d" % z), ind(w, off), F.Identity)
+                nm, lo = m["k"][0][0], m["k"][0][1]
+                mms([(ap("py%d" % z, s_(16 * i, 16 * i + 16)), ap("idb"), ap("g%d" % z, s_(512 * i, 512 * i + 512)), True, False) for i in (0, 1)] +
+                    [(ap("py%d" % z, s_(16 * i, 16 * i + 16)), ap("idn"), ap(nm, s_(lo + 512 * i, lo + 512 * i + 512)), False, True) for i in (0, 1)])
+                act(dst, ap("py%d" % z), F.Abs)
+
+        def sums(c, h, first, stop):
+            o = ap("kp%d" % (c % 2), s_(64 * h, 64 * h + 64))
+            mms([(o, ap("lr", r), ap("a%d" % c, s_(4 * h, 4 * h + 4), r), first and r == 0, stop and r == 15) for r in range(16)])
+
+        def step1(c):
+            q0, q = CH[c]
+            w = 16 * q
+            for h in range(q // 4):
+                z = h % 2
+                lo, o = 256 * q0 + 1024 * h, 32 * q0 + 64 * h
+                tt(ap("t%d" % z), ind(xall, ap("df", s_(o, o + 64))), ap(rep, s_(lo, lo + 1024)), A.add)
+                ts(ap("mb%d" % z), ap("t%d" % z), 0.0, A.max, 63.0, A.min)
+                second(c, h, xall, ap("df", s_(o + w, o + w + 64)), ap("mb%d" % z), (1, c, h) in VFUSED)
+                sums(c, h, True, True)
+            kq = ap("kp%d" % (c % 2), s_(0, w))
+            for i in (0, 1):
+                tt(ap("kd", s_(w * i, w * i + w)), kq, ap("dT", s_(32 * q0 + w * i, 32 * q0 + w * i + w)), A.add)
+            scan(ap("kk", s_(0, 2 * w)), ap("rmin", s_(0, 2 * w)), ap("kd", s_(0, 2 * w)), 134217728.0, A.max, A.min)
+            both, first = s_(2 * q0, 2 * q0 + 2 * q), s_(2 * q0, 2 * q0 + q)
+            cp(ap("di", both), ap("kk", s_(15, 2 * w, 16)))
+            ts(ap("dm2", both), ap("di", both), 2047, A.bitwise_and)
+            cp(ap("dlist", s_(q0, q0 + q)), ap("dm2", first))
+            ts(ap("al", both), ap("kk", s_(15, 2 * w, 16)), ap("thr"), A.is_lt)
+            tt(ap("ald", s_(q0, q0 + q)), ap("al", first), ap("dump", s_(q0, q0 + q)), A.mult)
+
+        def lanes():
+            cp(ap("df32"), ap("dm2"))
+            tt(ap("abd"), ap("df32"), ap("abf"), A.subtract)
+            tt(ap("abd"), ap("abd"), ap("al"), A.mult)
+            tt(ap("abn"), ap("abf"), ap("abd"), A.add)
+            if last:
+                for c, (q0, q) in enumerate(CH):
+                    store(T.ya[:, q0:q0 + q], ap("abn", s_(2 * q0, 2 * q0 + q)), "o%d" % (2 * c))
+                    store(T.yb[:, q0:q0 + q], ap("abn", s_(2 * q0 + q, 2 * q0 + 2 * q)), "o%d" % (2 * c + 1))
+                return
+            k = t + 1
+            cp(ap("abo%d" % k), ap("abn"))
+            i = remote(ap("abo%d" % k), [(nxt, "ab%d" % k, "aab%d" % k) if r1 is None else (r1, "rab%d" % k, "rab%d" % k)])
+            arrive("ab%d" % k, "aab%d" % k, prv, i, 8000)
+
+        def threshold():
+            asum, al = ap("asum"), ap("al")
+            op("V", 124, [asum], [al], lambda q: q.tensor_reduce(asum["ap"], al["ap"], AxisListType.X, A.add))
+            mms([(ap("ps1", s_(0, 1)), ap("onef"), ap("asum"), True, True)])
+            ts(ap("ai", s_(0, 1)), ap("ps1", s_(0, 1)), -0.5, A.mult, 2048.0, A.add)
+            ts(ap("ai", s_(1, 2)), ap("ai", s_(0, 1)), 63, A.bitwise_and)
+            tt(ap("tha"), ap("thq"), ap("ai", s_(1, 2)), A.add)
+            ts(ap("thr"), ap("tha"), 32768.0, A.mult, -16777216.0, A.add)
+
+        def step2a(c):
+            q0, q = CH[c]
+            w = 16 * q
+            x = s_(0, w)
+            s16, n16 = "s16%d" % c, "n16%d" % c
+            u = ap("ps%d" % (c % 2), x)
+            cp(ap(s16), ind(ap("sue", s_(0, 1280)), ap("dlist", s_(q0, q0 + q))))
+            for h in range(q // 4):
+                z, lo = h % 2, 256 * q0 + 1024 * h
+                tt(ap("t%d" % z), ind(xall, ap(s16, s_(64 * h, 64 * h + 64))), ap(rep, s_(lo, lo + 1024)), A.add)
+                ts(ap("e", s_(lo, lo + 1024)), ap("t%d" % z), 0.0, A.max, 63.0, A.min)
+                mms([(ap("ps%d" % (c % 2), s_(64 * h, 64 * h + 64)), ap("ww", j), ap("e", s_(lo + j, lo + 1024, 16)), j == 0, j == 15) for j in range(16)])
+            cp(ap("ui", x), u)
+            ts(ap("ua", x), ap("ui", x), 4095, A.bitwise_and)
+            ts(ap("ub", x), ap("ua", x), 1184.0, A.add)
+            tt(ap("uc", x), ap("ua", x), ap("ub", x), A.mult)
+            ts(ap("un", x), ap("uc", x), 5, A.arith_shift_right, 511, A.bitwise_and)
+            cp(ap(n16), ap("un", x))
+            b = s_(0, q // 2)
+            cp(ap("nh", b), ap(n16))
+            trans(ap("na", b), ap("nh", b))
+            kp = "kp%d" % (c % 2)
+            lst = [(ap(kp, x), ap("idb"), ap("kc3", x), True, False), (ap(kp, x), ap("idb"), ap("kc2", x), False, False)]
+            for k in range(q):
+                lst += [(ap(kp, s_(16 * k, 16 * k + 16)), ap(flipm[k % 2][gp]), ap("na", k // 2, gp), False, False) for gp in (0, 1)]
+            mms(lst)
+
+        def step2b(c):
+            q0, q = CH[c]
+            w = 16 * q
+            n16 = "n16%d" % c
+            for h in range(q // 4):
+                lo = 256 * q0 + 1024 * h
+                second(c, h, base, ap(n16, s_(64 * h, 64 * h + 64)), ap("e", s_(lo, lo + 1024)), (2, c, h) in VFUSED)
+                sums(c, h, False, h == q // 4 - 1)
+            kq = ap("kp%d" % (c % 2), s_(0, w))
+            scan(ap("kk2", s_(0, w)), ap("rmax", s_(0, w)), kq, -134217728.0, A.min, A.max)
+            q8 = s_(q0, q0 + q)
+            i0, i1, i2 = s_(0, q), s_(QM, QM + q), s_(2 * QM, 2 * QM + q)
+            cp(ap("i2", i0), ap("kk2", s_(15, w, 16)))
+            ts(ap("i2", i1), ap("i2", i0), 511, A.bitwise_and)
+            ts(ap("i2", i2), ap("i2", i0), 9, A.arith_shift_right, 15, A.bitwise_and)
+            tt(ap("nef", q8), ap("i2", i1), ap("ald", q8), A.max)
+            cp(ap("ne16", q8), ap("nef", q8))
+            tt(ap("sma", i0), ap("ebase", q8), ap("i2", i2), A.subtract)
+            cp(ap("eo16", q8), ap("sma", i0))
+            cp(ap("nr", s_(0, w)), ind(ap("it"), ap("ne16", q8)))
+            eq, v = "eq%d" % c, w + 2
+            for k in range(q):
+                ts(ap(eq, s_(v * k + 2, v * k + v)), ap("nr", s_(0, w)), ap("nef", s_(q0 + k, q0 + k + 1)), A.is_equal)
+            scan(ap("we", s_(0, q * v)), ap(eq), ap("cw%d" % q), 0.0, A.add, A.mult)
+            ts(ap("sma", i1), ap("we", s_(v - 1, q * v, v)), 1536.0, A.is_gt)
+            tt(ap("sma", i2), ap("sma", i1), ap("dump", q8), A.mult)
+            tt(ap("smb", i0), ap("sma", i2), ap("nef", q8), A.max)
+            cp(ap("nw16", q8), ap("smb", i0))
+            cp(ap("ew%d" % c), ind(ap("e", s_(256 * q0, 256 * (q0 + q))), ap("eo16", q8)))
+            b = s_(0, q // 2)
+            cp(ap("c16", s_(0, w)), ind(ap("coe"), ap("nw16", q8)))
+            cp(ap("nh", b), ap("c16", s_(0, w)))
+            trans(ap("na", b), ap("nh", b))
+            pz = "ps%d" % (c % 2)
+            mms([(ap(pz, s_(k, w, q)), ap(flipm[k % 2][gp]), ap("na", k // 2, gp), gp == 0, gp == 1) for k in range(q) for gp in (0, 1)])
+            cp(ap("ct%d" % c), ap(pz, s_(0, w)))
+            for k in range(16):
+                if k < VFLAG[c]:
+                    cp(ind(ap(fv), ap("ct%d" % c, k)), ap("oneb", s_(0, w)))
+                else:
+                    act(ind(ap(fs), ap("ct%d" % c, k)), ap("zf", s_(0, w)), F.Sigmoid)
+
+        def step4():
+            for c in range(NC - 1, -1, -1):
+                q0, q = CH[c]
+                cp(ind(ap("xw"), ap("nw16", s_(q0, q0 + q))), ap("ew%d" % c))
+            act(ap("fsb"), ap(fs, s_(512, 1280)), F.Copy)
+            o48 = ap("kp0", s_(0, 48))
+            mms([(o48, ap("lr", r), ap(fv, s_(512 + r, 1280, 16)), r == 0, False) for r in range(16)])
+            mms([(o48, ap("lr", r), ap("fsb", s_(r, 768, 16)), False, r == 15) for r in range(16)])
+            ts(ap("up0"), o48, 0.0, A.is_gt)
+            tt(ap("upb"), ap("up0"), ap("fl"), A.max)
+            oa, ob = ap("kp0", s_(0, 48)), ap("kp0", s_(64, 112))
+            mms([(oa, ap("blk"), ap("upb"), True, True), (ob, ap("trx"), ap("upb"), True, True)])
+            scan(ap("r0"), oa, ap("z48"), 0.0, A.add, A.add)
+            tt(ap("r1"), ap("r0"), ob, A.add)
+            ts(ap("r2"), ap("r1"), 192.0, A.is_le)
+            tt(ap("r3"), ap("r2"), ap("upb"), A.mult)
+            tt(ap("r4"), ap("r1"), ap("dv1"), A.subtract)
+            tt(ap("r4"), ap("r4"), ap("r3"), A.mult)
+            tt(ap("r4"), ap("r4"), ap("dv"), A.add)
+            cp(ap("pos"), ap("r4"))
+            if not last:
+                tt(ap("fl"), ap("upb"), ap("r3"), A.subtract)
+            cp(ap("cmp", s_(0, 192)), ap("it", s_(1280, 1472)))
+            cp(ind(ap("cmp"), ap("pos")), ap("it", s_(512, 1280)))
+            tt(ap("cmm"), ap("cmp", s_(0, 192)), ap("dm"), A.mult)
+            scan(ap("cms"), ap("sm"), ap("cmm"), 0.0, A.mult, A.max)
+            cp(ap("vl"), ap("cms", s_(15, 192, 16)))
+            cp(ap("sv"), ind(ap("sue"), ap("vl")))
+            for i in range(4):
+                x = s_(768 * i, 768 * i + 768)
+                src = ind(xall, ap("sv", s_(48 * i, 48 * i + 48)))
+                if i < VREN:
+                    cp(ap("gr", x), src)
+                else:
+                    act(ap("gr", x), src, F.Identity)
+                scan(ap("mx", x), ap("rx"), ap("gr", x), 0.0, A.mult, A.max)
+                scan(ap("mn", x), ap("rn"), ap("gr", x), 0.0, A.max, A.min)
+            tt(ap("sm2"), ap("mx", s_(15, 3072, 16)), ap("mn", s_(15, 3072, 16)), A.add)
+            ts(ap("si"), ap("sm2"), 0.5, A.mult, -0.25, A.add)
+            cp(ind(ap("xw"), ap("vl")), ap("si"))
+
+        for c in range(NC):
+            step1(c)
+        step2a(0)
+        lanes()
+        if not last:
+            threshold()
+        for c in range(NC):
+            if c:
+                step2a(c)
+            step2b(c)
+        step4()
+        if last:
+            store(T.yx[:], xall, "ox")
+
+    inputs()
+    consts_a()
+    reps(0)
+    hops = []
+    if r1 is None:
+        hops.append((nxt, "dl1", "adl1"))
+    if r2 is None:
+        hops.append((nx2, "dl2", "adl2"))
+    for r in sorted({x for x in (r1, r2) if x is not None}):
+        hops.append((r, "rdl", "rdl"))
+    snt = remote(ap("dl0"), hops)
+    arrive("dl1", "adl1", prv, snt, 8000)
+    arrive("dl2", "adl2", pr2, snt, 8000)
+    consts_b()
+    consts_c()
+    rnd(0)
+    reps(1)
+    rnd(1)
+    reps(2)
+    rnd(2)
+
+    n = len(ops)
+    succ = [[] for _ in range(n)]
+    npred = [0] * n
+    for i, o in enumerate(ops):
+        for j in o["wait"] | o["order"]:
+            succ[j].append(i)
+            npred[i] += 1
+    prio = [0.0] * n
+    for i in range(n - 1, -1, -1):
+        o = ops[i]
+        prio[i] = o["cost"] + o["lat"] + max([prio[j] for j in succ[i]], default=0.0)
+    free = {}
+    ready = {i: 0.0 for i in range(n) if npred[i] == 0}
+    rt = [0.0] * n
+    seq = []
+    while ready:
+        best = min(max(free.get(ops[i]["eng"], 0.0), r) for i, r in ready.items())
+        cand = [i for i, r in ready.items() if max(free.get(ops[i]["eng"], 0.0), r) <= best + 1e-6]
+        i = max(cand, key=lambda x: (prio[x], -x))
+        del ready[i]
+        o = ops[i]
+        free[o["eng"]] = best + o["cost"] if o["eng"] != "N" else 0.0
+        fin = best + o["cost"] + o["lat"]
+        o["start"], o["fin"] = best, fin
+        seq.append(i)
+        for j in succ[i]:
+            npred[j] -= 1
+            k = fin + 40 if i in ops[j]["wait"] else best
+            rt[j] = max(rt[j], k)
+            if npred[j] == 0:
+                ready[j] = rt[j]
+    INFO["ops"] = ops
+
+    queues = {"V": g.vector, "S": g.scalar, "T": g.tensor, "G": g, "Y": g.sync, "N": None}
+    esem = {"V": "cv", "S": "cs", "T": "ct", "G": "cg"}
+    count = {}
+    known = {e: {} for e in queues}
+    final = {}
+    for i in seq:
+        o = ops[i]
+        e, q = o["eng"], queues[o["eng"]]
+        if e != "N":
+            for j in sorted(o["wait"], key=lambda x: -ops[x]["fin"]):
+                s, v = ops[j]["done"]
+                if v and known[e].get(s, 0) < v:
+                    q.wait_ge(T.sem[s], v)
+                    known[e][s] = v
+                    for a, b in ops[j]["clk"].items():
+                        known[e][a] = max(known[e].get(a, 0), b)
+        ins = o["fn"](q)
+        if o["sem"] is None:
+            s = esem[e]
+            count[s] = count.get(s, 0) + 1
+            ins.then_inc(T.sem[s], 1)
+            o["done"] = (s, count[s])
+            final[s] = count[s]
+        else:
+            o["done"] = (o["sem"], o["val"])
+            if o["val"]:
+                if e != "N":
+                    ins.then_inc(T.sem[o["sem"]], o["val"])
+                final[o["sem"]] = o["val"]
+        o["clk"] = dict(known[e]) if e != "N" else {}
+    if loc[0]:
+        final["ls"] = loc[0]
+    for s in sorted(final):
+        g.wait_ge(T.sem[s], final[s])

@@ -3,13 +3,24 @@ A = AluOpType
 F = ActivationFunctionType
 B2, F4, I4, U2, H2 = "bfloat16", "float32", "int32", "uint16", "float16"
 SB = lambda w, d: ("sbuf", [128] + w, d)
-CH = [(0, 8), (8, 8)]
-NC = len(CH)
-QM = max(q for _, q in CH)
-VFUSED = ((1, 1, 0), (1, 1, 1), (2, 0, 0), (2, 1, 0))
-VFLAG = (2, 8)
-VREP = (6, 0, 4)
-VREN = 1
+Q1 = (8, 8)
+Q2 = (8, 8)
+CH1, CH = [[(sum(z[:i]), q) for i, q in enumerate(z)] for z in (Q1, Q2)]
+QM = max(Q2)
+K = {
+    "look": 400,
+    "hash": 4,
+    "ps": (),
+    "qv": ((2, 3),),
+    "vflag": (2, 8),
+    "vrep": 8,
+    "vren": 1,
+    "nren": 4,
+    "vcmp": 24,
+    "vput": 24,
+}
+X0, XB, XD, XE = 192, 704, 1472, 1728
+BIG = 67108864.0
 SCRATCH = {}
 
 
@@ -19,27 +30,23 @@ def declare(d, **kw):
             SCRATCH[n] = SB(list(w), d)
 
 
-declare(B2, xw=[1536], wtb=[1], dl0_dl1_dl2_rdl=[256], rep0_rep1_rep2=[4096], blk_rge_tri_trx_idb_idn_oneb_kc2_kc3=[128],
-        lr_ww=[16, 128], rx_rn_fsb=[768], t0_t1_mb0_mb1_g0_g1=[1024], e=[4096], upb=[48], fv=[1536], gr_mx_mn=[3072])
-declare(I4, coe_sue=[1536], lai=[32], thi_pi=[1], pr=[3], di_dm2=[32], ai=[2], ui_ua_ub_uc_un=[16 * QM], i2=[3 * QM], si=[192])
-declare(U2, ab0_ab1_ab2_rab1_rab2_abo1_abo2=[32], df=[512], dlist_ne16_nw16_eo16=[16], c16=[16 * QM], pos=[48], vl=[12], sv=[192])
-declare(F4, abf_abn_abd_df32_al=[32], pf=[4], opar_thf_thq_thr_asum_tha=[1], rowg_dif_e8_onef=[128], rowr_kc1_dT=[512], it=[1536],
-        rmin_rmax=[32 * QM], q16_lcol_dump_ebase_ald_nef=[16], v48_dv_dv1_z48_up0_fl_r0_r1_r2_r3_r4=[48], dm_sm_cmm_cms_sm2=[192], kd_kk_kk2_zf=[32 * QM],
-        sma=[3 * QM], smb=[QM], fs0_fs1=[1536], cmp=[960])
-declare(H2, m00_m01_m10_m11=[128], dfh_ta=[16, 2, 16], nh_na=[QM // 2, 2, 16], nr=[16 * QM])
+declare(B2, xa_xb=[XE], wtb=[1], dl0_dl1_dl2_rdl=[256], rep0_rep1_rep2_mb_e_gb_tb=[4096], blk_tri_trx_rowg=[128], oneb=[max(128, 16 * QM)],
+        kc1_kc3=[16 * max(Q1)], kc2=[16 * QM], dw_xs_iw_inw_lw_l2w_ww=[160], rowr_rx_rn_fsb=[768], upb=[50], fl=[48], fv=[1536], gr_mx_mn=[3072])
+declare(I4, coe=[1536], sue=[1280], lai=[4, 2, 4], di_dm=[32], thi_pi=[1], pr=[3], ai=[2], ui_ua_ub_uc_un=[256], i0_i1_i2=[16], mrg=[192])
+declare(U2, ab16=[32], df=[512], dlist_ne16_nw16_eo16=[16], pos=[48], sv=[192], s16_n16_ct=[256])
+declare(F4, abf1_abf2_rab1_rab2_abn0_abn1_abn2=[4, 2, 4], abd_al=[32], pf=[4], opar_par_npar_nopar_p16_thf_thq_thr_asum_wtf=[1], e8=[128], onef=[max(128, 16 * QM)],
+        it=[1536], q16_dump_ebase_ald_nef_sma_junk=[16], v48_dv_z48_r0_r1_r2_r3=[48], kk=[512], kf_fdt_kk2=[256],
+        fs=[1536], cmv_cms=[XD], suf=[768])
+declare(H2, p0_p1_n0_n1=[160], dfh_ta=[16, 2, 16], nh_na_ca=[8, 2, 16], nr_ch=[256])
+SCRATCH["ab"] = SB([16, 16, 16], B2)
+SCRATCH["ew"] = SB([256], B2)
 for _c, (_q0, _q) in enumerate(CH):
-    SCRATCH["a%d" % _c] = SB([_q, 16, 16], B2)
-    for _n in ("s16%d", "n16%d"):
-        SCRATCH[_n % _c] = SB([16 * _q], U2)
-    SCRATCH["ct%d" % _c] = SB([16, _q], U2)
-    SCRATCH["ew%d" % _c] = SB([16 * _q], B2)
-    SCRATCH["eq%d" % _c] = SB([_q * (16 * _q + 2)], B2)
-    SCRATCH["cwi%d" % _q] = SB([_q * (16 * _q + 2)], F4)
-    SCRATCH["cw%d" % _q] = SB([_q * (16 * _q + 2)], B2)
-SCRATCH["we"] = SB([QM * (16 * QM + 2)], B2)
-for _n in ("py0", "py1"):
-    SCRATCH[_n] = ("psum", [128, 32, 2, 16], F4)
-for _n in ("kp0", "kp1", "ps0", "ps1"):
+    SCRATCH["eq%d" % _c] = SB([_q * (16 * _q + 2)], H2)
+    SCRATCH["we%d" % _c] = SB([_q * (16 * _q + 2)], H2)
+    SCRATCH["cwi%d" % _q] = SB([_q * (16 * _q + 2)], B2)
+    SCRATCH["cw%d" % _q] = SB([_q * (16 * _q + 2)], H2)
+SCRATCH["py"] = ("psum", [128, 1024], F4)
+for _n in ("ka0", "ka1", "kb0", "kb1", "ps0", "ps1"):
     SCRATCH[_n] = ("psum", [128, 512], F4)
 
 PACK = {}
@@ -54,12 +61,12 @@ def pack(buf, d, names):
     SCRATCH[buf] = SB([n], d)
 
 
-pack("pkf", F4, "pf opar thf thq thr asum tha q16 lcol dump ebase ald nef v48 dv dv1 z48 up0 fl r0 r1 r2 r3 r4 sma smb abf abd df32 al")
-pack("pki", I4, "pi pr di dm2 ai i2")
-pack("pku", U2, "dlist ne16 nw16 eo16 pos vl")
-SEMAPHORES = ["cv", "cs", "ct", "cg", "ls", "rdl", "rab1", "rab2", "adl1", "adl2", "aab1", "aab2", "ox"] + ["ld%d" % n for n in range(16)] + ["o%d" % n for n in range(8)]
+pack("pkf", F4, "pf opar par npar nopar p16 thf thq thr asum q16 dump ebase ald nef sma junk v48 dv z48 r0 r1 r2 r3 abd al")
+pack("pki", I4, "pi pr di dm ai i0 i1 i2")
+pack("pku", U2, "dlist ne16 nw16 eo16 pos ab16")
+SEMAPHORES = ["cv", "cs", "ct", "cg", "ls", "rdl", "rab1", "rab2", "adl1", "adl2", "aab1", "aab2"] + ["ld%d" % n for n in range(8)] + ["o%d" % n for n in range(4)]
 SIZE = {B2: 2, F4: 4, I4: 4, U2: 2, H2: 2}
-INFO = {}
+COST = {"cyc": 0.9, "ga": 1.56, "sc": 3.8, "wake": 60}
 
 
 def relay_of(src, dst, topo):
@@ -91,7 +98,7 @@ def relay_program(g, core, T, topo, src):
     if n1:
         for t in (1, 2):
             g.wait_ge(T.sem["rab%d" % t], k)
-            n += send(g, T, topo, core, d1, T["ab%d" % t][:], T["rab%d" % t][:], "aab%d" % t)
+            n += send(g, T, topo, core, d1, T["abf%d" % t][:], T["rab%d" % t][:], "aab%d" % t)
     g.wait_ge(T.sem.ls, n)
 
 
@@ -110,6 +117,7 @@ def rank_program(g, core, T, topo):
         return
     ops = []
     acc = {}
+    cyc = COST["cyc"]
 
     def ap(name, *ix, p=None):
         if name in PACK:
@@ -118,19 +126,21 @@ def rank_program(g, core, T, topo):
             ix = (slice(o + r[0], o + r[-1] + 1, r.step),)
         sh = SCRATCH[name][1][1:]
         ix = list(ix) + [slice(None)] * (len(sh) - len(ix))
-        st, lo, hi, n = 1, 0, 0, 1
+        st, m, n = 1, 1, 1
         for d in range(len(sh) - 1, -1, -1):
             x = ix[d]
-            if isinstance(x, slice):
-                r = range(*x.indices(sh[d]))
-                lo, hi, n = lo + r[0] * st, hi + r[-1] * st, n * len(r)
+            r = range(*x.indices(sh[d])) if isinstance(x, slice) else [x]
+            if st == 1 and len(r) > 1 and r[1] - r[0] == 1:
+                m = ((1 << len(r)) - 1) << r[0]
             else:
-                lo, hi = lo + x * st, hi + x * st
+                m = sum(m << (v * st) for v in r)
+            n *= len(r)
             st *= sh[d]
         ps = SCRATCH[name][0] == "psum"
         if ps:
-            lo, hi = 0, st
-        return {"ap": T[name][tuple([slice(None) if p is None else slice(0, p)] + ix)], "k": [(name, lo, hi + 1)], "n": n,
+            bank = (1 << 512) - 1
+            m = sum(bank << b for b in range(0, st, 512) if m >> b & bank)
+        return {"ap": T[name][tuple([slice(None) if p is None else slice(0, p)] + ix)], "k": [(name, m)], "n": n,
                 "b": SIZE[SCRATCH[name][2]], "ps": ps, "ind": False}
 
     def ind(w, o):
@@ -144,10 +154,10 @@ def rank_program(g, core, T, topo):
         rk = [k for o in ins for k in o["k"]] + [k for o in outs for k in o["k"][1:]]
         wk = [o["k"][0] for o in outs]
         for kind, keys in (("r", rk), ("w", wk)):
-            for name, lo, hi in keys:
+            for name, m in keys:
                 psum = SCRATCH[name][0] == "psum"
-                for (l2, h2, j, k2) in acc.get(name, []):
-                    if j == i or l2 >= hi or h2 <= lo:
+                for (m2, j, k2) in acc.get(name, []):
+                    if j == i or not m & m2:
                         continue
                     if kind == "r" and k2 == "r" and not (psum and ops[j]["eng"] != eng):
                         continue
@@ -156,21 +166,21 @@ def rank_program(g, core, T, topo):
                     else:
                         wait.add(j)
         for kind, keys in (("r", rk), ("w", wk)):
-            for name, lo, hi in keys:
+            for name, m in keys:
                 lst = acc.setdefault(name, [])
                 if kind == "w":
-                    lst[:] = [x for x in lst if not (lo <= x[0] and x[1] <= hi)]
-                lst.append((lo, hi, i, kind))
+                    lst[:] = [x for x in lst if x[0] & ~m]
+                lst.append((m, i, kind))
         ops.append({"eng": eng, "cost": cost, "fn": fn, "wait": wait, "order": order - wait, "sem": sem, "val": val, "lat": lat})
         return i
 
     def vcost(o, ins, tt=False):
         for x in [o] + ins:
             if x["ind"]:
-                return 60 + x["n"] * (3.8 if x is o else 1.56)
+                return 50 + cyc * x["n"] * (COST["sc"] if x is o else COST["ga"])
         if tt:
-            return 60 + max(64, o["n"] * (1 if any(x["ps"] for x in ins) else 2))
-        return 60 + max(64, o["n"] * (0.5 if all(x["b"] == 2 for x in [o] + ins) else 1))
+            return 50 + cyc * max(64, o["n"] * (1 if any(x["ps"] for x in ins) else 2))
+        return 50 + cyc * max(64, (ins + [o])[0]["n"] * (0.5 if all(x["b"] == 2 for x in [o] + ins) else 1))
 
     def cp(o, i):
         op("V", vcost(o, [i]), [o], [i], lambda q: q.tensor_copy(o["ap"], i["ap"]))
@@ -195,16 +205,17 @@ def rank_program(g, core, T, topo):
     def fill(o, c):
         op("V", vcost(o, []), [o], [], lambda q: q.memset(o["ap"], c))
 
-    def act(o, i, f, scale=None):
-        n = i["n"] if i["ind"] else o["n"] if o["ind"] else i["n"]
-        cost = 80 + (n * 1.56 if i["ind"] else n * 3.8 if o["ind"] else max(64, n))
-        if scale is None:
+    def act(o, i, f, bias=None, scale=None, accum=None):
+        cost = 65 + cyc * (i["n"] * COST["ga"] if i["ind"] else o["n"] * COST["sc"] if o["ind"] else max(64, i["n"]))
+        if accum is not None:
+            op("S", cost + 20, [o, accum], [i], lambda q: q.activation(o["ap"], i["ap"], f, accum_out=accum["ap"]))
+        elif scale is None:
             op("S", cost, [o], [i], lambda q: q.activation(o["ap"], i["ap"], f))
         else:
-            op("S", cost, [o], [i], lambda q: q.activation(o["ap"], i["ap"], f, 0.0, scale))
+            op("S", cost, [o], [i], lambda q: q.activation(o["ap"], i["ap"], f, bias, scale))
 
     def mms(lst):
-        cost = 60 + sum(max(64, x[2]["n"]) * (4 if x[2]["b"] == 4 else 1) for x in lst)
+        cost = 30 + cyc * sum(max(64, x[2]["n"]) * (4 if x[2]["b"] == 4 else 1) + 10 for x in lst)
 
         def fn(q):
             for o, l, r, a, z in lst:
@@ -212,18 +223,24 @@ def rank_program(g, core, T, topo):
             return m
         op("T", cost, [x[0] for x in lst], [y for x in lst for y in x[1:3]], fn)
 
-    def load(eng, buf, src, n):
+    def load(eng, buf, src, n, lat=2500):
         q = {"Y": g.sync, "S": g.scalar}[eng]
-        op(eng, 100, [buf], [], lambda _q: q.dma_start(buf["ap"], src), sem="ld%d" % n, val=16, lat=2500)
+        return op(eng, 60, [buf], [], lambda _q: q.dma_start(buf["ap"], src), sem="ld%d" % n, val=16, lat=lat)
 
     def store(dst, buf, sem):
-        op("Y", 100, [], [buf], lambda _q: g.sync.dma_start(dst, buf["ap"]), sem=sem, val=16, lat=2500)
+        op("Y", 60, [], [buf], lambda _q: g.sync.dma_start(dst, buf["ap"]), sem=sem, val=16, lat=2500)
 
     def iota(o, pat, base, mult):
-        if o["k"][0][0] in ("coe", "pki", "sue"):
-            op("G", 130 + 2 * o["n"], [o], [], lambda q: q.iota(o["ap"], pat, base, mult))
+        if SCRATCH[o["k"][0][0]][2] == I4:
+            op("G", 130 + 2 * cyc * o["n"], [o], [], lambda q: q.iota(o["ap"], pat, base, mult))
         else:
-            op("G", 130 + 2 * o["n"], [o], [], lambda q: q.iota(o["ap"], pat, base, mult, allow_small_or_imprecise_dtypes=True))
+            op("G", 130 + 2 * cyc * o["n"], [o], [], lambda q: q.iota(o["ap"], pat, base, mult, allow_small_or_imprecise_dtypes=True))
+
+    def select(o, i, pat, f, other, base, mult):
+        op("G", 170 + 2 * cyc * o["n"], [o], [i], lambda q: q.affine_select(o["ap"], i["ap"], pat, f, other, base, mult))
+
+    def gcopy(o, i):
+        select(o, i, [[0, o["n"]]], A.is_ge, 0.0, 0, 0)
 
     loc = [0]
 
@@ -231,7 +248,7 @@ def rank_program(g, core, T, topo):
         for dst, land, rsem in hops:
             def fn(q, dst=dst, land=land, rsem=rsem):
                 loc[0] += send(g, T, topo, core, dst, T[land][:], stage["ap"], rsem)
-            i = op("G", 500, [], [stage], fn, sem="ls", val=0)
+            i = op("G", 600, [], [stage], fn, sem="ls", val=0)
         return i
 
     def arrive(land, rsem, src, after, lat):
@@ -244,306 +261,318 @@ def rank_program(g, core, T, topo):
     r1, r2 = relay_of(core, nxt, topo), relay_of(core, nx2, topo)
     a_ = s_(None, None)
     rcol = lambda: ap("pf", s_(0, 1))
-    flipm = [["m00", "m01"], ["m10", "m11"]]
+    idb = lambda: ap("iw", s_(16, 144))
+    idn = lambda: ap("inw", s_(16, 144))
+    onto = lambda tab, r: ap(tab, s_(15 - r, 143 - r))
+    flip = lambda tab, c1, gp: ap("%s%d" % (tab, c1), s_(16 - 16 * (gp - c1), 144 - 16 * (gp - c1)))
+    flat = lambda bank, a, b: ap(bank, s_(a, b))
+    turn = [0]
 
     def inputs():
-        n = 0
-        for c, (q0, q) in enumerate(CH):
-            load("Y", ap("lai", s_(2 * q0, 2 * q0 + q)), T.la[:, q0:q0 + q], n)
-            load("S", ap("lai", s_(2 * q0 + q, 2 * q0 + 2 * q)), T.lb[:, q0:q0 + q], n + 1)
-            n += 2
-        load("Y", ap("coe", s_(0, 1280)), T.co[:], n)
-        load("S", ap("dl0"), T.dl[:], n + 1)
-        load("Y", ap("xw", s_(0, 1280)), T.x0[:], n + 2)
-        load("S", ap("thi", p=8), T.th[:], n + 3)
-        load("S", ap("wtb"), T.wt[:], n + 4)
-        load("Y", ap("sue", s_(0, 1280)), T.su[:], n + 5)
+        for n, (eng, buf, src, lat) in enumerate((
+                ("Y", ap("dl0"), T.dl, 2500), ("Y", ap("coe", s_(0, 1280)), T.co, 4500), ("Y", ap("xa", s_(X0, XD)), T.x0, 5500),
+                ("S", ap("lai", s_(0, 2)), T.la, 2500), ("S", ap("lai", s_(2, 4)), T.lb, 2500),
+                ("Y", ap("sue"), T.su, 8000), ("Y", ap("wtb"), T.wt, 8000), ("Y", ap("thi", p=8), T.th, 8000))):
+            i = load(eng, buf, src[:], n, lat)
+            if n and ops[i - 1]["eng"] == eng:
+                ops[i]["order"].add(i - 1)
+            if n == 5:
+                ops[i]["order"].add(i - 3)
 
-    def consts_a():
+    def consts():
         iota(ap("pi"), [[0, 1]], 0, 1)
-        iota(ap("dif"), [[1, 128]], 0, -1)
-        iota(ap("rowg"), [[1, 8], [0, 16]], 0, 0)
-        iota(ap("rowr"), [[0, 32], [1, 16]], 0, 0)
-        ts(ap("pr", s_(0, 1)), ap("pi"), 15, A.bitwise_and)
-        ts(ap("pr", s_(1, 2)), ap("pi"), 4, A.arith_shift_right)
-        ts(ap("pr", s_(2, 3)), ap("pi"), 4, A.arith_shift_right, 1, A.bitwise_and)
+        iota(ap("dw"), [[1, 160]], -16, -1)
+        iota(ap("xs"), [[1, 160]], -15, 0)
+        iota(ap("kc1"), [[0, max(Q1)], [2048, 16]], 0, 0)
+        iota(ap("rowr"), [[0, 48], [1, 16]], 0, 0)
+        iota(ap("rowg"), [[16, 8], [0, 16]], 0, 0)
+        iota(ap("p16"), [[0, 1]], 0, 16)
+        for n, v in enumerate((15, 112, 16)):
+            ts(ap("pr", s_(n, n + 1)), ap("pi"), v, A.bitwise_and)
         cp(ap("pf", s_(0, 3)), ap("pr"))
-        cp(ap("pf", s_(3, 4)), ap("pi"))
-        par = ap("pf", s_(2, 3))
-        ts(ap("opar"), par, -1.0, A.mult, 1.0, A.add)
-        ts(ap("idb"), ap("dif"), 0.0, A.is_equal)
-        ts(ap("idn"), ap("dif"), 0.0, A.is_equal, -1.0, A.mult)
-        ts(ap("m00"), ap("dif"), 0.0, A.is_equal, ap("opar"), A.mult)
-        ts(ap("m11"), ap("dif"), 0.0, A.is_equal, par, A.mult)
-        ts(ap("m01"), ap("dif"), 16.0, A.is_equal, ap("opar"), A.mult)
-        ts(ap("m10"), ap("dif"), -16.0, A.is_equal, par, A.mult)
-        ts(ap("blk"), ap("rowg"), ap("pf", s_(1, 2)), A.is_equal)
-        ts(ap("kc1"), ap("rowr"), 2048.0, A.mult, -16777216.0, A.add)
-        fill(ap("lr"), 0.0)
-        for r in range(16):
-            act(ap("lr", r, s_(r, 128, 16)), ap("blk", s_(r, 128, 16)), F.Copy, 32768.0)
-
-    def consts_b():
-        w = 32 * QM
-        ts(ap("rmin"), ap("rowr", s_(0, w)), 0.0, A.is_equal, 268435456.0, A.mult)
-        ts(ap("rmin"), ap("rmin"), -134217728.0, A.add)
-        ts(ap("rmax"), ap("rmin"), -1.0, A.mult)
-        ts(ap("kc2"), ap("rowr", s_(0, 128)), -512.0, A.mult, 7680.0, A.add)
+        half, first = ap("pf", s_(2, 3)), ap("pf", s_(1, 2))
+        for n, a, b in (("par", 1, 0), ("opar", -1, 1), ("npar", -1, 0), ("nopar", 1, -1)):
+            ts(ap(n), half, a / 16.0, A.mult, float(b), A.add)
+        for n, c in (("p0", "opar"), ("p1", "par"), ("n0", "nopar"), ("n1", "npar")):
+            ts(ap(n), ap("dw"), 0.0, A.is_equal, ap(c), A.mult)
+        ts(ap("iw"), ap("dw"), 0.0, A.is_equal)
+        ts(ap("inw"), ap("dw"), 0.0, A.is_equal, -1.0, A.mult)
+        ts(ap("lw"), ap("xs"), first, A.is_equal, 32768.0, A.mult)
+        ts(ap("l2w"), ap("xs"), first, A.is_equal, 8192.0, A.mult)
+        act(ap("wtf"), ap("wtb"), F.Copy)
+        ts(ap("ww"), ap("xs"), first, A.is_equal, ap("wtf"), A.mult)
+        ts(ap("blk"), ap("rowg"), first, A.is_equal)
         fill(ap("kc3"), -16777216.0)
+        act(ap("rx"), ap("rowr"), F.Sign)
+        act(ap("rn"), ap("rx"), F.Silu, BIG, -BIG)
         cp(ap("thf", p=8), ap("thi", p=8))
-        ts(ap("e8", p=8), ap("rowg", p=8), ap("pf", s_(3, 4), p=8), A.is_equal)
-        mms([(ap("ps0", s_(0, 1)), ap("e8", p=8), ap("thf", p=8), True, True)])
-        cp(ap("thq"), ap("ps0", s_(0, 1)))
-        ts(ap("thr"), ap("thq"), 32768.0, A.mult, -16777216.0, A.add)
-        fill(ap("ww"), 0.0)
-        for j in range(16):
-            ts(ap("ww", j, s_(j, 128, 16)), ap("blk", s_(j, 128, 16)), ap("wtb"), A.mult)
-        iota(ap("q16"), [[16, 16]], 0, 0)
-        ts(ap("lcol"), ap("q16"), rcol(), A.add)
-        ts(ap("dump"), ap("lcol"), 1280.0, A.add)
+        ts(ap("e8", p=8), ap("rowg", p=8), ap("p16", p=8), A.is_equal)
+        o = ap("ps0", s_(0, 1))
+        mms([(o, ap("e8", p=8), ap("thf", p=8), True, True)])
+        ts(ap("thq"), o, 32768.0, A.mult, -16777216.0, A.add)
+        iota(ap("kc2"), [[0, QM], [-512, 16]], 7680, 0)
+        iota(ap("q16"), [[16, 16]], 1280, 0)
+        ts(ap("dump"), ap("q16"), rcol(), A.add)
+        ts(ap("ebase"), ap("dump"), 16.0, A.mult, 15.0 - 16 * 1280, A.add)
         iota(ap("it"), [[1, 1536]], 0, 0)
-        for c, (q0, q) in enumerate(CH):
-            iota(ap("eq%d" % c), [[0, q * (16 * q + 2)]], 0, 0)
-            ts(ap("ebase", s_(q0, q0 + q)), ap("lcol", s_(0, q)), 16.0, A.mult, 15.0, A.add)
         iota(ap("coe", s_(1280, 1536)), [[1, 256]], 1280, 0)
+        for c, (q0, q) in enumerate(CH):
+            fill(ap("eq%d" % c, s_(0, None, 16 * q + 2)), 0.0)
         for q in sorted({q for _, q in CH}):
             w, n = 16 * q + 2, q * (16 * q + 2)
-            iota(ap("cwi%d" % q), [[-16, q], [1, w]], -2, 0)
-            ts(ap("cwi%d" % q), ap("cwi%d" % q), rcol(), A.is_equal, 1023.0, A.mult)
-            ts(ap("cw%d" % q), ap("cwi%d" % q), 1.0, A.add)
-            fill(ap("cw%d" % q, s_(0, n, w)), 0.0)
-            fill(ap("cw%d" % q, s_(1, n, w)), 0.0)
-
-    def consts_c():
-        fill(ap("oneb"), 1.0)
-        fill(ap("onef"), 1.0)
-        fill(ap("zf"), 0.0)
-        fill(ap("z48"), 0.0)
-        fill(ap("fl"), 0.0)
-        iota(ap("xw", s_(1280, 1536)), [[0, 256]], 0, 0)
-        iota(ap("sue", s_(1280, 1536)), [[0, 256]], 0, 0)
-        iota(ap("v48"), [[16, 48]], 192, 0)
-        ts(ap("rge"), ap("rowr", s_(0, 128)), rcol(), A.is_ge)
-        tt(ap("tri"), ap("rge"), ap("blk"), A.mult)
-        tt(ap("trx"), ap("tri"), ap("blk"), A.subtract)
+            iota(ap("cwi%d" % q), [[-16, q], [1, w]], -1, 0)
+            ts(ap("cw%d" % q), ap("cwi%d" % q), rcol(), A.is_equal, 4096.0, A.mult)
+            fill(ap("cw%d" % q, s_(0, n, w)), -60000.0)
+            fill(ap("cw%d" % q, s_(w - 1, n, w)), -4096.0)
+        iota(ap("oneb"), [[0, max(128, 16 * QM)]], 1, 0)
+        iota(ap("onef"), [[0, max(128, 16 * QM)]], 1, 0)
+        iota(ap("z48"), [[0, 48]], 0, 0)
+        iota(ap("upb", s_(0, 2)), [[0, 2]], 0, 0)
+        iota(ap("v48"), [[16, 48]], XB, 0)
         ts(ap("dv"), ap("v48"), rcol(), A.add)
-        ts(ap("dv1"), ap("dv"), 1.0, A.add)
-        ts(ap("dm"), ap("rowr", s_(0, 192)), rcol(), A.is_equal)
-        ts(ap("sm"), ap("rowr", s_(0, 192)), 0.0, A.is_gt)
-        for h in range(2):
-            ts(ap("rx", s_(384 * h, 384 * h + 384)), ap("rowr", s_(0, 384)), 0.0, A.is_gt)
-            ts(ap("rn", s_(384 * h, 384 * h + 384)), ap("rowr", s_(0, 384)), 0.0, A.is_equal, 64.0, A.mult)
+        select(ap("tri"), ap("blk"), [[1, 128]], A.is_ge, 0.0, 0, -1)
+        select(ap("tri"), ap("tri"), [[1, 128]], A.not_equal, -255.0, 0, -1)
+        select(ap("trx"), ap("blk"), [[-1, 128]], A.is_ge, 0.0, 0, 1)
+        select(ap("trx"), ap("trx"), [[1, 128]], A.not_equal, 256.0, 0, -1)
+        ts(ap("suf"), ap("sue", s_(512, 1280)), 64.0, A.add)
 
     def reps(t):
         for k in range(16):
-            if k < VREP[t]:
-                cp(ap("rep%d" % t, s_(k, 4096, 16)), ap("dl%d" % t))
+            o, i = ap("rep%d" % t, s_(k, 4096, 16)), ap("dl%d" % t)
+            if t:
+                gcopy(o, i)
+            elif k < K["vrep"]:
+                cp(o, i)
             else:
-                act(ap("rep%d" % t, s_(k, 4096, 16)), ap("dl%d" % t), F.Copy)
+                act(o, i, F.Copy)
 
     def rnd(t):
-        rep, ab, last = "rep%d" % t, "ab%d" % t, t == 2
-        xall, base = ap("xw", s_(0, 1280)), ap("xw", s_(0, 512))
-        if t == 0:
-            cp(ap("ab0"), ap("lai"))
-        cp(ap("df"), ind(ap("coe", s_(0, 1280)), ap(ab)))
-        cp(ap("abf"), ap(ab))
-        cp(ap("dfh"), ap("df"))
-        trans(ap("ta"), ap("dfh"))
-        mms([(ap("py1", s_(0, 16), c1), ap(flipm[c1][gp]), ap("ta", a_, gp), gp == 0, gp == 1) for c1 in (0, 1) for gp in (0, 1)])
-        tt(ap("dT"), ap("py1", s_(0, 16)), ap("kc1"), A.add)
-        fs, fv = "fs%d" % (t % 2), "fv"
-        iota(ap(fs, s_(512, 1280)), [[0, 768]], 0, 0)
-        iota(ap(fv, s_(512, 1280)), [[0, 768]], 0, 0)
+        rep, last = "rep%d" % t, t == 2
+        cur, new = ("xa", "xb") if t % 2 == 0 else ("xb", "xa")
+        xall, base = ap(cur, s_(X0, XD)), ap(cur, s_(X0, XB))
+        oldn = "abf%d" % t if t else "lai"
+        old = ap(oldn)
+        cands = lambda side, h: ap("df", s_(256 * (h % 2) + 64 * (2 * side + h // 2), 256 * (h % 2) + 64 * (2 * side + h // 2) + 64))
+        thr = ap("thr") if t else ap("thq")
 
-        def second(c, h, w, off, m, fused):
-            dst = ap("a%d" % c, s_(4 * h, 4 * h + 4))
-            z = h % 2
-            if fused:
-                tt(ap("g%d" % z), ind(w, off), m, A.subtract)
-                act(dst, ap("g%d" % z), F.Abs)
+        def before():
+            for c1 in (0, 1):
+                cp(ap("ab16", s_(16 * c1, 16 * c1 + 16)), ap(oldn, a_, c1))
+            cp(ap("df"), ind(ap("coe", s_(0, 1280)), ap("ab16")))
+            for c1 in (0, 1):
+                cp(ap("dfh", a_, c1), ap("df", s_(256 * c1, 256 * c1 + 256)))
+            trans(ap("ta"), ap("dfh"))
+            mms([(ap("kb1", s_(64 * h, 64 * h + 64)), flip(tab, h % 2, gp), ap("ta", s_(b + h // 2 * 4, b + h // 2 * 4 + 4), gp),
+                  tab == "p" and gp == 0, tab == "n" and gp == 1) for h in range(4) for tab, b in (("p", 8), ("n", 0)) for gp in (0, 1)])
+            act(ap("fdt"), ap("kb1", s_(0, 256)), F.Copy)
+            iota(ap("fs", s_(512, 1280)), [[0, 768]], 0, 0)
+            iota(ap("fv", s_(512, 1280)), [[0, 768]], 0, 0)
+            iota(ap("cmv", s_(0, 192)), [[0, 192]], 0, 0)
+            if K["vcmp"] < 48:
+                iota(ap("cms", s_(0, 192)), [[0, 192]], 0, 0)
+
+        def two(i, a, na, b, nb, lo):
+            o = ap("py", s_(512 * i, 512 * i + 512))
+            mms([(o, l, ap(n, s_(lo + 512 * i, lo + 512 * i + 512)), z == 0, z == 1) for z, (l, n) in enumerate(((a, na), (b, nb)))])
+            return o
+
+        def moved(step, h, off, dst):
+            lo = 1024 * h
+            x = s_(lo, lo + 1024)
+            if (step, h) in K["ps"]:
+                act(ap("tb", x), ind(xall, off), F.Identity)
+                for i in (0, 1):
+                    ts(ap(dst, s_(lo + 512 * i, lo + 512 * i + 512)), two(i, idb(), "tb", idb(), rep, lo), 0.0, A.max, 63.0, A.min)
             else:
-                act(ap("g%d" % z), ind(w, off), F.Identity)
-                nm, lo = m["k"][0][0], m["k"][0][1]
-                mms([(ap("py%d" % z, s_(16 * i, 16 * i + 16)), ap("idb"), ap("g%d" % z, s_(512 * i, 512 * i + 512)), True, False) for i in (0, 1)] +
-                    [(ap("py%d" % z, s_(16 * i, 16 * i + 16)), ap("idn"), ap(nm, s_(lo + 512 * i, lo + 512 * i + 512)), False, True) for i in (0, 1)])
-                act(dst, ap("py%d" % z), F.Abs)
+                tt(ap("tb", x), ind(xall, off), ap(rep, x), A.add)
+                ts(ap(dst, x), ap("tb", x), 0.0, A.max, 63.0, A.min)
 
-        def sums(c, h, first, stop):
-            o = ap("kp%d" % (c % 2), s_(64 * h, 64 * h + 64))
-            mms([(o, ap("lr", r), ap("a%d" % c, s_(4 * h, 4 * h + 4), r), first and r == 0, stop and r == 15) for r in range(16)])
+        def distance(step, h, w, off, m, tab, kp, q0, q):
+            x = s_(1024 * h, 1024 * h + 1024)
+            if (step, h) in K["qv"]:
+                tt(ap("gb", x), ind(w, off), ap(m, x), A.subtract)
+                act(ap("ab", s_(4 * h, 4 * h + 4)), ap("gb", x), F.Abs)
+            else:
+                act(ap("gb", x), ind(w, off), F.Identity)
+                for i in (0, 1):
+                    act(ap("ab", s_(4 * h + 2 * i, 4 * h + 2 * i + 2)), two(i, idb(), "gb", idn(), m, 1024 * h), F.Abs)
+            o = flat(kp, 64 * h - 16 * q0, 64 * h - 16 * q0 + 64)
+            end = 4 * h + 4 == q0 + q
+            mms([(o, onto(tab, r), ap("ab", s_(4 * h, 4 * h + 4), r), False, end and r == 15) for r in range(16)])
 
         def step1(c):
-            q0, q = CH[c]
-            w = 16 * q
-            for h in range(q // 4):
-                z = h % 2
-                lo, o = 256 * q0 + 1024 * h, 32 * q0 + 64 * h
-                tt(ap("t%d" % z), ind(xall, ap("df", s_(o, o + 64))), ap(rep, s_(lo, lo + 1024)), A.add)
-                ts(ap("mb%d" % z), ap("t%d" % z), 0.0, A.max, 63.0, A.min)
-                second(c, h, xall, ap("df", s_(o + w, o + w + 64)), ap("mb%d" % z), (1, c, h) in VFUSED)
-                sums(c, h, True, True)
-            kq = ap("kp%d" % (c % 2), s_(0, w))
-            for i in (0, 1):
-                tt(ap("kd", s_(w * i, w * i + w)), kq, ap("dT", s_(32 * q0 + w * i, 32 * q0 + w * i + w)), A.add)
-            scan(ap("kk", s_(0, 2 * w)), ap("rmin", s_(0, 2 * w)), ap("kd", s_(0, 2 * w)), 134217728.0, A.max, A.min)
-            both, first = s_(2 * q0, 2 * q0 + 2 * q), s_(2 * q0, 2 * q0 + q)
-            cp(ap("di", both), ap("kk", s_(15, 2 * w, 16)))
-            ts(ap("dm2", both), ap("di", both), 2047, A.bitwise_and)
-            cp(ap("dlist", s_(q0, q0 + q)), ap("dm2", first))
-            ts(ap("al", both), ap("kk", s_(15, 2 * w, 16)), ap("thr"), A.is_lt)
-            tt(ap("ald", s_(q0, q0 + q)), ap("al", first), ap("dump", s_(q0, q0 + q)), A.mult)
+            q0, q = CH1[c]
+            kp, b, x = "ka%d" % (c % 2), s_(q0 // 2, (q0 + q) // 2), s_(0, 16 * q)
+            kq = flat(kp, 0, 16 * q)
+            mms([(kq, idb(), ap("kc3", x), True, False), (kq, idb(), ap("kc1", x), False, False)] +
+                [(flat(kp, 64 * c1, 64 * c1 + 64), flip("p", c1, gp), ap("ta", b, gp), False, False) for c1 in (0, 1) for gp in (0, 1)])
+            for h in range(q0 // 4, (q0 + q) // 4):
+                moved(1, h, cands(0, h), "mb")
+                distance(1, h, xall, cands(1, h), "mb", "lw", kp, q0, q)
+            x, q8 = s_(16 * q0, 16 * (q0 + q)), s_(q0, q0 + q)
+            scan(ap("kk", x), ap("rn", s_(0, 16 * q)), kq, 0.0, A.add, A.min)
+            cp(ap("di", q8), ap("kk", s_(16 * q0 + 15, 16 * (q0 + q), 16)))
+            ts(ap("dm", q8), ap("di", q8), 2047, A.bitwise_and)
+            cp(ap("dlist", q8), ap("dm", q8))
+            cp(ap("s16", x), ind(ap("sue"), ap("dlist", q8)))
+            tt(ap("kf", x), kq, ap("fdt", x), A.add)
 
         def lanes():
-            cp(ap("df32"), ap("dm2"))
-            tt(ap("abd"), ap("df32"), ap("abf"), A.subtract)
+            scan(ap("kk", s_(256, 512)), ap("rn", s_(0, 256)), ap("kf"), 0.0, A.add, A.min)
+            cp(ap("di", s_(16, 32)), ap("kk", s_(271, 512, 16)))
+            ts(ap("dm", s_(16, 32)), ap("di", s_(16, 32)), 2047, A.bitwise_and)
+            ts(ap("al"), ap("kk", s_(15, 512, 16)), thr, A.is_lt)
+            tt(ap("ald"), ap("al", s_(0, 16)), ap("dump"), A.mult)
+            abn = ap("abn%d" % t)
+            tt(ap("abd"), ap("dm"), old, A.subtract)
             tt(ap("abd"), ap("abd"), ap("al"), A.mult)
-            tt(ap("abn"), ap("abf"), ap("abd"), A.add)
+            tt(abn, ap("abd"), old, A.add)
             if last:
-                for c, (q0, q) in enumerate(CH):
-                    store(T.ya[:, q0:q0 + q], ap("abn", s_(2 * q0, 2 * q0 + q)), "o%d" % (2 * c))
-                    store(T.yb[:, q0:q0 + q], ap("abn", s_(2 * q0 + q, 2 * q0 + 2 * q)), "o%d" % (2 * c + 1))
+                store(T.ya[:], ap("abn2", s_(0, 2)), "o0")
+                store(T.yb[:], ap("abn2", s_(2, 4)), "o1")
                 return
             k = t + 1
-            cp(ap("abo%d" % k), ap("abn"))
-            i = remote(ap("abo%d" % k), [(nxt, "ab%d" % k, "aab%d" % k) if r1 is None else (r1, "rab%d" % k, "rab%d" % k)])
-            arrive("ab%d" % k, "aab%d" % k, prv, i, 8000)
+            i = remote(abn, [(nxt, "abf%d" % k, "aab%d" % k) if r1 is None else (r1, "rab%d" % k, "rab%d" % k)])
+            arrive("abf%d" % k, "aab%d" % k, prv, i, 8000)
+            act(ap("junk"), ap("al", s_(0, 16)), F.Copy, accum=ap("asum"))
 
         def threshold():
-            asum, al = ap("asum"), ap("al")
-            op("V", 124, [asum], [al], lambda q: q.tensor_reduce(asum["ap"], al["ap"], AxisListType.X, A.add))
-            mms([(ap("ps1", s_(0, 1)), ap("onef"), ap("asum"), True, True)])
-            ts(ap("ai", s_(0, 1)), ap("ps1", s_(0, 1)), -0.5, A.mult, 2048.0, A.add)
+            o = ap("ps1", s_(0, 1))
+            mms([(o, ap("onef", s_(0, 128)), ap("asum"), True, True)])
+            ts(ap("ai", s_(0, 1)), o, -1.0, A.mult, 2048.0, A.add)
             ts(ap("ai", s_(1, 2)), ap("ai", s_(0, 1)), 63, A.bitwise_and)
-            tt(ap("tha"), ap("thq"), ap("ai", s_(1, 2)), A.add)
-            ts(ap("thr"), ap("tha"), 32768.0, A.mult, -16777216.0, A.add)
+            ts(ap("thr"), ap("ai", s_(1, 2)), 32768.0, A.mult, ap("thq"), A.add)
 
         def step2a(c):
             q0, q = CH[c]
-            w = 16 * q
-            x = s_(0, w)
-            s16, n16 = "s16%d" % c, "n16%d" % c
-            u = ap("ps%d" % (c % 2), x)
-            cp(ap(s16), ind(ap("sue", s_(0, 1280)), ap("dlist", s_(q0, q0 + q))))
-            for h in range(q // 4):
-                z, lo = h % 2, 256 * q0 + 1024 * h
-                tt(ap("t%d" % z), ind(xall, ap(s16, s_(64 * h, 64 * h + 64))), ap(rep, s_(lo, lo + 1024)), A.add)
-                ts(ap("e", s_(lo, lo + 1024)), ap("t%d" % z), 0.0, A.max, 63.0, A.min)
-                mms([(ap("ps%d" % (c % 2), s_(64 * h, 64 * h + 64)), ap("ww", j), ap("e", s_(lo + j, lo + 1024, 16)), j == 0, j == 15) for j in range(16)])
-            cp(ap("ui", x), u)
-            ts(ap("ua", x), ap("ui", x), 4095, A.bitwise_and)
-            ts(ap("ub", x), ap("ua", x), 1184.0, A.add)
-            tt(ap("uc", x), ap("ua", x), ap("ub", x), A.mult)
-            ts(ap("un", x), ap("uc", x), 5, A.arith_shift_right, 511, A.bitwise_and)
-            cp(ap(n16), ap("un", x))
-            b = s_(0, q // 2)
-            cp(ap("nh", b), ap(n16))
-            trans(ap("na", b), ap("nh", b))
-            kp = "kp%d" % (c % 2)
-            lst = [(ap(kp, x), ap("idb"), ap("kc3", x), True, False), (ap(kp, x), ap("idb"), ap("kc2", x), False, False)]
-            for k in range(q):
-                lst += [(ap(kp, s_(16 * k, 16 * k + 16)), ap(flipm[k % 2][gp]), ap("na", k // 2, gp), False, False) for gp in (0, 1)]
-            mms(lst)
+            for p0 in range(q0, q0 + q, K["hash"]):
+                p = min(K["hash"], q0 + q - p0)
+                turn[0] += 1
+                bank, x = "ps%d" % (turn[0] % 2), s_(16 * p0, 16 * (p0 + p))
+                for h in range(p0 // 4, (p0 + p) // 4):
+                    moved(2, h, ap("s16", s_(64 * h, 64 * h + 64)), "e")
+                    o = ap(bank, s_(64 * h - 16 * p0, 64 * h - 16 * p0 + 64))
+                    mms([(o, onto("ww", j), ap("e", s_(1024 * h + j, 1024 * h + 1024, 16)), j == 0, j == 15) for j in range(16)])
+                cp(ap("ui", x), ap(bank, s_(0, 16 * p)))
+                ts(ap("ua", x), ap("ui", x), 4095, A.bitwise_and)
+                ts(ap("ub", x), ap("ua", x), 1184.0, A.add)
+                tt(ap("uc", x), ap("ua", x), ap("ub", x), A.mult)
+                ts(ap("un", x), ap("uc", x), 5, A.arith_shift_right, 511, A.bitwise_and)
+                cp(ap("n16", x), ap("un", x))
 
         def step2b(c):
             q0, q = CH[c]
             w = 16 * q
-            n16 = "n16%d" % c
-            for h in range(q // 4):
-                lo = 256 * q0 + 1024 * h
-                second(c, h, base, ap(n16, s_(64 * h, 64 * h + 64)), ap("e", s_(lo, lo + 1024)), (2, c, h) in VFUSED)
-                sums(c, h, False, h == q // 4 - 1)
-            kq = ap("kp%d" % (c % 2), s_(0, w))
-            scan(ap("kk2", s_(0, w)), ap("rmax", s_(0, w)), kq, -134217728.0, A.min, A.max)
-            q8 = s_(q0, q0 + q)
-            i0, i1, i2 = s_(0, q), s_(QM, QM + q), s_(2 * QM, 2 * QM + q)
-            cp(ap("i2", i0), ap("kk2", s_(15, w, 16)))
-            ts(ap("i2", i1), ap("i2", i0), 511, A.bitwise_and)
-            ts(ap("i2", i2), ap("i2", i0), 9, A.arith_shift_right, 15, A.bitwise_and)
-            tt(ap("nef", q8), ap("i2", i1), ap("ald", q8), A.max)
-            cp(ap("ne16", q8), ap("nef", q8))
-            tt(ap("sma", i0), ap("ebase", q8), ap("i2", i2), A.subtract)
-            cp(ap("eo16", q8), ap("sma", i0))
-            cp(ap("nr", s_(0, w)), ind(ap("it"), ap("ne16", q8)))
-            eq, v = "eq%d" % c, w + 2
-            for k in range(q):
-                ts(ap(eq, s_(v * k + 2, v * k + v)), ap("nr", s_(0, w)), ap("nef", s_(q0 + k, q0 + k + 1)), A.is_equal)
-            scan(ap("we", s_(0, q * v)), ap(eq), ap("cw%d" % q), 0.0, A.add, A.mult)
-            ts(ap("sma", i1), ap("we", s_(v - 1, q * v, v)), 1536.0, A.is_gt)
-            tt(ap("sma", i2), ap("sma", i1), ap("dump", q8), A.mult)
-            tt(ap("smb", i0), ap("sma", i2), ap("nef", q8), A.max)
-            cp(ap("nw16", q8), ap("smb", i0))
-            cp(ap("ew%d" % c), ind(ap("e", s_(256 * q0, 256 * (q0 + q))), ap("eo16", q8)))
-            b = s_(0, q // 2)
-            cp(ap("c16", s_(0, w)), ind(ap("coe"), ap("nw16", q8)))
-            cp(ap("nh", b), ap("c16", s_(0, w)))
+            x, b, q8 = s_(16 * q0, 16 * (q0 + q)), s_(q0 // 2, (q0 + q) // 2), s_(q0, q0 + q)
+            for c1 in (0, 1):
+                cp(ap("nh", b, c1), ap("n16", s_(16 * q0 + 64 * c1, 16 * q0 + 64 * c1 + 64)))
             trans(ap("na", b), ap("nh", b))
+            kp = "kb%d" % (c % 2)
+            mms([(flat(kp, 0, w), idb(), ap("kc2", s_(0, w)), True, False)] +
+                [(flat(kp, 64 * c1, 64 * c1 + 64), flip("p", c1, gp), ap("na", b, gp), False, False) for c1 in (0, 1) for gp in (0, 1)])
+            for h in range(q0 // 4, (q0 + q) // 4):
+                distance(2, h, base, ap("n16", s_(64 * h, 64 * h + 64)), "e", "l2w", kp, q0, q)
+            scan(ap("kk2", x), ap("rx", s_(0, w)), flat(kp, 0, w), 0.0, A.mult, A.max)
+            eq, we, v = "eq%d" % c, "we%d" % c, w + 2
+            cp(ap("i0", q8), ap("kk2", s_(16 * q0 + 15, 16 * (q0 + q), 16)))
+            ts(ap("i1", q8), ap("i0", q8), 511, A.bitwise_and)
+            tt(ap("nef", q8), ap("i1", q8), ap("ald", q8), A.max)
+            cp(ap("ne16", q8), ap("nef", q8))
+            cp(ap(eq, s_(v - 1, q * v, v)), ap("nef", q8))
+            cp(ap("nr", x), ind(ap("it"), ap("ne16", q8)))
+            for k in range(q):
+                y = s_(q0 + k, q0 + k + 1)
+                ts(ap(eq, s_(v * k + 1, v * k + v - 1)), ap("nr", x), ap("nef", y), A.is_equal, ap("dump", y), A.mult)
+            scan(ap(we), ap("cw%d" % q), ap(eq), 0.0, A.add, A.max)
+            cp(ap("nw16", q8), ap(we, s_(v - 1, q * v, v)))
+            cp(ap("ch", x), ind(ap("coe"), ap("nw16", q8)))
+            trans(ap("ca", b), ap("ch", x))
             pz = "ps%d" % (c % 2)
-            mms([(ap(pz, s_(k, w, q)), ap(flipm[k % 2][gp]), ap("na", k // 2, gp), gp == 0, gp == 1) for k in range(q) for gp in (0, 1)])
-            cp(ap("ct%d" % c), ap(pz, s_(0, w)))
+            mms([(ap(pz, s_(k, w, q)), flip("p", k % 2, gp), ap("ca", (q0 + k) // 2, gp), gp == 0, gp == 1) for k in range(q) for gp in (0, 1)])
+            cp(ap("ct", x), ap(pz, s_(0, w)))
             for k in range(16):
-                if k < VFLAG[c]:
-                    cp(ind(ap(fv), ap("ct%d" % c, k)), ap("oneb", s_(0, w)))
+                row = ap("ct", s_(16 * q0 + q * k, 16 * q0 + q * k + q))
+                if k < K["vflag"][c]:
+                    cp(ind(ap("fv"), row), ap("oneb", s_(0, w)))
                 else:
-                    act(ind(ap(fs), ap("ct%d" % c, k)), ap("zf", s_(0, w)), F.Sigmoid)
+                    act(ind(ap("fs"), row), ap("onef", s_(0, w)), F.Silu)
+
+        def step3():
+            ts(ap("i2"), ap("i0"), 9, A.arith_shift_right, 15, A.bitwise_and)
+            tt(ap("sma"), ap("ebase"), ap("i2"), A.subtract)
+            cp(ap("eo16"), ap("sma"))
+            cp(ap("ew"), ind(ap("e"), ap("eo16")))
+            for q0, q in reversed(CH):
+                cp(ind(ap(cur, s_(X0, XE)), ap("nw16", s_(q0, q0 + q))), ap("ew", s_(16 * q0, 16 * (q0 + q))))
+            if last:
+                store(T.yx[:, 0:512], base, "o2")
+            else:
+                gcopy(ap(new, s_(X0, XB)), base)
 
         def step4():
-            for c in range(NC - 1, -1, -1):
-                q0, q = CH[c]
-                cp(ind(ap("xw"), ap("nw16", s_(q0, q0 + q))), ap("ew%d" % c))
-            act(ap("fsb"), ap(fs, s_(512, 1280)), F.Copy)
-            o48 = ap("kp0", s_(0, 48))
-            mms([(o48, ap("lr", r), ap(fv, s_(512 + r, 1280, 16)), r == 0, False) for r in range(16)])
-            mms([(o48, ap("lr", r), ap("fsb", s_(r, 768, 16)), False, r == 15) for r in range(16)])
-            ts(ap("up0"), o48, 0.0, A.is_gt)
-            tt(ap("upb"), ap("up0"), ap("fl"), A.max)
-            oa, ob = ap("kp0", s_(0, 48)), ap("kp0", s_(64, 112))
-            mms([(oa, ap("blk"), ap("upb"), True, True), (ob, ap("trx"), ap("upb"), True, True)])
-            scan(ap("r0"), oa, ap("z48"), 0.0, A.add, A.add)
-            tt(ap("r1"), ap("r0"), ob, A.add)
-            ts(ap("r2"), ap("r1"), 192.0, A.is_le)
-            tt(ap("r3"), ap("r2"), ap("upb"), A.mult)
-            tt(ap("r4"), ap("r1"), ap("dv1"), A.subtract)
-            tt(ap("r4"), ap("r4"), ap("r3"), A.mult)
-            tt(ap("r4"), ap("r4"), ap("dv"), A.add)
-            cp(ap("pos"), ap("r4"))
+            act(ap("fsb"), ap("fs", s_(512, 1280)), F.Copy)
+            o48 = ap("py", s_(0, 48))
+            mms(([(o48, idb(), ap("fl"), True, False)] if t else []) +
+                [(o48, onto("lw", r), ap("fsb", s_(r, 768, 16)), r == 0 and not t, False) for r in range(16)])
+            mms([(o48, onto("lw", r), ap("fv", s_(512 + r, 1280, 16)), False, r == 15) for r in range(16)])
+            up = ap("upb", s_(2, 50))
+            ts(up, o48, 0.0, A.is_gt)
+            o = ap("py", s_(512, 560))
+            mms([(o, ap("tri"), up, True, False), (o, ap("trx"), ap("upb", s_(1, 49)), False, True)])
+            scan(ap("r0"), o, ap("z48"), 255.0, A.add, A.add)
+            ts(ap("r1"), ap("r0"), 192.0, A.is_ge, 2048.0, A.mult)
+            tt(ap("r2"), ap("r0"), ap("r1"), A.max)
+            tt(ap("r3"), ap("r2"), ap("dv"), A.min)
+            cp(ap("pos"), ap("r3"))
             if not last:
-                tt(ap("fl"), ap("upb"), ap("r3"), A.subtract)
-            cp(ap("cmp", s_(0, 192)), ap("it", s_(1280, 1472)))
-            cp(ind(ap("cmp"), ap("pos")), ap("it", s_(512, 1280)))
-            tt(ap("cmm"), ap("cmp", s_(0, 192)), ap("dm"), A.mult)
-            scan(ap("cms"), ap("sm"), ap("cmm"), 0.0, A.mult, A.max)
-            cp(ap("vl"), ap("cms", s_(15, 192, 16)))
-            cp(ap("sv"), ind(ap("sue"), ap("vl")))
-            for i in range(4):
-                x = s_(768 * i, 768 * i + 768)
-                src = ind(xall, ap("sv", s_(48 * i, 48 * i + 48)))
-                if i < VREN:
-                    cp(ap("gr", x), src)
+                tt(ap("fl"), ap("r1"), up, A.min)
+            n = K["vcmp"]
+            cp(ind(ap("cmv"), ap("pos", s_(0, n))), ap("suf", s_(0, 16 * n)))
+            if n < 48:
+                act(ind(ap("cms"), ap("pos", s_(n, 48))), ap("suf", s_(16 * n, 768)), F.Silu)
+                tt(ap("mrg"), ap("cmv", s_(0, 192)), ap("cms", s_(0, 192)), A.add)
+                ts(ap("sv"), ap("mrg"), -64.0, A.add)
+            else:
+                ts(ap("sv"), ap("cmv", s_(0, 192)), -64.0, A.add)
+            n = 192 // K["nren"]
+            for i in range(K["nren"]):
+                x = s_(16 * n * i, 16 * n * (i + 1))
+                src = ind(xall, ap("sv", s_(n * i, n * (i + 1))))
+                if i < K["vren"]:
+                    ts(ap("gr", x), src, 0.5, A.mult, 0.375, A.add)
                 else:
-                    act(ap("gr", x), src, F.Identity)
-                scan(ap("mx", x), ap("rx"), ap("gr", x), 0.0, A.mult, A.max)
-                scan(ap("mn", x), ap("rn"), ap("gr", x), 0.0, A.max, A.min)
-            tt(ap("sm2"), ap("mx", s_(15, 3072, 16)), ap("mn", s_(15, 3072, 16)), A.add)
-            ts(ap("si"), ap("sm2"), 0.5, A.mult, -0.25, A.add)
-            cp(ind(ap("xw"), ap("vl")), ap("si"))
+                    act(ap("gr", x), src, F.Identity, 0.375, 0.5)
+                for j in range(16 * n * i, 16 * n * (i + 1), 768):
+                    z = s_(j, min(j + 768, 16 * n * (i + 1)))
+                    y = s_(0, z.stop - z.start)
+                    scan(ap("mx", z), ap("rx", y), ap("gr", z), 0.0, A.mult, A.max)
+                    scan(ap("mn", z), ap("rn", y), ap("gr", z), 0.0, A.add, A.min)
+                o = ap("py", s_(n * i, n * (i + 1)))
+                mms([(o, idb(), ap(m, s_(16 * n * i + 15, 16 * n * (i + 1), 16)), m == "mx", m == "mn") for m in ("mx", "mn")])
+            ts(ap(cur, s_(0, 192)), ap("py", s_(0, 192)), 12582912.0, A.add, 12582913.0, A.subtract)
+            n = K["vput"]
+            win = ap(cur, s_(0, XD))
+            cp(ap(new, s_(XB, XB + 16 * n)), ind(win, ap("pos", s_(0, n))))
+            if n < 48:
+                act(ap(new, s_(XB + 16 * n, XD)), ind(win, ap("pos", s_(n, 48))), F.Identity)
+            if last:
+                store(T.yx[:, 512:1280], ap(new, s_(XB, XD)), "o3")
 
-        for c in range(NC):
+        before()
+        for c in range(len(CH1)):
             step1(c)
-        step2a(0)
         lanes()
+        for c in range(len(CH)):
+            step2a(c)
+        for c in range(len(CH)):
+            step2b(c)
         if not last:
             threshold()
-        for c in range(NC):
-            if c:
-                step2a(c)
-            step2b(c)
+        step3()
         step4()
-        if last:
-            store(T.yx[:], xall, "ox")
 
     inputs()
-    consts_a()
+    consts()
     reps(0)
     hops = []
     if r1 is None:
@@ -555,8 +584,6 @@ def rank_program(g, core, T, topo):
     snt = remote(ap("dl0"), hops)
     arrive("dl1", "adl1", prv, snt, 8000)
     arrive("dl2", "adl2", pr2, snt, 8000)
-    consts_b()
-    consts_c()
     rnd(0)
     reps(1)
     rnd(1)
@@ -573,15 +600,20 @@ def rank_program(g, core, T, topo):
     prio = [0.0] * n
     for i in range(n - 1, -1, -1):
         o = ops[i]
-        prio[i] = o["cost"] + o["lat"] + max([prio[j] for j in succ[i]], default=0.0)
+        prio[i] = o["cost"] + o["lat"] + max([prio[j] + COST["wake"] for j in succ[i]], default=0.0)
     free = {}
     ready = {i: 0.0 for i in range(n) if npred[i] == 0}
     rt = [0.0] * n
     seq = []
     while ready:
-        best = min(max(free.get(ops[i]["eng"], 0.0), r) for i, r in ready.items())
-        cand = [i for i, r in ready.items() if max(free.get(ops[i]["eng"], 0.0), r) <= best + 1e-6]
-        i = max(cand, key=lambda x: (prio[x], -x))
+        best, _, i = min((max(free.get(ops[i]["eng"], 0.0), r), -prio[i], i) for i, r in ready.items())
+        mine = [j for j in ready if ops[j]["eng"] == ops[i]["eng"]]
+        j = max([j for j in mine if ready[j] <= best + K["look"]], key=lambda x: (prio[x], -x))
+        if ready[j] > best:
+            fit = [x for x in mine if ready[x] <= best and best + ops[x]["cost"] <= ready[j] + COST["wake"]]
+            j = max(fit, key=lambda x: (prio[x], -x)) if fit else j
+        i = j
+        best = max(best, ready[i])
         del ready[i]
         o = ops[i]
         free[o["eng"]] = best + o["cost"] if o["eng"] != "N" else 0.0
@@ -590,11 +622,10 @@ def rank_program(g, core, T, topo):
         seq.append(i)
         for j in succ[i]:
             npred[j] -= 1
-            k = fin + 40 if i in ops[j]["wait"] else best
+            k = fin + COST["wake"] if i in ops[j]["wait"] else best
             rt[j] = max(rt[j], k)
             if npred[j] == 0:
                 ready[j] = rt[j]
-    INFO["ops"] = ops
 
     queues = {"V": g.vector, "S": g.scalar, "T": g.tensor, "G": g, "Y": g.sync, "N": None}
     esem = {"V": "cv", "S": "cs", "T": "ct", "G": "cg"}

@@ -1,3 +1,4 @@
+import math
 from concourse.mybir import dt, AluOpType, AxisListType, ActivationFunctionType
 A = AluOpType
 F = ActivationFunctionType
@@ -8,18 +9,35 @@ Q2 = (8, 8)
 CH1, CH = [[(sum(z[:i]), q) for i, q in enumerate(z)] for z in (Q1, Q2)]
 QM = max(Q2)
 K = {
-    "look": 400,
-    "hash": 4,
+    "passes": 3,
+    "tries": 6000,
+    "moves": 8000,
+    "heat": 150,
+    "trust": False,
+    "pex": 1,
+    "nfs": 2,
+    "nfv": 1,
+    "wide": (),
+    "seed": 7,
+    "slack": 500,
+    "alike": False,
+    "order": "a0 b0 a1 b1 a2 b2 a3 b3 m0 c0 h0 c1 h1 m1 L d0 d1 c2 h2 c3 h3 M0 d2 d3 N M1 R",
+    "vct": (0, 1),
+    "fsb": False,
+    "pd": (),
+    "qd": (),
+    "sc": (),
+    "from": 0,
     "ps": (),
-    "qv": ((2, 3),),
-    "vflag": (2, 8),
+    "qv": ((1, 3), (2, 1), (2, 3)),
+    "vflag": (2, 9),
     "vrep": 8,
     "vren": 1,
     "nren": 4,
     "vcmp": 24,
     "vput": 24,
 }
-X0, XB, XD, XE = 192, 704, 1472, 1728
+X0, XB, XD, XE = 256, 768, 1536, 1808
 BIG = 67108864.0
 SCRATCH = {}
 
@@ -30,13 +48,15 @@ def declare(d, **kw):
             SCRATCH[n] = SB(list(w), d)
 
 
-declare(B2, xa_xb=[XE], wtb=[1], dl0_dl1_dl2_rdl=[256], rep0_rep1_rep2_mb_e_gb_tb=[4096], blk_tri_trx_rowg=[128], oneb=[max(128, 16 * QM)],
-        kc1_kc3=[16 * max(Q1)], kc2=[16 * QM], dw_xs_iw_inw_lw_l2w_ww=[160], rowr_rx_rn_fsb=[768], upb=[50], fl=[48], fv=[1536], gr_mx_mn=[3072])
-declare(I4, coe=[1536], sue=[1280], lai=[4, 2, 4], di_dm=[32], thi_pi=[1], pr=[3], ai=[2], ui_ua_ub_uc_un=[256], i0_i1_i2=[16], mrg=[192])
-declare(U2, ab16=[32], df=[512], dlist_ne16_nw16_eo16=[16], pos=[48], sv=[192], s16_n16_ct=[256])
+declare(B2, xa_xb=[XE], wtb=[1], dl0_dl1_dl2_rdl=[256], rep0_rep1_rep2_mb_e_gb_tb_tc=[4096], blk_tri_trx_rowg=[128], oneb=[max(128, 16 * QM)],
+        kc1_kc3=[16 * max(Q1)], kc2=[16 * QM], dw_xs_iw_inw_lw_l2w_ww_ik_ikn=[160], rowr_rx_rn_fb0_fb1_kw_f2=[768], upb=[50], fv0_fv1=[1552], gr_mx_mn=[3072])
+declare(I4, coe=[1552], sue=[1280], lai=[4, 2, 4], di_dm=[32], thi_pi=[1], pr=[5], ai=[2], ui_ua_ub_uc_un=[256], i0_i1_i2=[16], mrg=[192])
+declare(U2, ab16=[32], df=[512], dlist_ne16_nw16_eo16_nw2=[16], own=[8], pos_put=[48], sv=[192], s16_n16_ct=[256])
+declare(F4, c2_c3=[256], kt_ow1_ow2=[1], ow3=[8], u2_r4=[48])
+declare(B2, fl=[48])
 declare(F4, abf1_abf2_rab1_rab2_abn0_abn1_abn2=[4, 2, 4], abd_al=[32], pf=[4], opar_par_npar_nopar_p16_thf_thq_thr_asum_wtf=[1], e8=[128], onef=[max(128, 16 * QM)],
-        it=[1536], q16_dump_ebase_ald_nef_sma_junk=[16], v48_dv_z48_r0_r1_r2_r3=[48], kk=[512], kf_fdt_kk2=[256],
-        fs=[1536], cmv_cms=[XD], suf=[768])
+        it=[1552], q16_dump_ebase_ald_nef_sma_junk=[16], v48_dv_z48_r0_r1_r2_r3=[48], kk=[512], kf_fdt_kk2=[256],
+        fs0_fs1=[1552], cmv_cms=[XD], suf=[768])
 declare(H2, p0_p1_n0_n1=[160], dfh_ta=[16, 2, 16], nh_na_ca=[8, 2, 16], nr_ch=[256])
 SCRATCH["ab"] = SB([16, 16, 16], B2)
 SCRATCH["ew"] = SB([256], B2)
@@ -61,12 +81,13 @@ def pack(buf, d, names):
     SCRATCH[buf] = SB([n], d)
 
 
-pack("pkf", F4, "pf opar par npar nopar p16 thf thq thr asum q16 dump ebase ald nef sma junk v48 dv z48 r0 r1 r2 r3 abd al")
+pack("pkf", F4, "pf opar par npar nopar p16 thf thq thr asum q16 dump ebase ald nef sma junk v48 dv z48 r0 r1 r2 r3 abd al kt ow1 ow2 ow3 u2 r4 wtf")
 pack("pki", I4, "pi pr di dm ai i0 i1 i2")
-pack("pku", U2, "dlist ne16 nw16 eo16 pos ab16")
-SEMAPHORES = ["cv", "cs", "ct", "cg", "ls", "rdl", "rab1", "rab2", "adl1", "adl2", "aab1", "aab2"] + ["ld%d" % n for n in range(8)] + ["o%d" % n for n in range(4)]
+pack("pku", U2, "dlist ne16 nw16 eo16 pos put ab16 nw2 own")
+SEMAPHORES = ["cv", "cs", "ct", "cg", "ls", "rdl", "rab1", "rab2", "adl1", "adl2", "aab1", "aab2"] + ["ld%d" % n for n in range(8)] + ["o%d" % n for n in range(4)] + \
+    ["ad%d" % n for n in range(1, 25)]
 SIZE = {B2: 2, F4: 4, I4: 4, U2: 2, H2: 2}
-COST = {"cyc": 0.9, "ga": 1.56, "sc": 3.8, "wake": 60}
+COST = {"cyc": 0.83, "ga": 1.56, "sc": 3.8, "wake": 140, "mm": 10, "gdma": 800, "add": 4600, "far": 14000}
 
 
 def relay_of(src, dst, topo):
@@ -106,6 +127,134 @@ def s_(a, b, c=None):
     return slice(a, b, c)
 
 
+PLANS = {}
+
+
+def plan(ops):
+    n = len(ops)
+    cost = [o["cost"] for o in ops]
+    pred, succ = [[] for _ in ops], [[] for _ in ops]
+    for i, o in enumerate(ops):
+        for j in o["wait"] | o["order"]:
+            lag = ops[j]["lat"] + COST["wake"] if j in o["wait"] else 0.0
+            pred[i].append((j, lag))
+            succ[j].append((i, lag))
+
+    def place(urg, before, after, tail):
+        left = [len(x) for x in before]
+        free = [(urg[i], -i) for i in range(n) if not left[i]]
+        busy, at = {e: [] for e in "VSTGYN"}, [0.0] * n
+        while free:
+            top = max(free)
+            free.remove(top)
+            i = -top[1]
+            t0 = max([at[j] + cost[j] + lag for j, lag in before[i]], default=tail[i])
+            line = busy[ops[i]["eng"]]
+            k = len(line)
+            while k and line[k - 1][1] > t0:
+                k -= 1
+            while k < len(line) and line[k][0] < t0 + cost[i]:
+                t0 = max(t0, line[k][1])
+                k += 1
+            line.insert(k, (t0, t0 + cost[i]))
+            at[i] = t0
+            for j, _ in after[i]:
+                left[j] -= 1
+                if not left[j]:
+                    free.append((urg[j], -j))
+        return at
+
+    lat, zero = [o["lat"] for o in ops], [0.0] * n
+    urg = [0.0] * n
+    for i in range(n - 1, -1, -1):
+        urg[i] = cost[i] + max([urg[j] + lag for j, lag in succ[i]], default=lat[i])
+    best = None
+    for urg in (urg, [-i for i in range(n)]):
+        for _ in range(K["passes"]):
+            at = place(urg, pred, succ, zero)
+            end = max(at[i] + cost[i] + lat[i] for i in range(n))
+            if best is None or end < best[0]:
+                best = (end, at)
+            back = place([at[i] + cost[i] for i in range(n)], succ, pred, lat)
+            urg = [back[i] + cost[i] for i in range(n)]
+    part = {}
+    for i, o in enumerate(ops):
+        part.setdefault((o["task"], o["eng"]), []).append(i)
+    part = list(part.values())
+    seed, now = K["seed"], best
+    for k in range(K["tries"]):
+        pick = []
+        for m in (len(part), 8001, 4):
+            seed = (seed * 1103515245 + 12345) % 2147483648
+            pick.append((seed >> 8) % m)
+        urg = [-x for x in now[1]]
+        for i in part[pick[0]]:
+            if pick[2] == 3 or ops[i]["round"] == pick[2] or K["alike"]:
+                urg[i] += pick[1] - 4000
+        at = place(urg, pred, succ, zero)
+        end = max(at[i] + cost[i] + lat[i] for i in range(n))
+        if end <= now[0] + K["slack"] * (1 - k / K["tries"]):
+            now = (end, at)
+            best = min(best, now)
+    line = {}
+    for i in sorted(range(n), key=lambda i: (best[1][i], i)):
+        line.setdefault(ops[i]["eng"] if ops[i]["eng"] != "N" else i, []).append(i)
+
+    def run():
+        prev, nxt = [-1] * n, [-1] * n
+        for s in line.values():
+            for a, b in zip(s, s[1:]):
+                prev[b], nxt[a] = a, b
+        left = [len(pred[i]) + (prev[i] >= 0) for i in range(n)]
+        free = [i for i in range(n) if not left[i]]
+        fin, why, done = [0.0] * n, [-1] * n, 0
+        while free:
+            i = free.pop()
+            done += 1
+            w = prev[i]
+            t0 = fin[w] if w >= 0 else 0.0
+            for j, lag in pred[i]:
+                if fin[j] + lag > t0:
+                    t0, w = fin[j] + lag, j
+            fin[i], why[i] = t0 + cost[i], w
+            for j in [x for x, _ in succ[i]] + [nxt[i]] * (nxt[i] >= 0):
+                left[j] -= 1
+                if not left[j]:
+                    free.append(j)
+        if done < n:
+            return None
+        end, i = max((fin[i] + lat[i], i) for i in range(n))
+        held = []
+        while i >= 0:
+            if why[i] >= 0 and why[i] == prev[i]:
+                held.append(i)
+            i = why[i]
+        return end, fin, held
+
+    now = run()
+    for k in range(K["moves"]):
+        pick = []
+        for m in (len(now[2]), 2, 5, 1000):
+            seed = (seed * 1103515245 + 12345) % 2147483648
+            pick.append((seed >> 8) % m)
+        i = now[2][pick[0]]
+        s = line[ops[i]["eng"]]
+        old, p, d = list(s), s.index(i), (1, 1, 2, 3, 5)[pick[2]]
+        if pick[1]:
+            s.insert(max(0, p - d), s.pop(p))
+        else:
+            s.insert(p - 1 + d, s.pop(p - 1))
+        new = run()
+        if new and new[0] - now[0] <= -math.log((pick[3] + 1) / 1000) * K["heat"] * (1 - k / K["moves"]):
+            now = new
+            if now[0] < best[0]:
+                best = (now[0], [now[1][i] - cost[i] for i in range(n)])
+        else:
+            s[:] = old
+    K["end"] = best[0]
+    return best[1]
+
+
 def rank_program(g, core, T, topo):
     rank = T.rank_of(core)
     if rank is None:
@@ -117,6 +266,7 @@ def rank_program(g, core, T, topo):
         return
     ops = []
     acc = {}
+    task = ["", 0]
     cyc = COST["cyc"]
 
     def ap(name, *ix, p=None):
@@ -163,6 +313,8 @@ def rank_program(g, core, T, topo):
                         continue
                     if psum and eng == "T" and ops[j]["eng"] == "T":
                         order.add(j)
+                    elif K["trust"] and kind == "w" and eng == ops[j]["eng"] and eng in "VS" and sem is None and ops[j]["sem"] is None:
+                        order.add(j)
                     else:
                         wait.add(j)
         for kind, keys in (("r", rk), ("w", wk)):
@@ -171,7 +323,8 @@ def rank_program(g, core, T, topo):
                 if kind == "w":
                     lst[:] = [x for x in lst if x[0] & ~m]
                 lst.append((m, i, kind))
-        ops.append({"eng": eng, "cost": cost, "fn": fn, "wait": wait, "order": order - wait, "sem": sem, "val": val, "lat": lat})
+        ops.append({"eng": eng, "cost": cost, "fn": fn, "wait": wait, "order": order - wait, "sem": sem, "val": val, "lat": lat,
+                    "task": task[0] or (outs + ins)[0]["k"][0][0], "round": task[1]})
         return i
 
     def vcost(o, ins, tt=False):
@@ -215,7 +368,7 @@ def rank_program(g, core, T, topo):
             op("S", cost, [o], [i], lambda q: q.activation(o["ap"], i["ap"], f, bias, scale))
 
     def mms(lst):
-        cost = 30 + cyc * sum(max(64, x[2]["n"]) * (4 if x[2]["b"] == 4 else 1) + 10 for x in lst)
+        cost = sum(COST["mm"] + cyc * max(64, x[2]["n"]) * (4 if x[2]["b"] == 4 else 1) for x in lst)
 
         def fn(q):
             for o, l, r, a, z in lst:
@@ -229,6 +382,12 @@ def rank_program(g, core, T, topo):
 
     def store(dst, buf, sem):
         op("Y", 60, [], [buf], lambda _q: g.sync.dma_start(dst, buf["ap"]), sem=sem, val=16, lat=2500)
+
+    adds = [0]
+
+    def add(o, i):
+        adds[0] += 1
+        op("G", COST["gdma"], [o], [o, i], lambda q: q.dma_start(o["ap"], i["ap"], accum_op=A.add), sem="ad%d" % adds[0], val=16, lat=COST["add"])
 
     def iota(o, pat, base, mult):
         if SCRATCH[o["k"][0][0]][2] == I4:
@@ -244,12 +403,11 @@ def rank_program(g, core, T, topo):
 
     loc = [0]
 
-    def remote(stage, hops):
-        for dst, land, rsem in hops:
-            def fn(q, dst=dst, land=land, rsem=rsem):
+    def remote(stage, hops, cost=600):
+        def fn(q):
+            for dst, land, rsem in hops:
                 loc[0] += send(g, T, topo, core, dst, T[land][:], stage["ap"], rsem)
-            i = op("G", 600, [], [stage], fn, sem="ls", val=0)
-        return i
+        return op("G", cost, [], [stage], fn, sem="ls", val=0)
 
     def arrive(land, rsem, src, after, lat):
         rl = relay_of(src, core, topo)
@@ -282,14 +440,14 @@ def rank_program(g, core, T, topo):
     def consts():
         iota(ap("pi"), [[0, 1]], 0, 1)
         iota(ap("dw"), [[1, 160]], -16, -1)
+        iota(ap("rowr"), [[0, 48], [1, 16]], 0, 0)
         iota(ap("xs"), [[1, 160]], -15, 0)
         iota(ap("kc1"), [[0, max(Q1)], [2048, 16]], 0, 0)
-        iota(ap("rowr"), [[0, 48], [1, 16]], 0, 0)
         iota(ap("rowg"), [[16, 8], [0, 16]], 0, 0)
         iota(ap("p16"), [[0, 1]], 0, 16)
         for n, v in enumerate((15, 112, 16)):
             ts(ap("pr", s_(n, n + 1)), ap("pi"), v, A.bitwise_and)
-        cp(ap("pf", s_(0, 3)), ap("pr"))
+        cp(ap("pf", s_(0, 3)), ap("pr", s_(0, 3)))
         half, first = ap("pf", s_(2, 3)), ap("pf", s_(1, 2))
         for n, a, b in (("par", 1, 0), ("opar", -1, 1), ("npar", -1, 0), ("nopar", 1, -1)):
             ts(ap(n), half, a / 16.0, A.mult, float(b), A.add)
@@ -311,11 +469,11 @@ def rank_program(g, core, T, topo):
         mms([(o, ap("e8", p=8), ap("thf", p=8), True, True)])
         ts(ap("thq"), o, 32768.0, A.mult, -16777216.0, A.add)
         iota(ap("kc2"), [[0, QM], [-512, 16]], 7680, 0)
-        iota(ap("q16"), [[16, 16]], 1280, 0)
+        iota(ap("q16"), [[16, 16]], 1296, 0)
         ts(ap("dump"), ap("q16"), rcol(), A.add)
-        ts(ap("ebase"), ap("dump"), 16.0, A.mult, 15.0 - 16 * 1280, A.add)
-        iota(ap("it"), [[1, 1536]], 0, 0)
-        iota(ap("coe", s_(1280, 1536)), [[1, 256]], 1280, 0)
+        ts(ap("ebase"), ap("dump"), 16.0, A.mult, 15.0 - 16 * 1296, A.add)
+        iota(ap("it"), [[1, 1552]], 0, 0)
+        iota(ap("coe", s_(1280, 1552)), [[1, 272]], 1280, 0)
         for c, (q0, q) in enumerate(CH):
             fill(ap("eq%d" % c, s_(0, None, 16 * q + 2)), 0.0)
         for q in sorted({q for _, q in CH}):
@@ -331,10 +489,22 @@ def rank_program(g, core, T, topo):
         iota(ap("v48"), [[16, 48]], XB, 0)
         ts(ap("dv"), ap("v48"), rcol(), A.add)
         select(ap("tri"), ap("blk"), [[1, 128]], A.is_ge, 0.0, 0, -1)
-        select(ap("tri"), ap("tri"), [[1, 128]], A.not_equal, -255.0, 0, -1)
-        select(ap("trx"), ap("blk"), [[-1, 128]], A.is_ge, 0.0, 0, 1)
-        select(ap("trx"), ap("trx"), [[1, 128]], A.not_equal, 256.0, 0, -1)
+        select(ap("trx"), ap("blk"), [[-1, 128]], A.is_gt, 0.0, 0, 1)
+        act(ap("ik"), ap("iw"), F.Identity, 0.0, 2048.0)
+        act(ap("ikn"), ap("iw"), F.Identity, 0.0, -2048.0)
+        for x in ("xa", "xb"):
+            iota(ap(x, s_(192, X0)), [[0, X0 - 192]], 0, 0)
         ts(ap("suf"), ap("sue", s_(512, 1280)), 64.0, A.add)
+        ts(ap("kw"), ap("rowr"), rcol(), A.is_gt, 32.0, A.mult)
+        scan(ap("junk"), ap("kw", s_(0, 16)), ap("oneb", s_(0, 16)), 0.0, A.mult, A.add)
+        ts(ap("kt"), ap("junk", s_(15, 16)), 0.5, A.mult)
+        if K["vct"]:
+            ts(ap("pr", s_(3, 4)), ap("pi"), 7, A.bitwise_and)
+            ts(ap("pr", s_(4, 5)), ap("pi"), 3, A.arith_shift_right, 1, A.bitwise_and)
+            ts(ap("ow1"), ap("pr", s_(3, 4)), 32.0, A.mult, half, A.add)
+            tt(ap("ow2"), ap("ow1"), ap("pr", s_(4, 5)), A.add)
+            iota(ap("ow3"), [[2, 8]], 0, 0)
+            ts(ap("own"), ap("ow3"), ap("ow2"), A.add)
 
     def reps(t):
         for k in range(16):
@@ -346,7 +516,7 @@ def rank_program(g, core, T, topo):
             else:
                 act(o, i, F.Copy)
 
-    def rnd(t):
+    def rnd(t, ahead=False):
         rep, last = "rep%d" % t, t == 2
         cur, new = ("xa", "xb") if t % 2 == 0 else ("xb", "xa")
         xall, base = ap(cur, s_(X0, XD)), ap(cur, s_(X0, XB))
@@ -362,11 +532,18 @@ def rank_program(g, core, T, topo):
             for c1 in (0, 1):
                 cp(ap("dfh", a_, c1), ap("df", s_(256 * c1, 256 * c1 + 256)))
             trans(ap("ta"), ap("dfh"))
-            mms([(ap("kb1", s_(64 * h, 64 * h + 64)), flip(tab, h % 2, gp), ap("ta", s_(b + h // 2 * 4, b + h // 2 * 4 + 4), gp),
+            mms([(ap("ka1", s_(64 * h, 64 * h + 64)), flip(tab, h % 2, gp), ap("ta", s_(b + h // 2 * 4, b + h // 2 * 4 + 4), gp),
                   tab == "p" and gp == 0, tab == "n" and gp == 1) for h in range(4) for tab, b in (("p", 8), ("n", 0)) for gp in (0, 1)])
-            act(ap("fdt"), ap("kb1", s_(0, 256)), F.Copy)
-            iota(ap("fs", s_(512, 1280)), [[0, 768]], 0, 0)
-            iota(ap("fv", s_(512, 1280)), [[0, 768]], 0, 0)
+            act(ap("fdt"), ap("ka1", s_(0, 256)), F.Copy)
+            for c, (q0, q) in enumerate(CH1):
+                kp, b, x = "ka%d" % c, s_(q0 // 2, (q0 + q) // 2), s_(0, 16 * q)
+                kq = flat(kp, 0, 16 * q)
+                mms([(kq, idb(), ap("kc3", x), True, False), (kq, idb(), ap("kc1", x), False, False)] +
+                    [(flat(kp, 64 * c1, 64 * c1 + 64), flip("p", c1, gp), ap("ta", b, gp), False, False) for c1 in (0, 1) for gp in (0, 1)])
+
+        def clear():
+            for x in ["fs%d" % n for n in range(K["nfs"])] + ["fv%d" % n for n in range(K["nfv"])]:
+                iota(ap(x, s_(512, 1280)), [[0, 768]], 0, 0)
             iota(ap("cmv", s_(0, 192)), [[0, 192]], 0, 0)
             if K["vcmp"] < 48:
                 iota(ap("cms", s_(0, 192)), [[0, 192]], 0, 0)
@@ -384,45 +561,60 @@ def rank_program(g, core, T, topo):
                 for i in (0, 1):
                     ts(ap(dst, s_(lo + 512 * i, lo + 512 * i + 512)), two(i, idb(), "tb", idb(), rep, lo), 0.0, A.max, 63.0, A.min)
             else:
-                tt(ap("tb", x), ind(xall, off), ap(rep, x), A.add)
-                ts(ap(dst, x), ap("tb", x), 0.0, A.max, 63.0, A.min)
+                if (step, h) in K["pd"] and t >= K["from"]:
+                    act(ap("tb", x), ind(xall, off), F.Identity)
+                    add(ap("tb", x), ap(rep, x))
+                else:
+                    tt(ap("tb", x), ind(xall, off), ap(rep, x), A.add)
+                if (step, h) in K["sc"]:
+                    act(ap("tc", x), ap("tb", x), F.Relu, 63.0, -1.0)
+                    act(ap(dst, x), ap("tc", x), F.Relu, 63.0, -1.0)
+                else:
+                    ts(ap(dst, x), ap("tb", x), 0.0, A.max, 63.0, A.min)
 
         def distance(step, h, w, off, m, tab, kp, q0, q):
             x = s_(1024 * h, 1024 * h + 1024)
             if (step, h) in K["qv"]:
                 tt(ap("gb", x), ind(w, off), ap(m, x), A.subtract)
                 act(ap("ab", s_(4 * h, 4 * h + 4)), ap("gb", x), F.Abs)
+            elif (step, h) in K["qd"] and t >= K["from"]:
+                act(ap("gb", x), ind(w, off), F.Identity, 0.0, -1.0)
+                add(ap("gb", x), ap(m, x))
+                act(ap("ab", s_(4 * h, 4 * h + 4)), ap("gb", x), F.Abs)
             else:
+                task[0] += "g"
                 act(ap("gb", x), ind(w, off), F.Identity)
+                task[0] = task[0][:-1]
                 for i in (0, 1):
                     act(ap("ab", s_(4 * h + 2 * i, 4 * h + 2 * i + 2)), two(i, idb(), "gb", idn(), m, 1024 * h), F.Abs)
             o = flat(kp, 64 * h - 16 * q0, 64 * h - 16 * q0 + 64)
             end = 4 * h + 4 == q0 + q
             mms([(o, onto(tab, r), ap("ab", s_(4 * h, 4 * h + 4), r), False, end and r == 15) for r in range(16)])
 
-        def step1(c):
+        def first(h):
+            moved(1, h, cands(0, h), "mb")
+
+        def second(h):
+            distance(1, h, xall, cands(1, h), "mb", "lw", "ka%d" % (h // 2), *CH1[h // 2])
+
+        def least(c):
             q0, q = CH1[c]
-            kp, b, x = "ka%d" % (c % 2), s_(q0 // 2, (q0 + q) // 2), s_(0, 16 * q)
-            kq = flat(kp, 0, 16 * q)
-            mms([(kq, idb(), ap("kc3", x), True, False), (kq, idb(), ap("kc1", x), False, False)] +
-                [(flat(kp, 64 * c1, 64 * c1 + 64), flip("p", c1, gp), ap("ta", b, gp), False, False) for c1 in (0, 1) for gp in (0, 1)])
-            for h in range(q0 // 4, (q0 + q) // 4):
-                moved(1, h, cands(0, h), "mb")
-                distance(1, h, xall, cands(1, h), "mb", "lw", kp, q0, q)
-            x, q8 = s_(16 * q0, 16 * (q0 + q)), s_(q0, q0 + q)
+            x, q8, kq = s_(16 * q0, 16 * (q0 + q)), s_(q0, q0 + q), flat("ka%d" % c, 0, 16 * q)
+            ends = ap("kk", s_(16 * q0 + 15, 16 * (q0 + q), 16))
             scan(ap("kk", x), ap("rn", s_(0, 16 * q)), kq, 0.0, A.add, A.min)
-            cp(ap("di", q8), ap("kk", s_(16 * q0 + 15, 16 * (q0 + q), 16)))
+            cp(ap("di", q8), ends)
             ts(ap("dm", q8), ap("di", q8), 2047, A.bitwise_and)
             cp(ap("dlist", q8), ap("dm", q8))
             cp(ap("s16", x), ind(ap("sue"), ap("dlist", q8)))
             tt(ap("kf", x), kq, ap("fdt", x), A.add)
+            if c == len(CH1) - 1:
+                ts(ap("ald"), ap("kk", s_(15, 256, 16)), thr, A.is_lt, 1280.0, A.mult)
 
         def lanes():
             scan(ap("kk", s_(256, 512)), ap("rn", s_(0, 256)), ap("kf"), 0.0, A.add, A.min)
             cp(ap("di", s_(16, 32)), ap("kk", s_(271, 512, 16)))
             ts(ap("dm", s_(16, 32)), ap("di", s_(16, 32)), 2047, A.bitwise_and)
             ts(ap("al"), ap("kk", s_(15, 512, 16)), thr, A.is_lt)
-            tt(ap("ald"), ap("al", s_(0, 16)), ap("dump"), A.mult)
             abn = ap("abn%d" % t)
             tt(ap("abd"), ap("dm"), old, A.subtract)
             tt(ap("abd"), ap("abd"), ap("al"), A.mult)
@@ -433,7 +625,7 @@ def rank_program(g, core, T, topo):
                 return
             k = t + 1
             i = remote(abn, [(nxt, "abf%d" % k, "aab%d" % k) if r1 is None else (r1, "rab%d" % k, "rab%d" % k)])
-            arrive("abf%d" % k, "aab%d" % k, prv, i, 8000)
+            arrive("abf%d" % k, "aab%d" % k, prv, i, COST["far"])
             act(ap("junk"), ap("al", s_(0, 16)), F.Copy, accum=ap("asum"))
 
         def threshold():
@@ -443,35 +635,41 @@ def rank_program(g, core, T, topo):
             ts(ap("ai", s_(1, 2)), ap("ai", s_(0, 1)), 63, A.bitwise_and)
             ts(ap("thr"), ap("ai", s_(1, 2)), 32768.0, A.mult, ap("thq"), A.add)
 
-        def step2a(c):
-            q0, q = CH[c]
-            for p0 in range(q0, q0 + q, K["hash"]):
-                p = min(K["hash"], q0 + q - p0)
-                turn[0] += 1
-                bank, x = "ps%d" % (turn[0] % 2), s_(16 * p0, 16 * (p0 + p))
-                for h in range(p0 // 4, (p0 + p) // 4):
-                    moved(2, h, ap("s16", s_(64 * h, 64 * h + 64)), "e")
-                    o = ap(bank, s_(64 * h - 16 * p0, 64 * h - 16 * p0 + 64))
-                    mms([(o, onto("ww", j), ap("e", s_(1024 * h + j, 1024 * h + 1024, 16)), j == 0, j == 15) for j in range(16)])
-                cp(ap("ui", x), ap(bank, s_(0, 16 * p)))
-                ts(ap("ua", x), ap("ui", x), 4095, A.bitwise_and)
-                ts(ap("ub", x), ap("ua", x), 1184.0, A.add)
-                tt(ap("uc", x), ap("ua", x), ap("ub", x), A.mult)
-                ts(ap("un", x), ap("uc", x), 5, A.arith_shift_right, 511, A.bitwise_and)
-                cp(ap("n16", x), ap("un", x))
+        def third(h):
+            moved(2, h, ap("s16", s_(64 * h, 64 * h + 64)), "e")
+            o = ap("ps%d" % (h // 2), s_(64 * (h % 2), 64 * (h % 2) + 64)) if h // 2 in K["wide"] else ap("ps%d" % (h % 2), s_(0, 64))
+            mms([(o, onto("ww", j), ap("e", s_(1024 * h + j, 1024 * h + 1024, 16)), j == 0, j == 15) for j in range(16)])
 
-        def step2b(c):
+        def spot(h):
+            x, u = s_(64 * h, 64 * h + 64), ap("ps%d" % (h % 2), s_(0, 64))
+            if h // 2 in K["wide"]:
+                if h % 2 == 0:
+                    return
+                x, u = s_(64 * h - 64, 64 * h + 64), ap("ps%d" % (h // 2), s_(0, 128))
+            cp(ap("ui", x), u)
+            ts(ap("ua", x), ap("ui", x), 4095, A.bitwise_and)
+            ts(ap("ub", x), ap("ua", x), 1184.0, A.add)
+            tt(ap("uc", x), ap("ua", x), ap("ub", x), A.mult)
+            ts(ap("un", x), ap("uc", x), 5, A.arith_shift_right, 511, A.bitwise_and)
+            cp(ap("n16", x), ap("un", x))
+
+        def fourth(h):
+            c = h // 2
             q0, q = CH[c]
-            w = 16 * q
+            kp, b = "kb%d" % c, s_(q0 // 2, (q0 + q) // 2)
+            if h % 2 == 0:
+                mms([(flat(kp, 0, 16 * q), idb(), ap("kc2", s_(0, 16 * q)), True, False)])
+            else:
+                for c1 in (0, 1):
+                    cp(ap("nh", b, c1), ap("n16", s_(16 * q0 + 64 * c1, 16 * q0 + 64 * c1 + 64)))
+                trans(ap("na", b), ap("nh", b))
+                mms([(flat(kp, 64 * c1, 64 * c1 + 64), flip("p", c1, gp), ap("na", b, gp), False, False) for c1 in (0, 1) for gp in (0, 1)])
+            distance(2, h, base, ap("n16", s_(64 * h, 64 * h + 64)), "e", "l2w", kp, q0, q)
+
+        def largest(c):
+            q0, q = CH[c]
+            w, kp = 16 * q, "kb%d" % c
             x, b, q8 = s_(16 * q0, 16 * (q0 + q)), s_(q0 // 2, (q0 + q) // 2), s_(q0, q0 + q)
-            for c1 in (0, 1):
-                cp(ap("nh", b, c1), ap("n16", s_(16 * q0 + 64 * c1, 16 * q0 + 64 * c1 + 64)))
-            trans(ap("na", b), ap("nh", b))
-            kp = "kb%d" % (c % 2)
-            mms([(flat(kp, 0, w), idb(), ap("kc2", s_(0, w)), True, False)] +
-                [(flat(kp, 64 * c1, 64 * c1 + 64), flip("p", c1, gp), ap("na", b, gp), False, False) for c1 in (0, 1) for gp in (0, 1)])
-            for h in range(q0 // 4, (q0 + q) // 4):
-                distance(2, h, base, ap("n16", s_(64 * h, 64 * h + 64)), "e", "l2w", kp, q0, q)
             scan(ap("kk2", x), ap("rx", s_(0, w)), flat(kp, 0, w), 0.0, A.mult, A.max)
             eq, we, v = "eq%d" % c, "we%d" % c, w + 2
             cp(ap("i0", q8), ap("kk2", s_(16 * q0 + 15, 16 * (q0 + q), 16)))
@@ -485,23 +683,31 @@ def rank_program(g, core, T, topo):
                 ts(ap(eq, s_(v * k + 1, v * k + v - 1)), ap("nr", x), ap("nef", y), A.is_equal, ap("dump", y), A.mult)
             scan(ap(we), ap("cw%d" % q), ap(eq), 0.0, A.add, A.max)
             cp(ap("nw16", q8), ap(we, s_(v - 1, q * v, v)))
-            cp(ap("ch", x), ind(ap("coe"), ap("nw16", q8)))
-            trans(ap("ca", b), ap("ch", x))
-            pz = "ps%d" % (c % 2)
-            mms([(ap(pz, s_(k, w, q)), flip("p", k % 2, gp), ap("ca", (q0 + k) // 2, gp), gp == 0, gp == 1) for k in range(q) for gp in (0, 1)])
-            cp(ap("ct", x), ap(pz, s_(0, w)))
+            if c in K["vct"]:
+                for c1 in (0, 1):
+                    cp(ap("nw2", s_(c1, 2 * q, 2)), ap(we, s_(v - 1, q * v, v)))
+                cp(ap("c2"), ind(ap("coe"), ap("nw2")))
+                trans(ap("c3"), ap("c2"))
+                cp(ap("ct", x), ind(ap("c3"), ap("own")))
+            else:
+                cp(ap("ch", x), ind(ap("coe"), ap("nw16", q8)))
+                trans(ap("ca", b), ap("ch", x))
+                pz = "ps%d" % (c % 2)
+                mms([(ap(pz, s_(k, w, q)), flip("p", k % 2, gp), ap("ca", (q0 + k) // 2, gp), gp == 0, gp == 1) for k in range(q) for gp in (0, 1)])
+                cp(ap("ct", x), ap(pz, s_(0, w)))
+            task[0] = "F%d" % c
             for k in range(16):
                 row = ap("ct", s_(16 * q0 + q * k, 16 * q0 + q * k + q))
                 if k < K["vflag"][c]:
-                    cp(ind(ap("fv"), row), ap("oneb", s_(0, w)))
+                    cp(ind(ap("fv%d" % ((K["vflag"][c] - 1 - k) % K["nfv"])), row), ap("oneb", s_(0, w)))
                 else:
-                    act(ind(ap("fs"), row), ap("onef", s_(0, w)), F.Silu)
+                    act(ind(ap("fs%d" % (k % K["nfs"])), row), ap("onef", s_(0, w)), F.Silu)
 
         def step3():
             ts(ap("i2"), ap("i0"), 9, A.arith_shift_right, 15, A.bitwise_and)
             tt(ap("sma"), ap("ebase"), ap("i2"), A.subtract)
             cp(ap("eo16"), ap("sma"))
-            cp(ap("ew"), ind(ap("e"), ap("eo16")))
+            act(ap("ew"), ind(ap("e"), ap("eo16")), F.Identity)
             for q0, q in reversed(CH):
                 cp(ind(ap(cur, s_(X0, XE)), ap("nw16", s_(q0, q0 + q))), ap("ew", s_(16 * q0, 16 * (q0 + q))))
             if last:
@@ -510,20 +716,32 @@ def rank_program(g, core, T, topo):
                 gcopy(ap(new, s_(X0, XB)), base)
 
         def step4():
-            act(ap("fsb"), ap("fs", s_(512, 1280)), F.Copy)
+            up, left = ap("upb", s_(2, 50)), ap("upb", s_(1, 49))
             o48 = ap("py", s_(0, 48))
-            mms(([(o48, idb(), ap("fl"), True, False)] if t else []) +
-                [(o48, onto("lw", r), ap("fsb", s_(r, 768, 16)), r == 0 and not t, False) for r in range(16)])
-            mms([(o48, onto("lw", r), ap("fv", s_(512 + r, 1280, 16)), False, r == 15) for r in range(16)])
-            up = ap("upb", s_(2, 50))
-            ts(up, o48, 0.0, A.is_gt)
+            both = K["pex"] == 2
+            tabs = [("fb%d" % n, 0) for n in range(K["nfs"])] + [("fv%d" % n, 512) for n in range(K["nfv"] - 1, -both, -1)]
+            for n in range(K["nfs"]):
+                act(ap("fb%d" % n), ap("fs%d" % n, s_(512, 1280)), F.Copy)
+            if t:
+                mms([(o48, idb(), ap("fl"), True, False)])
+            for n, (x, a) in enumerate(tabs):
+                mms([(o48, onto("lw", r), ap(x, s_(a + r, a + 768, 16)), r + n + t == 0, r == 15 and n == len(tabs) - 1) for r in range(16)])
+            if both:
+                ts(up, o48, 0.0, A.is_gt)
+            else:
+                ts(ap("u2"), o48, -1e24, A.mult, ap("kt"), A.add)
+                scan(ap("f2"), ap("kw"), ap("fv0", s_(512, 1280)), 0.0, A.mult, A.add)
+                tt(up, ap("f2", s_(15, 768, 16)), ap("u2"), A.is_gt)
             o = ap("py", s_(512, 560))
-            mms([(o, ap("tri"), up, True, False), (o, ap("trx"), ap("upb", s_(1, 49)), False, True)])
-            scan(ap("r0"), o, ap("z48"), 255.0, A.add, A.add)
-            ts(ap("r1"), ap("r0"), 192.0, A.is_ge, 2048.0, A.mult)
+            mms([(o, ap("tri"), up, True, False), (o, ap("ikn", s_(16, 144)), up, False, False),
+                 (o, ap("trx"), left, False, False), (o, ap("ik", s_(16, 144)), left, False, True)])
+            scan(ap("r0"), o, ap("z48"), 2047.0, A.add, A.add)
+            tt(ap("r4"), ap("r0"), ap("dv"), A.min)
+            cp(ap("pos"), ap("r4"))
+            ts(ap("r1"), ap("r0"), 192.0, A.is_ge, 1e25, A.mult)
             tt(ap("r2"), ap("r0"), ap("r1"), A.max)
             tt(ap("r3"), ap("r2"), ap("dv"), A.min)
-            cp(ap("pos"), ap("r3"))
+            cp(ap("put"), ap("r3"))
             if not last:
                 tt(ap("fl"), ap("r1"), up, A.min)
             n = K["vcmp"]
@@ -552,24 +770,31 @@ def rank_program(g, core, T, topo):
             ts(ap(cur, s_(0, 192)), ap("py", s_(0, 192)), 12582912.0, A.add, 12582913.0, A.subtract)
             n = K["vput"]
             win = ap(cur, s_(0, XD))
-            cp(ap(new, s_(XB, XB + 16 * n)), ind(win, ap("pos", s_(0, n))))
+            cp(ap(new, s_(XB, XB + 16 * n)), ind(win, ap("put", s_(0, n))))
             if n < 48:
-                act(ap(new, s_(XB + 16 * n, XD)), ind(win, ap("pos", s_(n, 48))), F.Identity)
+                act(ap(new, s_(XB + 16 * n, XD)), ind(win, ap("put", s_(n, 48))), F.Identity)
             if last:
                 store(T.yx[:, 512:1280], ap(new, s_(XB, XD)), "o3")
 
-        before()
-        for c in range(len(CH1)):
-            step1(c)
-        lanes()
-        for c in range(len(CH)):
-            step2a(c)
-        for c in range(len(CH)):
-            step2b(c)
-        if not last:
-            threshold()
-        step3()
+        if ahead:
+            return before()
+        task[:] = ["clear", t]
+        clear()
+        tasks = {"a": first, "b": second, "m": least, "c": third, "h": spot, "d": fourth, "M": largest}
+        for x in K["order"].split():
+            task[0] = x
+            if x[0] in tasks:
+                tasks[x[0]](int(x[1]))
+            elif x == "L":
+                lanes()
+            elif x == "N" and not last:
+                threshold()
+                rnd(t + 1, True)
+            elif x == "R":
+                step3()
+        task[0] = "D"
         step4()
+        task[0] = "rep"
 
     inputs()
     consts()
@@ -581,51 +806,22 @@ def rank_program(g, core, T, topo):
         hops.append((nx2, "dl2", "adl2"))
     for r in sorted({x for x in (r1, r2) if x is not None}):
         hops.append((r, "rdl", "rdl"))
-    snt = remote(ap("dl0"), hops)
-    arrive("dl1", "adl1", prv, snt, 8000)
-    arrive("dl2", "adl2", pr2, snt, 8000)
+    snt = remote(ap("dl0"), hops, 4000)
+    arrive("dl1", "adl1", prv, snt, COST["far"] + 8000)
+    arrive("dl2", "adl2", pr2, snt, COST["far"] + 8000)
+    rnd(0, True)
     rnd(0)
     reps(1)
     rnd(1)
     reps(2)
     rnd(2)
 
-    n = len(ops)
-    succ = [[] for _ in range(n)]
-    npred = [0] * n
-    for i, o in enumerate(ops):
-        for j in o["wait"] | o["order"]:
-            succ[j].append(i)
-            npred[i] += 1
-    prio = [0.0] * n
-    for i in range(n - 1, -1, -1):
-        o = ops[i]
-        prio[i] = o["cost"] + o["lat"] + max([prio[j] + COST["wake"] for j in succ[i]], default=0.0)
-    free = {}
-    ready = {i: 0.0 for i in range(n) if npred[i] == 0}
-    rt = [0.0] * n
-    seq = []
-    while ready:
-        best, _, i = min((max(free.get(ops[i]["eng"], 0.0), r), -prio[i], i) for i, r in ready.items())
-        mine = [j for j in ready if ops[j]["eng"] == ops[i]["eng"]]
-        j = max([j for j in mine if ready[j] <= best + K["look"]], key=lambda x: (prio[x], -x))
-        if ready[j] > best:
-            fit = [x for x in mine if ready[x] <= best and best + ops[x]["cost"] <= ready[j] + COST["wake"]]
-            j = max(fit, key=lambda x: (prio[x], -x)) if fit else j
-        i = j
-        best = max(best, ready[i])
-        del ready[i]
-        o = ops[i]
-        free[o["eng"]] = best + o["cost"] if o["eng"] != "N" else 0.0
-        fin = best + o["cost"] + o["lat"]
-        o["start"], o["fin"] = best, fin
-        seq.append(i)
-        for j in succ[i]:
-            npred[j] -= 1
-            k = fin + COST["wake"] if i in ops[j]["wait"] else best
-            rt[j] = max(rt[j], k)
-            if npred[j] == 0:
-                ready[j] = rt[j]
+    if len(ops) not in PLANS:
+        PLANS[len(ops)] = plan(ops)
+    start = PLANS[len(ops)]
+    for o, t0 in zip(ops, start):
+        o["fin"] = t0 + o["cost"] + o["lat"]
+    seq = sorted(range(len(ops)), key=lambda i: (start[i], i))
 
     queues = {"V": g.vector, "S": g.scalar, "T": g.tensor, "G": g, "Y": g.sync, "N": None}
     esem = {"V": "cv", "S": "cs", "T": "ct", "G": "cg"}

@@ -10,18 +10,25 @@ CH1, CH = [[(sum(z[:i]), q) for i, q in enumerate(z)] for z in (Q1, Q2)]
 QM = max(Q2)
 K = {
     "passes": 3,
-    "tries": 6000,
-    "moves": 8000,
-    "heat": 150,
+    "tries": 2500,
+    "moves": 2500,
+    "starts": 5,
+    "more": 9000,
+    "joint": 1500,
+    "prices": ((0.3, (1.4, 1.7, 1.9)), (0.3, (1.05, 0.85, 0.65)), (0.4, (1, 1, 1))),
+    "heat": 250,
     "trust": False,
     "pex": 1,
     "nfs": 2,
     "nfv": 1,
     "wide": (),
-    "seed": 7,
-    "slack": 500,
+    "spare": {(1, 1): "kb", (1, 3): "kb", (2, 2): "ka", (2, 3): "ka"},
+    "sct": (),
+    "sal": True,
+    "seed": 61,
+    "slack": 150,
     "alike": False,
-    "order": "a0 b0 a1 b1 a2 b2 a3 b3 m0 c0 h0 c1 h1 m1 L d0 d1 c2 h2 c3 h3 M0 d2 d3 N M1 R",
+    "order": "a0 b0 a1 b1 a2 b2 a3 b3 m0 c0 h0 c1 h1 m1 L d0 c2 d1 h2 c3 h3 d2 M0 d3 N M1 R",
     "vct": (0, 1),
     "fsb": False,
     "pd": (),
@@ -29,9 +36,9 @@ K = {
     "sc": (),
     "from": 0,
     "ps": (),
-    "qv": ((1, 3), (2, 1), (2, 3)),
+    "qv": ((2, 1),),
     "vflag": (2, 9),
-    "vrep": 8,
+    "vrep": 12,
     "vren": 1,
     "nren": 4,
     "vcmp": 24,
@@ -49,14 +56,14 @@ def declare(d, **kw):
 
 
 declare(B2, xa_xb=[XE], wtb=[1], dl0_dl1_dl2_rdl=[256], rep0_rep1_rep2_mb_e_gb_tb_tc=[4096], blk_tri_trx_rowg=[128], oneb=[max(128, 16 * QM)],
-        kc1_kc3=[16 * max(Q1)], kc2=[16 * QM], dw_xs_iw_inw_lw_l2w_ww_ik_ikn=[160], rowr_rx_rn_fb0_fb1_kw_f2=[768], upb=[50], fv0_fv1=[1552], gr_mx_mn=[3072])
+        kc1_kc3=[16 * max(Q1)], kc2=[16 * QM], dw_xs_iw_inw_lw_l2w_ww_ik_ikn=[160], rowr_rx_rn_fb0_fb1_kw_f1_f2=[768], upb=[50], fv0_fv1=[1552], gr_mx_mn=[3072])
 declare(I4, coe=[1552], sue=[1280], lai=[4, 2, 4], di_dm=[32], thi_pi=[1], pr=[5], ai=[2], ui_ua_ub_uc_un=[256], i0_i1_i2=[16], mrg=[192])
-declare(U2, ab16=[32], df=[512], dlist_ne16_nw16_eo16_nw2=[16], own=[8], pos_put=[48], sv=[192], s16_n16_ct=[256])
-declare(F4, c2_c3=[256], kt_ow1_ow2=[1], ow3=[8], u2_r4=[48])
+declare(U2, ab16=[32], df=[512], dlist_ne16_nw16_eo16_own=[16], nw2=[32], pos_put=[48], sv=[192], s16_n16_ct=[256])
+declare(F4, c2_c3=[512], kt_ow1_ow2_r4n=[1], ow3=[8], u2_r4=[48])
 declare(B2, fl=[48])
 declare(F4, abf1_abf2_rab1_rab2_abn0_abn1_abn2=[4, 2, 4], abd_al=[32], pf=[4], opar_par_npar_nopar_p16_thf_thq_thr_asum_wtf=[1], e8=[128], onef=[max(128, 16 * QM)],
         it=[1552], q16_dump_ebase_ald_nef_sma_junk=[16], v48_dv_z48_r0_r1_r2_r3=[48], kk=[512], kf_fdt_kk2=[256],
-        fs0_fs1=[1552], cmv_cms=[XD], suf=[768])
+        fs0_fs1_cof=[1552], sgn=[32], cmv_cms=[XD], suf=[768])
 declare(H2, p0_p1_n0_n1=[160], dfh_ta=[16, 2, 16], nh_na_ca=[8, 2, 16], nr_ch=[256])
 SCRATCH["ab"] = SB([16, 16, 16], B2)
 SCRATCH["ew"] = SB([256], B2)
@@ -87,7 +94,7 @@ pack("pku", U2, "dlist ne16 nw16 eo16 pos put ab16 nw2 own")
 SEMAPHORES = ["cv", "cs", "ct", "cg", "ls", "rdl", "rab1", "rab2", "adl1", "adl2", "aab1", "aab2"] + ["ld%d" % n for n in range(8)] + ["o%d" % n for n in range(4)] + \
     ["ad%d" % n for n in range(1, 25)]
 SIZE = {B2: 2, F4: 4, I4: 4, U2: 2, H2: 2}
-COST = {"cyc": 0.83, "ga": 1.56, "sc": 3.8, "wake": 140, "mm": 10, "gdma": 800, "add": 4600, "far": 14000}
+COST = {"cyc": 0.83, "ga": 1.56, "sc": 3.8, "wake": 140, "mm": 10, "gdma": 800, "add": 4600, "far": 10000}
 
 
 def relay_of(src, dst, topo):
@@ -131,6 +138,21 @@ PLANS = {}
 
 
 def plan(ops):
+    start, end = [0.0] * len(ops), 0.0
+    for t in range(3):
+        mine = [i for i, o in enumerate(ops) if o["round"] == t]
+        new = {i: k for k, i in enumerate(mine)}
+        part = [dict(ops[i], **{x: {new[j] for j in ops[i][x] if j in new} for x in ("wait", "order")}) for i in mine]
+        at = min(improve(part, K["tries"], K["moves"], K["seed"] + k) for k in range(K["starts"]))[1]
+        _, at, last = improve(part, 0, K["more"], K["seed"], at)
+        for i, t0 in zip(mine, at):
+            start[i] = end + t0
+        end += last + COST["wake"]
+    _, start, K["end"] = improve(ops, 0, K["joint"], K["seed"], start)
+    return start
+
+
+def improve(ops, tries, moves, seed, given=None):
     n = len(ops)
     cost = [o["cost"] for o in ops]
     pred, succ = [[] for _ in ops], [[] for _ in ops]
@@ -169,7 +191,9 @@ def plan(ops):
     for i in range(n - 1, -1, -1):
         urg[i] = cost[i] + max([urg[j] + lag for j, lag in succ[i]], default=lat[i])
     best = None
-    for urg in (urg, [-i for i in range(n)]):
+    if given:
+        best = (0.0, given)
+    for urg in (urg, [-i for i in range(n)]) if given is None else ():
         for _ in range(K["passes"]):
             at = place(urg, pred, succ, zero)
             end = max(at[i] + cost[i] + lat[i] for i in range(n))
@@ -181,19 +205,21 @@ def plan(ops):
     for i, o in enumerate(ops):
         part.setdefault((o["task"], o["eng"]), []).append(i)
     part = list(part.values())
-    seed, now = K["seed"], best
-    for k in range(K["tries"]):
+    now = best
+    for k in range(tries):
         pick = []
-        for m in (len(part), 8001, 4):
+        for m in (len(part), 2001, 3, 5, 64, 1000):
             seed = (seed * 1103515245 + 12345) % 2147483648
             pick.append((seed >> 8) % m)
         urg = [-x for x in now[1]]
-        for i in part[pick[0]]:
-            if pick[2] == 3 or ops[i]["round"] == pick[2] or K["alike"]:
-                urg[i] += pick[1] - 4000
+        some = part[pick[0]]
+        if pick[3] < 2:
+            some = some[pick[4] % len(some):][:1 + 2 * pick[3]]
+        for i in some:
+            urg[i] += (pick[1] - 1000) * (1, 3, 6)[pick[2]]
         at = place(urg, pred, succ, zero)
         end = max(at[i] + cost[i] + lat[i] for i in range(n))
-        if end <= now[0] + K["slack"] * (1 - k / K["tries"]):
+        if end - now[0] <= -math.log((pick[5] + 1) / 1000) * K["slack"] * (1 - k / tries):
             now = (end, at)
             best = min(best, now)
     line = {}
@@ -207,32 +233,39 @@ def plan(ops):
                 prev[b], nxt[a] = a, b
         left = [len(pred[i]) + (prev[i] >= 0) for i in range(n)]
         free = [i for i in range(n) if not left[i]]
-        fin, why, done = [0.0] * n, [-1] * n, 0
+        seq = []
         while free:
             i = free.pop()
-            done += 1
-            w = prev[i]
-            t0 = fin[w] if w >= 0 else 0.0
-            for j, lag in pred[i]:
-                if fin[j] + lag > t0:
-                    t0, w = fin[j] + lag, j
-            fin[i], why[i] = t0 + cost[i], w
-            for j in [x for x, _ in succ[i]] + [nxt[i]] * (nxt[i] >= 0):
+            seq.append(i)
+            for j in after[i] + [nxt[i]] * (nxt[i] >= 0):
                 left[j] -= 1
                 if not left[j]:
                     free.append(j)
-        if done < n:
+        if len(seq) < n:
             return None
-        end, i = max((fin[i] + lat[i], i) for i in range(n))
-        held = []
-        while i >= 0:
-            if why[i] >= 0 and why[i] == prev[i]:
-                held.append(i)
-            i = why[i]
-        return end, fin, held
+        total, held = 0.0, []
+        for weight, price in prices:
+            fin, why = [0.0] * n, [-1] * n
+            for i in seq:
+                w = prev[i]
+                t0 = fin[w] if w >= 0 else 0.0
+                for j, lag in pred[i]:
+                    if fin[j] + lag > t0:
+                        t0, w = fin[j] + lag, j
+                fin[i], why[i] = t0 + price[i], w
+            end, i = max((fin[i] + lat[i], i) for i in range(n))
+            total += weight * end
+            while i >= 0:
+                if why[i] >= 0 and why[i] == prev[i]:
+                    held.append(i)
+                i = why[i]
+        return total, fin, held, end
 
+    after = [[j for j, _ in x] for x in succ]
+    prices = [(w, [o["fix"] + (o["cost"] - o["fix"]) * k[o["kind"]] for o in ops]) for w, k in K["prices"]]
     now = run()
-    for k in range(K["moves"]):
+    best = (now[0], [now[1][i] - cost[i] for i in range(n)], now[3])
+    for k in range(moves):
         pick = []
         for m in (len(now[2]), 2, 5, 1000):
             seed = (seed * 1103515245 + 12345) % 2147483648
@@ -245,14 +278,13 @@ def plan(ops):
         else:
             s.insert(p - 1 + d, s.pop(p - 1))
         new = run()
-        if new and new[0] - now[0] <= -math.log((pick[3] + 1) / 1000) * K["heat"] * (1 - k / K["moves"]):
+        if new and new[0] - now[0] <= -math.log((pick[3] + 1) / 1000) * K["heat"] * (1 - k / moves) / (1 if given is None else 4):
             now = new
             if now[0] < best[0]:
-                best = (now[0], [now[1][i] - cost[i] for i in range(n)])
+                best = (now[0], [now[1][i] - cost[i] for i in range(n)], now[3])
         else:
             s[:] = old
-    K["end"] = best[0]
-    return best[1]
+    return best
 
 
 def rank_program(g, core, T, topo):
@@ -324,7 +356,9 @@ def rank_program(g, core, T, topo):
                     lst[:] = [x for x in lst if x[0] & ~m]
                 lst.append((m, i, kind))
         ops.append({"eng": eng, "cost": cost, "fn": fn, "wait": wait, "order": order - wait, "sem": sem, "val": val, "lat": lat,
-                    "task": task[0] or (outs + ins)[0]["k"][0][0], "round": task[1]})
+                    "task": task[0] or (outs + ins)[0]["k"][0][0], "round": task[1],
+                    "fix": {"V": 50, "S": 65, "T": cost / 8, "G": 150}.get(eng, cost) if sem is None else cost,
+                    "kind": 2 if any(o["ind"] for o in outs) else 1 if any(o["ind"] for o in ins) else 0})
         return i
 
     def vcost(o, ins, tt=False):
@@ -362,6 +396,8 @@ def rank_program(g, core, T, topo):
         cost = 65 + cyc * (i["n"] * COST["ga"] if i["ind"] else o["n"] * COST["sc"] if o["ind"] else max(64, i["n"]))
         if accum is not None:
             op("S", cost + 20, [o, accum], [i], lambda q: q.activation(o["ap"], i["ap"], f, accum_out=accum["ap"]))
+        elif isinstance(bias, dict):
+            op("S", cost, [o], [i, bias], lambda q: q.activation(o["ap"], i["ap"], f, bias["ap"], scale))
         elif scale is None:
             op("S", cost, [o], [i], lambda q: q.activation(o["ap"], i["ap"], f))
         else:
@@ -430,12 +466,12 @@ def rank_program(g, core, T, topo):
         for n, (eng, buf, src, lat) in enumerate((
                 ("Y", ap("dl0"), T.dl, 2500), ("Y", ap("coe", s_(0, 1280)), T.co, 4500), ("Y", ap("xa", s_(X0, XD)), T.x0, 5500),
                 ("S", ap("lai", s_(0, 2)), T.la, 2500), ("S", ap("lai", s_(2, 4)), T.lb, 2500),
-                ("Y", ap("sue"), T.su, 8000), ("Y", ap("wtb"), T.wt, 8000), ("Y", ap("thi", p=8), T.th, 8000))):
+                ("Y", ap("sue"), T.su, 5000), ("Y", ap("wtb"), T.wt, 5000), ("Y", ap("thi", p=8), T.th, 5000))):
             i = load(eng, buf, src[:], n, lat)
             if n and ops[i - 1]["eng"] == eng:
                 ops[i]["order"].add(i - 1)
             if n == 5:
-                ops[i]["order"].add(i - 3)
+                ops[i]["wait"].add(i - 3)
 
     def consts():
         iota(ap("pi"), [[0, 1]], 0, 1)
@@ -456,22 +492,23 @@ def rank_program(g, core, T, topo):
         ts(ap("iw"), ap("dw"), 0.0, A.is_equal)
         ts(ap("inw"), ap("dw"), 0.0, A.is_equal, -1.0, A.mult)
         ts(ap("lw"), ap("xs"), first, A.is_equal, 32768.0, A.mult)
-        ts(ap("l2w"), ap("xs"), first, A.is_equal, 8192.0, A.mult)
+        ts(ap("l2w"), ap("xs"), first, A.is_equal, -32768.0, A.mult)
         act(ap("wtf"), ap("wtb"), F.Copy)
         ts(ap("ww"), ap("xs"), first, A.is_equal, ap("wtf"), A.mult)
         ts(ap("blk"), ap("rowg"), first, A.is_equal)
         fill(ap("kc3"), -16777216.0)
         act(ap("rx"), ap("rowr"), F.Sign)
         act(ap("rn"), ap("rx"), F.Silu, BIG, -BIG)
+        ops[-1]["cost"] += 1300
         cp(ap("thf", p=8), ap("thi", p=8))
         ts(ap("e8", p=8), ap("rowg", p=8), ap("p16", p=8), A.is_equal)
         o = ap("ps0", s_(0, 1))
         mms([(o, ap("e8", p=8), ap("thf", p=8), True, True)])
         ts(ap("thq"), o, 32768.0, A.mult, -16777216.0, A.add)
-        iota(ap("kc2"), [[0, QM], [-512, 16]], 7680, 0)
+        iota(ap("kc2"), [[0, QM], [2048, 16]], -32768, 0)
         iota(ap("q16"), [[16, 16]], 1296, 0)
         ts(ap("dump"), ap("q16"), rcol(), A.add)
-        ts(ap("ebase"), ap("dump"), 16.0, A.mult, 15.0 - 16 * 1296, A.add)
+        ts(ap("ebase"), ap("dump"), 16.0, A.mult, -16.0 * 1296, A.add)
         iota(ap("it"), [[1, 1552]], 0, 0)
         iota(ap("coe", s_(1280, 1552)), [[1, 272]], 1280, 0)
         for c, (q0, q) in enumerate(CH):
@@ -495,16 +532,20 @@ def rank_program(g, core, T, topo):
         for x in ("xa", "xb"):
             iota(ap(x, s_(192, X0)), [[0, X0 - 192]], 0, 0)
         ts(ap("suf"), ap("sue", s_(512, 1280)), 64.0, A.add)
-        ts(ap("kw"), ap("rowr"), rcol(), A.is_gt, 32.0, A.mult)
+        if K["sct"]:
+            cp(ap("cof", s_(0, 512)), ap("coe", s_(0, 512)))
+            iota(ap("cof", s_(512, 1552)), [[1, 1040]], 512, 0)
+        act(ap("r4n"), rcol(), F.Identity, 0.0, -4.0)
+        act(ap("kw"), ap("rowr"), F.Relu, ap("r4n"), 4.0)
         scan(ap("junk"), ap("kw", s_(0, 16)), ap("oneb", s_(0, 16)), 0.0, A.mult, A.add)
         ts(ap("kt"), ap("junk", s_(15, 16)), 0.5, A.mult)
-        if K["vct"]:
-            ts(ap("pr", s_(3, 4)), ap("pi"), 7, A.bitwise_and)
-            ts(ap("pr", s_(4, 5)), ap("pi"), 3, A.arith_shift_right, 1, A.bitwise_and)
+        for q in sorted({CH[c][1] for c in K["vct"]}):
+            ts(ap("pr", s_(3, 4)), ap("pi"), q - 1, A.bitwise_and)
+            ts(ap("pr", s_(4, 5)), ap("pi"), q.bit_length() - 1, A.arith_shift_right, 16 // q - 1, A.bitwise_and)
             ts(ap("ow1"), ap("pr", s_(3, 4)), 32.0, A.mult, half, A.add)
             tt(ap("ow2"), ap("ow1"), ap("pr", s_(4, 5)), A.add)
-            iota(ap("ow3"), [[2, 8]], 0, 0)
-            ts(ap("own"), ap("ow3"), ap("ow2"), A.add)
+            iota(ap("ow3", s_(0, q)), [[16 // q, q]], 0, 0)
+            ts(ap("own", s_(q, 2 * q)), ap("ow3", s_(0, q)), ap("ow2"), A.add)
 
     def reps(t):
         for k in range(16):
@@ -548,8 +589,8 @@ def rank_program(g, core, T, topo):
             if K["vcmp"] < 48:
                 iota(ap("cms", s_(0, 192)), [[0, 192]], 0, 0)
 
-        def two(i, a, na, b, nb, lo):
-            o = ap("py", s_(512 * i, 512 * i + 512))
+        def two(i, a, na, b, nb, lo, spare=None):
+            o = ap("%s%d" % (spare, i)) if spare else ap("py", s_(512 * i, 512 * i + 512))
             mms([(o, l, ap(n, s_(lo + 512 * i, lo + 512 * i + 512)), z == 0, z == 1) for z, (l, n) in enumerate(((a, na), (b, nb)))])
             return o
 
@@ -586,7 +627,7 @@ def rank_program(g, core, T, topo):
                 act(ap("gb", x), ind(w, off), F.Identity)
                 task[0] = task[0][:-1]
                 for i in (0, 1):
-                    act(ap("ab", s_(4 * h + 2 * i, 4 * h + 2 * i + 2)), two(i, idb(), "gb", idn(), m, 1024 * h), F.Abs)
+                    act(ap("ab", s_(4 * h + 2 * i, 4 * h + 2 * i + 2)), two(i, idb(), "gb", idn(), m, 1024 * h, K["spare"].get((step, h))), F.Abs)
             o = flat(kp, 64 * h - 16 * q0, 64 * h - 16 * q0 + 64)
             end = 4 * h + 4 == q0 + q
             mms([(o, onto(tab, r), ap("ab", s_(4 * h, 4 * h + 4), r), False, end and r == 15) for r in range(16)])
@@ -608,13 +649,15 @@ def rank_program(g, core, T, topo):
             cp(ap("s16", x), ind(ap("sue"), ap("dlist", q8)))
             tt(ap("kf", x), kq, ap("fdt", x), A.add)
             if c == len(CH1) - 1:
-                ts(ap("ald"), ap("kk", s_(15, 256, 16)), thr, A.is_lt, 1280.0, A.mult)
+                act(ap("sgn", s_(0, 16)), ap("kk", s_(15, 256, 16)), F.Sign, thr, -1.0)
+                for y in (0, 16):
+                    act(ap("al", s_(y, y + 16)), ap("sgn", s_(0, 16)), F.Relu)
+                act(ap("ald"), ap("al", s_(0, 16)), F.Identity, 16777216.0, 1280.0 - 33554432.0)
 
         def lanes():
             scan(ap("kk", s_(256, 512)), ap("rn", s_(0, 256)), ap("kf"), 0.0, A.add, A.min)
             cp(ap("di", s_(16, 32)), ap("kk", s_(271, 512, 16)))
             ts(ap("dm", s_(16, 32)), ap("di", s_(16, 32)), 2047, A.bitwise_and)
-            ts(ap("al"), ap("kk", s_(15, 512, 16)), thr, A.is_lt)
             abn = ap("abn%d" % t)
             tt(ap("abd"), ap("dm"), old, A.subtract)
             tt(ap("abd"), ap("abd"), ap("al"), A.mult)
@@ -654,29 +697,29 @@ def rank_program(g, core, T, topo):
             cp(ap("n16", x), ap("un", x))
 
         def fourth(h):
-            c = h // 2
+            c = max(c for c, (q0, q) in enumerate(CH) if q0 <= 4 * h)
             q0, q = CH[c]
-            kp, b = "kb%d" % c, s_(q0 // 2, (q0 + q) // 2)
-            if h % 2 == 0:
-                mms([(flat(kp, 0, 16 * q), idb(), ap("kc2", s_(0, 16 * q)), True, False)])
-            else:
+            kp, b = "kb%d" % (c % 2), s_(q0 // 2, (q0 + q) // 2)
+            if 4 * h == q0:
+                mms([(flat(kp, 0, 16 * q), idn(), ap("kc3", s_(0, 16 * q)), True, False), (flat(kp, 0, 16 * q), idb(), ap("kc2", s_(0, 16 * q)), False, False)])
+            if 4 * h + 4 == q0 + q:
                 for c1 in (0, 1):
-                    cp(ap("nh", b, c1), ap("n16", s_(16 * q0 + 64 * c1, 16 * q0 + 64 * c1 + 64)))
+                    cp(ap("nh", b, c1), ap("n16", s_(16 * q0 + 8 * q * c1, 16 * q0 + 8 * q * (c1 + 1))))
                 trans(ap("na", b), ap("nh", b))
-                mms([(flat(kp, 64 * c1, 64 * c1 + 64), flip("p", c1, gp), ap("na", b, gp), False, False) for c1 in (0, 1) for gp in (0, 1)])
+                mms([(flat(kp, 8 * q * c1, 8 * q * (c1 + 1)), flip("p", c1, gp), ap("na", b, gp), False, False) for c1 in (0, 1) for gp in (0, 1)])
             distance(2, h, base, ap("n16", s_(64 * h, 64 * h + 64)), "e", "l2w", kp, q0, q)
 
         def largest(c):
             q0, q = CH[c]
-            w, kp = 16 * q, "kb%d" % c
+            w, kp = 16 * q, "kb%d" % (c % 2)
             x, b, q8 = s_(16 * q0, 16 * (q0 + q)), s_(q0 // 2, (q0 + q) // 2), s_(q0, q0 + q)
-            scan(ap("kk2", x), ap("rx", s_(0, w)), flat(kp, 0, w), 0.0, A.mult, A.max)
+            scan(ap("kk2", x), ap("rn", s_(0, w)), flat(kp, 0, w), 0.0, A.add, A.min)
             eq, we, v = "eq%d" % c, "we%d" % c, w + 2
-            cp(ap("i0", q8), ap("kk2", s_(16 * q0 + 15, 16 * (q0 + q), 16)))
-            ts(ap("i1", q8), ap("i0", q8), 511, A.bitwise_and)
-            tt(ap("nef", q8), ap("i1", q8), ap("ald", q8), A.max)
-            cp(ap("ne16", q8), ap("nef", q8))
-            cp(ap(eq, s_(v - 1, q * v, v)), ap("nef", q8))
+            tt(ap("i0", q8), ap("kk2", s_(16 * q0 + 15, 16 * (q0 + q), 16)), ap("ald", q8), A.min)
+            ts(ap("i1", q8), ap("i0", q8), 2047, A.bitwise_and)
+            cp(ap("ne16", q8), ap("i1", q8))
+            cp(ap("nef", q8), ap("i1", q8))
+            cp(ap(eq, s_(v - 1, q * v, v)), ap("i1", q8))
             cp(ap("nr", x), ind(ap("it"), ap("ne16", q8)))
             for k in range(q):
                 y = s_(q0 + k, q0 + k + 1)
@@ -684,11 +727,15 @@ def rank_program(g, core, T, topo):
             scan(ap(we), ap("cw%d" % q), ap(eq), 0.0, A.add, A.max)
             cp(ap("nw16", q8), ap(we, s_(v - 1, q * v, v)))
             if c in K["vct"]:
+                y = s_(32 * q0, 32 * (q0 + q))
                 for c1 in (0, 1):
-                    cp(ap("nw2", s_(c1, 2 * q, 2)), ap(we, s_(v - 1, q * v, v)))
-                cp(ap("c2"), ind(ap("coe"), ap("nw2")))
-                trans(ap("c3"), ap("c2"))
-                cp(ap("ct", x), ind(ap("c3"), ap("own")))
+                    cp(ap("nw2", s_(2 * q0 + c1, 2 * (q0 + q), 2)), ap(we, s_(v - 1, q * v, v)))
+                if c in K["sct"]:
+                    act(ap("c2", y), ind(ap("cof"), ap("nw2", s_(2 * q0, 2 * (q0 + q)))), F.Identity)
+                else:
+                    cp(ap("c2", y), ind(ap("coe"), ap("nw2", s_(2 * q0, 2 * (q0 + q)))))
+                trans(ap("c3", y), ap("c2", y))
+                cp(ap("ct", x), ind(ap("c3", y), ap("own", s_(q, 2 * q))))
             else:
                 cp(ap("ch", x), ind(ap("coe"), ap("nw16", q8)))
                 trans(ap("ca", b), ap("ch", x))
@@ -704,8 +751,8 @@ def rank_program(g, core, T, topo):
                     act(ind(ap("fs%d" % (k % K["nfs"])), row), ap("onef", s_(0, w)), F.Silu)
 
         def step3():
-            ts(ap("i2"), ap("i0"), 9, A.arith_shift_right, 15, A.bitwise_and)
-            tt(ap("sma"), ap("ebase"), ap("i2"), A.subtract)
+            ts(ap("i2"), ap("i0"), 11, A.arith_shift_right, 15, A.bitwise_and)
+            tt(ap("sma"), ap("ebase"), ap("i2"), A.add)
             cp(ap("eo16"), ap("sma"))
             act(ap("ew"), ind(ap("e"), ap("eo16")), F.Identity)
             for q0, q in reversed(CH):
@@ -719,8 +766,9 @@ def rank_program(g, core, T, topo):
             up, left = ap("upb", s_(2, 50)), ap("upb", s_(1, 49))
             o48 = ap("py", s_(0, 48))
             both = K["pex"] == 2
-            tabs = [("fb%d" % n, 0) for n in range(K["nfs"])] + [("fv%d" % n, 512) for n in range(K["nfv"] - 1, -both, -1)]
-            for n in range(K["nfs"]):
+            nb = K["nfs"] - (K["pex"] == 3)
+            tabs = [("fb%d" % n, 0) for n in range(nb)] + [("fv%d" % n, 512) for n in range(K["nfv"] - 1, -both, -1)]
+            for n in range(nb):
                 act(ap("fb%d" % n), ap("fs%d" % n, s_(512, 1280)), F.Copy)
             if t:
                 mms([(o48, idb(), ap("fl"), True, False)])
@@ -729,16 +777,21 @@ def rank_program(g, core, T, topo):
             if both:
                 ts(up, o48, 0.0, A.is_gt)
             else:
-                ts(ap("u2"), o48, -1e24, A.mult, ap("kt"), A.add)
+                act(ap("u2"), o48, F.Identity, ap("kt"), -1e24)
                 scan(ap("f2"), ap("kw"), ap("fv0", s_(512, 1280)), 0.0, A.mult, A.add)
-                tt(up, ap("f2", s_(15, 768, 16)), ap("u2"), A.is_gt)
+                late = ap("f2", s_(15, 768, 16))
+                if K["pex"] == 3:
+                    tt(ap("u2"), ap("u2"), late, A.subtract)
+                    scan(ap("f1"), ap("kw"), ap("fs%d" % nb, s_(512, 1280)), 0.0, A.mult, A.add)
+                    late = ap("f1", s_(15, 768, 16))
+                tt(up, late, ap("u2"), A.is_gt)
             o = ap("py", s_(512, 560))
             mms([(o, ap("tri"), up, True, False), (o, ap("ikn", s_(16, 144)), up, False, False),
                  (o, ap("trx"), left, False, False), (o, ap("ik", s_(16, 144)), left, False, True)])
             scan(ap("r0"), o, ap("z48"), 2047.0, A.add, A.add)
             tt(ap("r4"), ap("r0"), ap("dv"), A.min)
             cp(ap("pos"), ap("r4"))
-            ts(ap("r1"), ap("r0"), 192.0, A.is_ge, 1e25, A.mult)
+            act(ap("r1"), ap("r0"), F.Relu, -191.0 * 4096, 4096.0)
             tt(ap("r2"), ap("r0"), ap("r1"), A.max)
             tt(ap("r3"), ap("r2"), ap("dv"), A.min)
             cp(ap("put"), ap("r3"))

import math
from concourse.mybir import dt, AluOpType, AxisListType, ActivationFunctionType
A = AluOpType
F = ActivationFunctionType
B2, F4, I4, U2, H2 = "bfloat16", "float32", "int32", "uint16", "float16"
SB = lambda w, d: ("sbuf", [128] + w, d)
Q1 = (8, 8)
Q2 = (8, 8)
CH1, CH = [[(sum(z[:i]), q) for i, q in enumerate(z)] for z in (Q1, Q2)]
QM = max(Q2)
K = {
    "passes": 3,
    "tries": 2500,
    "moves": 2500,
    "starts": 5,
    "more": 9000,
    "joint": 1500,
    "prices": ((0.3, (1.4, 1.7, 1.9)), (0.3, (1.05, 0.85, 0.65)), (0.4, (1, 1, 1))),
    "heat": 250,
    "trust": False,
    "pex": 1,
    "nfs": 2,
    "nfv": 1,
    "wide": (),
    "spare": {(1, 1): "kb", (1, 3): "kb", (2, 2): "ka", (2, 3): "ka"},
    "sct": (),
    "sal": True,
    "seed": 61,
    "slack": 150,
    "alike": False,
    "order": "a0 b0 a1 b1 a2 b2 a3 b3 m0 c0 h0 c1 h1 m1 L d0 c2 d1 h2 c3 h3 d2 M0 d3 N M1 R",
    "vct": (0, 1),
    "fsb": False,
    "pd": (),
    "qd": (),
    "sc": (),
    "from": 0,
    "ps": (),
    "qv": ((2, 1),),
    "vflag": (2, 9),
    "vrep": 12,
    "vren": 1,
    "nren": 4,
    "vcmp": 24,
    "vput": 24,
}
X0, XB, XD, XE = 256, 768, 1536, 1808
BIG = 67108864.0
SCRATCH = {}


def declare(d, **kw):
    for names, w in kw.items():
        for n in names.split("_"):
            SCRATCH[n] = SB(list(w), d)


declare(B2, xa_xb=[XE], wtb=[1], dl0_dl1_dl2_rdl=[256], rep0_rep1_rep2_mb_e_gb_tb_tc=[4096], blk_tri_trx_rowg=[128], oneb=[max(128, 16 * QM)],
        kc1_kc3=[16 * max(Q1)], kc2=[16 * QM], dw_xs_iw_inw_lw_l2w_ww_ik_ikn=[160], rowr_rx_rn_fb0_fb1_kw_f1_f2=[768], upb=[50], fv0_fv1=[1552], gr_mx_mn=[3072])
declare(I4, coe=[1552], sue=[1280], lai=[4, 2, 4], di_dm=[32], thi_pi=[1], pr=[5], ai=[2], ui_ua_ub_uc_un=[256], i0_i1_i2=[16], mrg=[192])
declare(U2, ab16=[32], df=[512], dlist_ne16_nw16_eo16_own=[16], nw2=[32], pos_put=[48], sv=[192], s16_n16_ct=[256])
declare(F4, c2_c3=[512], kt_ow1_ow2_r4n=[1], ow3=[8], u2_r4=[48])
declare(B2, fl=[48])
declare(F4, abf1_abf2_rab1_rab2_abn0_abn1_abn2=[4, 2, 4], abd_al=[32], pf=[4], opar_par_npar_nopar_p16_thf_thq_thr_asum_wtf=[1], e8=[128], onef=[max(128, 16 * QM)],
        it=[1552], q16_dump_ebase_ald_nef_sma_junk=[16], v48_dv_z48_r0_r1_r2_r3=[48], kk=[512], kf_fdt_kk2=[256],
        fs0_fs1_cof=[1552], sgn=[32], cmv_cms=[XD], suf=[768])
declare(H2, p0_p1_n0_n1=[160], dfh_ta=[16, 2, 16], nh_na_ca=[8, 2, 16], nr_ch=[256])
SCRATCH["ab"] = SB([16, 16, 16], B2)
SCRATCH["ew"] = SB([256], B2)
for _c, (_q0, _q) in enumerate(CH):
    SCRATCH["eq%d" % _c] = SB([_q * (16 * _q + 2)], H2)
    SCRATCH["we%d" % _c] = SB([_q * (16 * _q + 2)], H2)
    SCRATCH["cwi%d" % _q] = SB([_q * (16 * _q + 2)], B2)
    SCRATCH["cw%d" % _q] = SB([_q * (16 * _q + 2)], H2)
SCRATCH["py"] = ("psum", [128, 1024], F4)
for _n in ("ka0", "ka1", "kb0", "kb1", "ps0", "ps1"):
    SCRATCH[_n] = ("psum", [128, 512], F4)

PACK = {}


def pack(buf, d, names):
    n = 0
    for x in names.split():
        w = SCRATCH.pop(x)[1][1]
        PACK[x] = (buf, n, w)
        n += w + w % 2
    SCRATCH[buf] = SB([n], d)


pack("pkf", F4, "pf opar par npar nopar p16 thf thq thr asum q16 dump ebase ald nef sma junk v48 dv z48 r0 r1 r2 r3 abd al kt ow1 ow2 ow3 u2 r4 wtf")
pack("pki", I4, "pi pr di dm ai i0 i1 i2")
pack("pku", U2, "dlist ne16 nw16 eo16 pos put ab16 nw2 own")
SEMAPHORES = ["cv", "cs", "ct", "cg", "ls", "rdl", "rab1", "rab2", "adl1", "adl2", "aab1", "aab2"] + ["ld%d" % n for n in range(8)] + ["o%d" % n for n in range(4)] + \
    ["ad%d" % n for n in range(1, 25)]
SIZE = {B2: 2, F4: 4, I4: 4, U2: 2, H2: 2}
COST = {"cyc": 0.83, "ga": 1.56, "sc": 3.8, "wake": 140, "mm": 10, "gdma": 800, "add": 4600, "far": 10000}


def relay_of(src, dst, topo):
    if topo.may_write(src, dst):
        return None
    c = [x for x in topo.cores_of(src) if x != src and topo.may_write(x, dst)]
    c.sort(key=lambda x: (topo.die(x) != topo.die(src), x))
    return c[0]


def send(g, T, topo, src, dst, out, in_, rsem):
    rid, pid = topo.addr(dst, src)
    g.remote_dma(out, in_, T.sem[rsem], T.sem.ls, pid, rid, topo.mask(src, dst))
    return len(topo.engines(src, dst))


def relay_program(g, core, T, topo, src):
    i = T.rank_of(src)
    d1, d2 = T.cores[(i + 1) % 8], T.cores[(i + 2) % 8]
    n1 = relay_of(src, d1, topo) == core
    n2 = relay_of(src, d2, topo) == core
    k = len(topo.engines(src, core))
    n = 0
    g.wait_ge(T.sem.rdl, k)
    if n1:
        n += send(g, T, topo, core, d1, T.dl1[:], T.rdl[:], "adl1")
    if n2:
        n += send(g, T, topo, core, d2, T.dl2[:], T.rdl[:], "adl2")
    if n1:
        for t in (1, 2):
            g.wait_ge(T.sem["rab%d" % t], k)
            n += send(g, T, topo, core, d1, T["abf%d" % t][:], T["rab%d" % t][:], "aab%d" % t)
    g.wait_ge(T.sem.ls, n)


def s_(a, b, c=None):
    return slice(a, b, c)


PLANS = {}


def plan(ops):
    start, end = [0.0] * len(ops), 0.0
    for t in range(3):
        mine = [i for i, o in enumerate(ops) if o["round"] == t]
        new = {i: k for k, i in enumerate(mine)}
        part = [dict(ops[i], **{x: {new[j] for j in ops[i][x] if j in new} for x in ("wait", "order")}) for i in mine]
        at = min(improve(part, K["tries"], K["moves"], K["seed"] + k) for k in range(K["starts"]))[1]
        _, at, last = improve(part, 0, K["more"], K["seed"], at)
        for i, t0 in zip(mine, at):
            start[i] = end + t0
        end += last + COST["wake"]
    _, start, K["end"] = improve(ops, 0, K["joint"], K["seed"], start)
    return start


def improve(ops, tries, moves, seed, given=None):
    n = len(ops)
    cost = [o["cost"] for o in ops]
    pred, succ = [[] for _ in ops], [[] for _ in ops]
    for i, o in enumerate(ops):
        for j in o["wait"] | o["order"]:
            lag = ops[j]["lat"] + COST["wake"] if j in o["wait"] else 0.0
            pred[i].append((j, lag))
            succ[j].append((i, lag))

    def place(urg, before, after, tail):
        left = [len(x) for x in before]
        free = [(urg[i], -i) for i in range(n) if not left[i]]
        busy, at = {e: [] for e in "VSTGYN"}, [0.0] * n
        while free:
            top = max(free)
            free.remove(top)
            i = -top[1]
            t0 = max([at[j] + cost[j] + lag for j, lag in before[i]], default=tail[i])
            line = busy[ops[i]["eng"]]
            k = len(line)
            while k and line[k - 1][1] > t0:
                k -= 1
            while k < len(line) and line[k][0] < t0 + cost[i]:
                t0 = max(t0, line[k][1])
                k += 1
            line.insert(k, (t0, t0 + cost[i]))
            at[i] = t0
            for j, _ in after[i]:
                left[j] -= 1
                if not left[j]:
                    free.append((urg[j], -j))
        return at

    lat, zero = [o["lat"] for o in ops], [0.0] * n
    urg = [0.0] * n
    for i in range(n - 1, -1, -1):
        urg[i] = cost[i] + max([urg[j] + lag for j, lag in succ[i]], default=lat[i])
    best = None
    if given:
        best = (0.0, given)
    for urg in (urg, [-i for i in range(n)]) if given is None else ():
        for _ in range(K["passes"]):
            at = place(urg, pred, succ, zero)
            end = max(at[i] + cost[i] + lat[i] for i in range(n))
            if best is None or end < best[0]:
                best = (end, at)
            back = place([at[i] + cost[i] for i in range(n)], succ, pred, lat)
            urg = [back[i] + cost[i] for i in range(n)]
    part = {}
    for i, o in enumerate(ops):
        part.setdefault((o["task"], o["eng"]), []).append(i)
    part = list(part.values())
    now = best
    for k in range(tries):
        pick = []
        for m in (len(part), 2001, 3, 5, 64, 1000):
            seed = (seed * 1103515245 + 12345) % 2147483648
            pick.append((seed >> 8) % m)
        urg = [-x for x in now[1]]
        some = part[pick[0]]
        if pick[3] < 2:
            some = some[pick[4] % len(some):][:1 + 2 * pick[3]]
        for i in some:
            urg[i] += (pick[1] - 1000) * (1, 3, 6)[pick[2]]
        at = place(urg, pred, succ, zero)
        end = max(at[i] + cost[i] + lat[i] for i in range(n))
        if end - now[0] <= -math.log((pick[5] + 1) / 1000) * K["slack"] * (1 - k / tries):
            now = (end, at)
            best = min(best, now)
    line = {}
    for i in sorted(range(n), key=lambda i: (best[1][i], i)):
        line.setdefault(ops[i]["eng"] if ops[i]["eng"] != "N" else i, []).append(i)

    def run():
        prev, nxt = [-1] * n, [-1] * n
        for s in line.values():
            for a, b in zip(s, s[1:]):
                prev[b], nxt[a] = a, b
        left = [len(pred[i]) + (prev[i] >= 0) for i in range(n)]
        free = [i for i in range(n) if not left[i]]
        seq = []
        while free:
            i = free.pop()
            seq.append(i)
            for j in after[i] + [nxt[i]] * (nxt[i] >= 0):
                left[j] -= 1
                if not left[j]:
                    free.append(j)
        if len(seq) < n:
            return None
        total, held = 0.0, []
        for weight, price in prices:
            fin, why = [0.0] * n, [-1] * n
            for i in seq:
                w = prev[i]
                t0 = fin[w] if w >= 0 else 0.0
                for j, lag in pred[i]:
                    if fin[j] + lag > t0:
                        t0, w = fin[j] + lag, j
                fin[i], why[i] = t0 + price[i], w
            end, i = max((fin[i] + lat[i], i) for i in range(n))
            total += weight * end
            while i >= 0:
                if why[i] >= 0 and why[i] == prev[i]:
                    held.append(i)
                i = why[i]
        return total, fin, held, end

    after = [[j for j, _ in x] for x in succ]
    prices = [(w, [o["fix"] + (o["cost"] - o["fix"]) * k[o["kind"]] for o in ops]) for w, k in K["prices"]]
    now = run()
    best = (now[0], [now[1][i] - cost[i] for i in range(n)], now[3])
    for k in range(moves):
        pick = []
        for m in (len(now[2]), 2, 5, 1000):
            seed = (seed * 1103515245 + 12345) % 2147483648
            pick.append((seed >> 8) % m)
        i = now[2][pick[0]]
        s = line[ops[i]["eng"]]
        old, p, d = list(s), s.index(i), (1, 1, 2, 3, 5)[pick[2]]
        if pick[1]:
            s.insert(max(0, p - d), s.pop(p))
        else:
            s.insert(p - 1 + d, s.pop(p - 1))
        new = run()
        if new and new[0] - now[0] <= -math.log((pick[3] + 1) / 1000) * K["heat"] * (1 - k / moves) / (1 if given is None else 4):
            now = new
            if now[0] < best[0]:
                best = (now[0], [now[1][i] - cost[i] for i in range(n)], now[3])
        else:
            s[:] = old
    return best


def rank_program(g, core, T, topo):
    rank = T.rank_of(core)
    if rank is None:
        for src in T.cores:
            if core in topo.cores_of(src):
                i = T.rank_of(src)
                if core in [relay_of(src, T.cores[(i + s) % 8], topo) for s in (1, 2)]:
                    relay_program(g, core, T, topo, src)
        return
    ops = []
    acc = {}
    task = ["", 0]
    cyc = COST["cyc"]

    def ap(name, *ix, p=None):
        if name in PACK:
            name, o, w = PACK[name]
            r = range(*(ix[0] if ix else slice(None)).indices(w))
            ix = (slice(o + r[0], o + r[-1] + 1, r.step),)
        sh = SCRATCH[name][1][1:]
        ix = list(ix) + [slice(None)] * (len(sh) - len(ix))
        st, m, n = 1, 1, 1
        for d in range(len(sh) - 1, -1, -1):
            x = ix[d]
            r = range(*x.indices(sh[d])) if isinstance(x, slice) else [x]
            if st == 1 and len(r) > 1 and r[1] - r[0] == 1:
                m = ((1 << len(r)) - 1) << r[0]
            else:
                m = sum(m << (v * st) for v in r)
            n *= len(r)
            st *= sh[d]
        ps = SCRATCH[name][0] == "psum"
        if ps:
            bank = (1 << 512) - 1
            m = sum(bank << b for b in range(0, st, 512) if m >> b & bank)
        return {"ap": T[name][tuple([slice(None) if p is None else slice(0, p)] + ix)], "k": [(name, m)], "n": n,
                "b": SIZE[SCRATCH[name][2]], "ps": ps, "ind": False}

    def ind(w, o):
        r = dict(w)
        r.update({"ap": w["ap"].indirect(o["ap"]), "k": w["k"] + o["k"], "n": 16 * o["n"], "ind": True})
        return r

    def op(eng, cost, outs, ins, fn, sem=None, val=1, lat=0.0):
        i = len(ops)
        wait, order = set(), set()
        rk = [k for o in ins for k in o["k"]] + [k for o in outs for k in o["k"][1:]]
        wk = [o["k"][0] for o in outs]
        for kind, keys in (("r", rk), ("w", wk)):
            for name, m in keys:
                psum = SCRATCH[name][0] == "psum"
                for (m2, j, k2) in acc.get(name, []):
                    if j == i or not m & m2:
                        continue
                    if kind == "r" and k2 == "r" and not (psum and ops[j]["eng"] != eng):
                        continue
                    if psum and eng == "T" and ops[j]["eng"] == "T":
                        order.add(j)
                    elif K["trust"] and kind == "w" and eng == ops[j]["eng"] and eng in "VS" and sem is None and ops[j]["sem"] is None:
                        order.add(j)
                    else:
                        wait.add(j)
        for kind, keys in (("r", rk), ("w", wk)):
            for name, m in keys:
                lst = acc.setdefault(name, [])
                if kind == "w":
                    lst[:] = [x for x in lst if x[0] & ~m]
                lst.append((m, i, kind))
        ops.append({"eng": eng, "cost": cost, "fn": fn, "wait": wait, "order": order - wait, "sem": sem, "val": val, "lat": lat,
                    "task": task[0] or (outs + ins)[0]["k"][0][0], "round": task[1],
                    "fix": {"V": 50, "S": 65, "T": cost / 8, "G": 150}.get(eng, cost) if sem is None else cost,
                    "kind": 2 if any(o["ind"] for o in outs) else 1 if any(o["ind"] for o in ins) else 0})
        return i

    def vcost(o, ins, tt=False):
        for x in [o] + ins:
            if x["ind"]:
                return 50 + cyc * x["n"] * (COST["sc"] if x is o else COST["ga"])
        if tt:
            return 50 + cyc * max(64, o["n"] * (1 if any(x["ps"] for x in ins) else 2))
        return 50 + cyc * max(64, (ins + [o])[0]["n"] * (0.5 if all(x["b"] == 2 for x in [o] + ins) else 1))

    def cp(o, i):
        op("V", vcost(o, [i]), [o], [i], lambda q: q.tensor_copy(o["ap"], i["ap"]))

    def tt(o, a, b, f):
        op("V", vcost(o, [a, b], True), [o], [a, b], lambda q: q.tensor_tensor(o["ap"], a["ap"], b["ap"], f))

    def ts(o, a, s1, f1, s2=None, f2=None):
        sc = [x for x in (s1, s2) if isinstance(x, dict)]
        v = [x["ap"] if isinstance(x, dict) else x for x in (s1, s2)]
        if f2 is None:
            op("V", vcost(o, [a]), [o], [a] + sc, lambda q: q.tensor_scalar(o["ap"], a["ap"], v[0], None, f1))
        else:
            op("V", vcost(o, [a]), [o], [a] + sc, lambda q: q.tensor_scalar(o["ap"], a["ap"], v[0], v[1], f1, f2))

    def scan(o, a, b, init, f1, f2):
        op("V", vcost(o, [a, b]), [o], [a, b], lambda q: q.tensor_tensor_scan(o["ap"], a["ap"], b["ap"], init, f1, f2))

    def trans(o, i):
        op("V", vcost(o, [i]), [o], [i], lambda q: q.transpose(o["ap"], i["ap"]))

    def fill(o, c):
        op("V", vcost(o, []), [o], [], lambda q: q.memset(o["ap"], c))

    def act(o, i, f, bias=None, scale=None, accum=None):
        cost = 65 + cyc * (i["n"] * COST["ga"] if i["ind"] else o["n"] * COST["sc"] if o["ind"] else max(64, i["n"]))
        if accum is not None:
            op("S", cost + 20, [o, accum], [i], lambda q: q.activation(o["ap"], i["ap"], f, accum_out=accum["ap"]))
        elif isinstance(bias, dict):
            op("S", cost, [o], [i, bias], lambda q: q.activation(o["ap"], i["ap"], f, bias["ap"], scale))
        elif scale is None:
            op("S", cost, [o], [i], lambda q: q.activation(o["ap"], i["ap"], f))
        else:
            op("S", cost, [o], [i], lambda q: q.activation(o["ap"], i["ap"], f, bias, scale))

    def mms(lst):
        cost = sum(COST["mm"] + cyc * max(64, x[2]["n"]) * (4 if x[2]["b"] == 4 else 1) for x in lst)

        def fn(q):
            for o, l, r, a, z in lst:
                m = q.matmul(o["ap"], l["ap"], r["ap"], a, z)
            return m
        op("T", cost, [x[0] for x in lst], [y for x in lst for y in x[1:3]], fn)

    def load(eng, buf, src, n, lat=2500):
        q = {"Y": g.sync, "S": g.scalar}[eng]
        return op(eng, 60, [buf], [], lambda _q: q.dma_start(buf["ap"], src), sem="ld%d" % n, val=16, lat=lat)

    def store(dst, buf, sem):
        op("Y", 60, [], [buf], lambda _q: g.sync.dma_start(dst, buf["ap"]), sem=sem, val=16, lat=2500)

    adds = [0]

    def add(o, i):
        adds[0] += 1
        op("G", COST["gdma"], [o], [o, i], lambda q: q.dma_start(o["ap"], i["ap"], accum_op=A.add), sem="ad%d" % adds[0], val=16, lat=COST["add"])

    def iota(o, pat, base, mult):
        if SCRATCH[o["k"][0][0]][2] == I4:
            op("G", 130 + 2 * cyc * o["n"], [o], [], lambda q: q.iota(o["ap"], pat, base, mult))
        else:
            op("G", 130 + 2 * cyc * o["n"], [o], [], lambda q: q.iota(o["ap"], pat, base, mult, allow_small_or_imprecise_dtypes=True))

    def select(o, i, pat, f, other, base, mult):
        op("G", 170 + 2 * cyc * o["n"], [o], [i], lambda q: q.affine_select(o["ap"], i["ap"], pat, f, other, base, mult))

    def gcopy(o, i):
        select(o, i, [[0, o["n"]]], A.is_ge, 0.0, 0, 0)

    loc = [0]

    def remote(stage, hops, cost=600):
        def fn(q):
            for dst, land, rsem in hops:
                loc[0] += send(g, T, topo, core, dst, T[land][:], stage["ap"], rsem)
        return op("G", cost, [], [stage], fn, sem="ls", val=0)

    def arrive(land, rsem, src, after, lat):
        rl = relay_of(src, core, topo)
        n = len(topo.engines(src if rl is None else rl, core))
        i = op("N", 0, [ap(land)], [], lambda q: None, sem=rsem, val=n, lat=lat)
        ops[i]["wait"].add(after)

    nxt, nx2, prv, pr2 = [T.cores[(rank + s) % 8] for s in (1, 2, -1, -2)]
    r1, r2 = relay_of(core, nxt, topo), relay_of(core, nx2, topo)
    a_ = s_(None, None)
    rcol = lambda: ap("pf", s_(0, 1))
    idb = lambda: ap("iw", s_(16, 144))
    idn = lambda: ap("inw", s_(16, 144))
    onto = lambda tab, r: ap(tab, s_(15 - r, 143 - r))
    flip = lambda tab, c1, gp: ap("%s%d" % (tab, c1), s_(16 - 16 * (gp - c1), 144 - 16 * (gp - c1)))
    flat = lambda bank, a, b: ap(bank, s_(a, b))
    turn = [0]

    def inputs():
        for n, (eng, buf, src, lat) in enumerate((
                ("Y", ap("dl0"), T.dl, 2500), ("Y", ap("coe", s_(0, 1280)), T.co, 4500), ("Y", ap("xa", s_(X0, XD)), T.x0, 5500),
                ("S", ap("lai", s_(0, 2)), T.la, 2500), ("S", ap("lai", s_(2, 4)), T.lb, 2500),
                ("Y", ap("sue"), T.su, 5000), ("Y", ap("wtb"), T.wt, 5000), ("Y", ap("thi", p=8), T.th, 5000))):
            i = load(eng, buf, src[:], n, lat)
            if n and ops[i - 1]["eng"] == eng:
                ops[i]["order"].add(i - 1)
            if n == 5:
                ops[i]["wait"].add(i - 3)

    def consts():
        iota(ap("pi"), [[0, 1]], 0, 1)
        iota(ap("dw"), [[1, 160]], -16, -1)
        iota(ap("rowr"), [[0, 48], [1, 16]], 0, 0)
        iota(ap("xs"), [[1, 160]], -15, 0)
        iota(ap("kc1"), [[0, max(Q1)], [2048, 16]], 0, 0)
        iota(ap("rowg"), [[16, 8], [0, 16]], 0, 0)
        iota(ap("p16"), [[0, 1]], 0, 16)
        for n, v in enumerate((15, 112, 16)):
            ts(ap("pr", s_(n, n + 1)), ap("pi"), v, A.bitwise_and)
        cp(ap("pf", s_(0, 3)), ap("pr", s_(0, 3)))
        half, first = ap("pf", s_(2, 3)), ap("pf", s_(1, 2))
        for n, a, b in (("par", 1, 0), ("opar", -1, 1), ("npar", -1, 0), ("nopar", 1, -1)):
            ts(ap(n), half, a / 16.0, A.mult, float(b), A.add)
        for n, c in (("p0", "opar"), ("p1", "par"), ("n0", "nopar"), ("n1", "npar")):
            ts(ap(n), ap("dw"), 0.0, A.is_equal, ap(c), A.mult)
        ts(ap("iw"), ap("dw"), 0.0, A.is_equal)
        ts(ap("inw"), ap("dw"), 0.0, A.is_equal, -1.0, A.mult)
        ts(ap("lw"), ap("xs"), first, A.is_equal, 32768.0, A.mult)
        ts(ap("l2w"), ap("xs"), first, A.is_equal, -32768.0, A.mult)
        act(ap("wtf"), ap("wtb"), F.Copy)
        ts(ap("ww"), ap("xs"), first, A.is_equal, ap("wtf"), A.mult)
        ts(ap("blk"), ap("rowg"), first, A.is_equal)
        fill(ap("kc3"), -16777216.0)
        act(ap("rx"), ap("rowr"), F.Sign)
        act(ap("rn"), ap("rx"), F.Silu, BIG, -BIG)
        ops[-1]["cost"] += 1300
        cp(ap("thf", p=8), ap("thi", p=8))
        ts(ap("e8", p=8), ap("rowg", p=8), ap("p16", p=8), A.is_equal)
        o = ap("ps0", s_(0, 1))
        mms([(o, ap("e8", p=8), ap("thf", p=8), True, True)])
        ts(ap("thq"), o, 32768.0, A.mult, -16777216.0, A.add)
        iota(ap("kc2"), [[0, QM], [2048, 16]], -32768, 0)
        iota(ap("q16"), [[16, 16]], 1296, 0)
        ts(ap("dump"), ap("q16"), rcol(), A.add)
        ts(ap("ebase"), ap("dump"), 16.0, A.mult, -16.0 * 1296, A.add)
        iota(ap("it"), [[1, 1552]], 0, 0)
        iota(ap("coe", s_(1280, 1552)), [[1, 272]], 1280, 0)
        for c, (q0, q) in enumerate(CH):
            fill(ap("eq%d" % c, s_(0, None, 16 * q + 2)), 0.0)
        for q in sorted({q for _, q in CH}):
            w, n = 16 * q + 2, q * (16 * q + 2)
            iota(ap("cwi%d" % q), [[-16, q], [1, w]], -1, 0)
            ts(ap("cw%d" % q), ap("cwi%d" % q), rcol(), A.is_equal, 4096.0, A.mult)
            fill(ap("cw%d" % q, s_(0, n, w)), -60000.0)
            fill(ap("cw%d" % q, s_(w - 1, n, w)), -4096.0)
        iota(ap("oneb"), [[0, max(128, 16 * QM)]], 1, 0)
        iota(ap("onef"), [[0, max(128, 16 * QM)]], 1, 0)
        iota(ap("z48"), [[0, 48]], 0, 0)
        iota(ap("upb", s_(0, 2)), [[0, 2]], 0, 0)
        iota(ap("v48"), [[16, 48]], XB, 0)
        ts(ap("dv"), ap("v48"), rcol(), A.add)
        select(ap("tri"), ap("blk"), [[1, 128]], A.is_ge, 0.0, 0, -1)
        select(ap("trx"), ap("blk"), [[-1, 128]], A.is_gt, 0.0, 0, 1)
        act(ap("ik"), ap("iw"), F.Identity, 0.0, 2048.0)
        act(ap("ikn"), ap("iw"), F.Identity, 0.0, -2048.0)
        for x in ("xa", "xb"):
            iota(ap(x, s_(192, X0)), [[0, X0 - 192]], 0, 0)
        ts(ap("suf"), ap("sue", s_(512, 1280)), 64.0, A.add)
        if K["sct"]:
            cp(ap("cof", s_(0, 512)), ap("coe", s_(0, 512)))
            iota(ap("cof", s_(512, 1552)), [[1, 1040]], 512, 0)
        act(ap("r4n"), rcol(), F.Identity, 0.0, -4.0)
        act(ap("kw"), ap("rowr"), F.Relu, ap("r4n"), 4.0)
        scan(ap("junk"), ap("kw", s_(0, 16)), ap("oneb", s_(0, 16)), 0.0, A.mult, A.add)
        ts(ap("kt"), ap("junk", s_(15, 16)), 0.5, A.mult)
        for q in sorted({CH[c][1] for c in K["vct"]}):
            ts(ap("pr", s_(3, 4)), ap("pi"), q - 1, A.bitwise_and)
            ts(ap("pr", s_(4, 5)), ap("pi"), q.bit_length() - 1, A.arith_shift_right, 16 // q - 1, A.bitwise_and)
            ts(ap("ow1"), ap("pr", s_(3, 4)), 32.0, A.mult, half, A.add)
            tt(ap("ow2"), ap("ow1"), ap("pr", s_(4, 5)), A.add)
            iota(ap("ow3", s_(0, q)), [[16 // q, q]], 0, 0)
            ts(ap("own", s_(q, 2 * q)), ap("ow3", s_(0, q)), ap("ow2"), A.add)

    def reps(t):
        for k in range(16):
            o, i = ap("rep%d" % t, s_(k, 4096, 16)), ap("dl%d" % t)
            if t:
                gcopy(o, i)
            elif k < K["vrep"]:
                cp(o, i)
            else:
                act(o, i, F.Copy)

    def rnd(t, ahead=False):
        rep, last = "rep%d" % t, t == 2
        cur, new = ("xa", "xb") if t % 2 == 0 else ("xb", "xa")
        xall, base = ap(cur, s_(X0, XD)), ap(cur, s_(X0, XB))
        oldn = "abf%d" % t if t else "lai"
        old = ap(oldn)
        cands = lambda side, h: ap("df", s_(256 * (h % 2) + 64 * (2 * side + h // 2), 256 * (h % 2) + 64 * (2 * side + h // 2) + 64))
        thr = ap("thr") if t else ap("thq")

        def before():
            for c1 in (0, 1):
                cp(ap("ab16", s_(16 * c1, 16 * c1 + 16)), ap(oldn, a_, c1))
            cp(ap("df"), ind(ap("coe", s_(0, 1280)), ap("ab16")))
            for c1 in (0, 1):
                cp(ap("dfh", a_, c1), ap("df", s_(256 * c1, 256 * c1 + 256)))
            trans(ap("ta"), ap("dfh"))
            mms([(ap("ka1", s_(64 * h, 64 * h + 64)), flip(tab, h % 2, gp), ap("ta", s_(b + h // 2 * 4, b + h // 2 * 4 + 4), gp),
                  tab == "p" and gp == 0, tab == "n" and gp == 1) for h in range(4) for tab, b in (("p", 8), ("n", 0)) for gp in (0, 1)])
            act(ap("fdt"), ap("ka1", s_(0, 256)), F.Copy)
            for c, (q0, q) in enumerate(CH1):
                kp, b, x = "ka%d" % c, s_(q0 // 2, (q0 + q) // 2), s_(0, 16 * q)
                kq = flat(kp, 0, 16 * q)
                mms([(kq, idb(), ap("kc3", x), True, False), (kq, idb(), ap("kc1", x), False, False)] +
                    [(flat(kp, 64 * c1, 64 * c1 + 64), flip("p", c1, gp), ap("ta", b, gp), False, False) for c1 in (0, 1) for gp in (0, 1)])

        def clear():
            for x in ["fs%d" % n for n in range(K["nfs"])] + ["fv%d" % n for n in range(K["nfv"])]:
                iota(ap(x, s_(512, 1280)), [[0, 768]], 0, 0)
            iota(ap("cmv", s_(0, 192)), [[0, 192]], 0, 0)
            if K["vcmp"] < 48:
                iota(ap("cms", s_(0, 192)), [[0, 192]], 0, 0)

        def two(i, a, na, b, nb, lo, spare=None):
            o = ap("%s%d" % (spare, i)) if spare else ap("py", s_(512 * i, 512 * i + 512))
            mms([(o, l, ap(n, s_(lo + 512 * i, lo + 512 * i + 512)), z == 0, z == 1) for z, (l, n) in enumerate(((a, na), (b, nb)))])
            return o

        def moved(step, h, off, dst):
            lo = 1024 * h
            x = s_(lo, lo + 1024)
            if (step, h) in K["ps"]:
                act(ap("tb", x), ind(xall, off), F.Identity)
                for i in (0, 1):
                    ts(ap(dst, s_(lo + 512 * i, lo + 512 * i + 512)), two(i, idb(), "tb", idb(), rep, lo), 0.0, A.max, 63.0, A.min)
            else:
                if (step, h) in K["pd"] and t >= K["from"]:
                    act(ap("tb", x), ind(xall, off), F.Identity)
                    add(ap("tb", x), ap(rep, x))
                else:
                    tt(ap("tb", x), ind(xall, off), ap(rep, x), A.add)
                if (step, h) in K["sc"]:
                    act(ap("tc", x), ap("tb", x), F.Relu, 63.0, -1.0)
                    act(ap(dst, x), ap("tc", x), F.Relu, 63.0, -1.0)
                else:
                    ts(ap(dst, x), ap("tb", x), 0.0, A.max, 63.0, A.min)

        def distance(step, h, w, off, m, tab, kp, q0, q):
            x = s_(1024 * h, 1024 * h + 1024)
            if (step, h) in K["qv"]:
                tt(ap("gb", x), ind(w, off), ap(m, x), A.subtract)
                act(ap("ab", s_(4 * h, 4 * h + 4)), ap("gb", x), F.Abs)
            elif (step, h) in K["qd"] and t >= K["from"]:
                act(ap("gb", x), ind(w, off), F.Identity, 0.0, -1.0)
                add(ap("gb", x), ap(m, x))
                act(ap("ab", s_(4 * h, 4 * h + 4)), ap("gb", x), F.Abs)
            else:
                task[0] += "g"
                act(ap("gb", x), ind(w, off), F.Identity)
                task[0] = task[0][:-1]
                for i in (0, 1):
                    act(ap("ab", s_(4 * h + 2 * i, 4 * h + 2 * i + 2)), two(i, idb(), "gb", idn(), m, 1024 * h, K["spare"].get((step, h))), F.Abs)
            o = flat(kp, 64 * h - 16 * q0, 64 * h - 16 * q0 + 64)
            end = 4 * h + 4 == q0 + q
            mms([(o, onto(tab, r), ap("ab", s_(4 * h, 4 * h + 4), r), False, end and r == 15) for r in range(16)])

        def first(h):
            moved(1, h, cands(0, h), "mb")

        def second(h):
            distance(1, h, xall, cands(1, h), "mb", "lw", "ka%d" % (h // 2), *CH1[h // 2])

        def least(c):
            q0, q = CH1[c]
            x, q8, kq = s_(16 * q0, 16 * (q0 + q)), s_(q0, q0 + q), flat("ka%d" % c, 0, 16 * q)
            ends = ap("kk", s_(16 * q0 + 15, 16 * (q0 + q), 16))
            scan(ap("kk", x), ap("rn", s_(0, 16 * q)), kq, 0.0, A.add, A.min)
            cp(ap("di", q8), ends)
            ts(ap("dm", q8), ap("di", q8), 2047, A.bitwise_and)
            cp(ap("dlist", q8), ap("dm", q8))
            cp(ap("s16", x), ind(ap("sue"), ap("dlist", q8)))
            tt(ap("kf", x), kq, ap("fdt", x), A.add)
            if c == len(CH1) - 1:
                act(ap("sgn", s_(0, 16)), ap("kk", s_(15, 256, 16)), F.Sign, thr, -1.0)
                for y in (0, 16):
                    act(ap("al", s_(y, y + 16)), ap("sgn", s_(0, 16)), F.Relu)
                act(ap("ald"), ap("al", s_(0, 16)), F.Identity, 16777216.0, 1280.0 - 33554432.0)

        def lanes():
            scan(ap("kk", s_(256, 512)), ap("rn", s_(0, 256)), ap("kf"), 0.0, A.add, A.min)
            cp(ap("di", s_(16, 32)), ap("kk", s_(271, 512, 16)))
            ts(ap("dm", s_(16, 32)), ap("di", s_(16, 32)), 2047, A.bitwise_and)
            abn = ap("abn%d" % t)
            tt(ap("abd"), ap("dm"), old, A.subtract)
            tt(ap("abd"), ap("abd"), ap("al"), A.mult)
            tt(abn, ap("abd"), old, A.add)
            if last:
                store(T.ya[:], ap("abn2", s_(0, 2)), "o0")
                store(T.yb[:], ap("abn2", s_(2, 4)), "o1")
                return
            k = t + 1
            i = remote(abn, [(nxt, "abf%d" % k, "aab%d" % k) if r1 is None else (r1, "rab%d" % k, "rab%d" % k)])
            arrive("abf%d" % k, "aab%d" % k, prv, i, COST["far"])
            act(ap("junk"), ap("al", s_(0, 16)), F.Copy, accum=ap("asum"))

        def threshold():
            o = ap("ps1", s_(0, 1))
            mms([(o, ap("onef", s_(0, 128)), ap("asum"), True, True)])
            ts(ap("ai", s_(0, 1)), o, -1.0, A.mult, 2048.0, A.add)
            ts(ap("ai", s_(1, 2)), ap("ai", s_(0, 1)), 63, A.bitwise_and)
            ts(ap("thr"), ap("ai", s_(1, 2)), 32768.0, A.mult, ap("thq"), A.add)

        def third(h):
            moved(2, h, ap("s16", s_(64 * h, 64 * h + 64)), "e")
            o = ap("ps%d" % (h // 2), s_(64 * (h % 2), 64 * (h % 2) + 64)) if h // 2 in K["wide"] else ap("ps%d" % (h % 2), s_(0, 64))
            mms([(o, onto("ww", j), ap("e", s_(1024 * h + j, 1024 * h + 1024, 16)), j == 0, j == 15) for j in range(16)])

        def spot(h):
            x, u = s_(64 * h, 64 * h + 64), ap("ps%d" % (h % 2), s_(0, 64))
            if h // 2 in K["wide"]:
                if h % 2 == 0:
                    return
                x, u = s_(64 * h - 64, 64 * h + 64), ap("ps%d" % (h // 2), s_(0, 128))
            cp(ap("ui", x), u)
            ts(ap("ua", x), ap("ui", x), 4095, A.bitwise_and)
            ts(ap("ub", x), ap("ua", x), 1184.0, A.add)
            tt(ap("uc", x), ap("ua", x), ap("ub", x), A.mult)
            ts(ap("un", x), ap("uc", x), 5, A.arith_shift_right, 511, A.bitwise_and)
            cp(ap("n16", x), ap("un", x))

        def fourth(h):
            c = max(c for c, (q0, q) in enumerate(CH) if q0 <= 4 * h)
            q0, q = CH[c]
            kp, b = "kb%d" % (c % 2), s_(q0 // 2, (q0 + q) // 2)
            if 4 * h == q0:
                mms([(flat(kp, 0, 16 * q), idn(), ap("kc3", s_(0, 16 * q)), True, False), (flat(kp, 0, 16 * q), idb(), ap("kc2", s_(0, 16 * q)), False, False)])
            if 4 * h + 4 == q0 + q:
                for c1 in (0, 1):
                    cp(ap("nh", b, c1), ap("n16", s_(16 * q0 + 8 * q * c1, 16 * q0 + 8 * q * (c1 + 1))))
                trans(ap("na", b), ap("nh", b))
                mms([(flat(kp, 8 * q * c1, 8 * q * (c1 + 1)), flip("p", c1, gp), ap("na", b, gp), False, False) for c1 in (0, 1) for gp in (0, 1)])
            distance(2, h, base, ap("n16", s_(64 * h, 64 * h + 64)), "e", "l2w", kp, q0, q)

        def largest(c):
            q0, q = CH[c]
            w, kp = 16 * q, "kb%d" % (c % 2)
            x, b, q8 = s_(16 * q0, 16 * (q0 + q)), s_(q0 // 2, (q0 + q) // 2), s_(q0, q0 + q)
            scan(ap("kk2", x), ap("rn", s_(0, w)), flat(kp, 0, w), 0.0, A.add, A.min)
            eq, we, v = "eq%d" % c, "we%d" % c, w + 2
            tt(ap("i0", q8), ap("kk2", s_(16 * q0 + 15, 16 * (q0 + q), 16)), ap("ald", q8), A.min)
            ts(ap("i1", q8), ap("i0", q8), 2047, A.bitwise_and)
            cp(ap("ne16", q8), ap("i1", q8))
            cp(ap("nef", q8), ap("i1", q8))
            cp(ap(eq, s_(v - 1, q * v, v)), ap("i1", q8))
            cp(ap("nr", x), ind(ap("it"), ap("ne16", q8)))
            for k in range(q):
                y = s_(q0 + k, q0 + k + 1)
                ts(ap(eq, s_(v * k + 1, v * k + v - 1)), ap("nr", x), ap("nef", y), A.is_equal, ap("dump", y), A.mult)
            scan(ap(we), ap("cw%d" % q), ap(eq), 0.0, A.add, A.max)
            cp(ap("nw16", q8), ap(we, s_(v - 1, q * v, v)))
            if c in K["vct"]:
                y = s_(32 * q0, 32 * (q0 + q))
                for c1 in (0, 1):
                    cp(ap("nw2", s_(2 * q0 + c1, 2 * (q0 + q), 2)), ap(we, s_(v - 1, q * v, v)))
                if c in K["sct"]:
                    act(ap("c2", y), ind(ap("cof"), ap("nw2", s_(2 * q0, 2 * (q0 + q)))), F.Identity)
                else:
                    cp(ap("c2", y), ind(ap("coe"), ap("nw2", s_(2 * q0, 2 * (q0 + q)))))
                trans(ap("c3", y), ap("c2", y))
                cp(ap("ct", x), ind(ap("c3", y), ap("own", s_(q, 2 * q))))
            else:
                cp(ap("ch", x), ind(ap("coe"), ap("nw16", q8)))
                trans(ap("ca", b), ap("ch", x))
                pz = "ps%d" % (c % 2)
                mms([(ap(pz, s_(k, w, q)), flip("p", k % 2, gp), ap("ca", (q0 + k) // 2, gp), gp == 0, gp == 1) for k in range(q) for gp in (0, 1)])
                cp(ap("ct", x), ap(pz, s_(0, w)))
            task[0] = "F%d" % c
            for k in range(16):
                row = ap("ct", s_(16 * q0 + q * k, 16 * q0 + q * k + q))
                if k < K["vflag"][c]:
                    cp(ind(ap("fv%d" % ((K["vflag"][c] - 1 - k) % K["nfv"])), row), ap("oneb", s_(0, w)))
                else:
                    act(ind(ap("fs%d" % (k % K["nfs"])), row), ap("onef", s_(0, w)), F.Silu)

        def step3():
            ts(ap("i2"), ap("i0"), 11, A.arith_shift_right, 15, A.bitwise_and)
            tt(ap("sma"), ap("ebase"), ap("i2"), A.add)
            cp(ap("eo16"), ap("sma"))
            act(ap("ew"), ind(ap("e"), ap("eo16")), F.Identity)
            for q0, q in reversed(CH):
                cp(ind(ap(cur, s_(X0, XE)), ap("nw16", s_(q0, q0 + q))), ap("ew", s_(16 * q0, 16 * (q0 + q))))
            if last:
                store(T.yx[:, 0:512], base, "o2")
            else:
                gcopy(ap(new, s_(X0, XB)), base)

        def step4():
            up, left = ap("upb", s_(2, 50)), ap("upb", s_(1, 49))
            o48 = ap("py", s_(0, 48))
            both = K["pex"] == 2
            nb = K["nfs"] - (K["pex"] == 3)
            tabs = [("fb%d" % n, 0) for n in range(nb)] + [("fv%d" % n, 512) for n in range(K["nfv"] - 1, -both, -1)]
            for n in range(nb):
                act(ap("fb%d" % n), ap("fs%d" % n, s_(512, 1280)), F.Copy)
            if t:
                mms([(o48, idb(), ap("fl"), True, False)])
            for n, (x, a) in enumerate(tabs):
                mms([(o48, onto("lw", r), ap(x, s_(a + r, a + 768, 16)), r + n + t == 0, r == 15 and n == len(tabs) - 1) for r in range(16)])
            if both:
                ts(up, o48, 0.0, A.is_gt)
            else:
                act(ap("u2"), o48, F.Identity, ap("kt"), -1e24)
                scan(ap("f2"), ap("kw"), ap("fv0", s_(512, 1280)), 0.0, A.mult, A.add)
                late = ap("f2", s_(15, 768, 16))
                if K["pex"] == 3:
                    tt(ap("u2"), ap("u2"), late, A.subtract)
                    scan(ap("f1"), ap("kw"), ap("fs%d" % nb, s_(512, 1280)), 0.0, A.mult, A.add)
                    late = ap("f1", s_(15, 768, 16))
                tt(up, late, ap("u2"), A.is_gt)
            o = ap("py", s_(512, 560))
            mms([(o, ap("tri"), up, True, False), (o, ap("ikn", s_(16, 144)), up, False, False),
                 (o, ap("trx"), left, False, False), (o, ap("ik", s_(16, 144)), left, False, True)])
            scan(ap("r0"), o, ap("z48"), 2047.0, A.add, A.add)
            tt(ap("r4"), ap("r0"), ap("dv"), A.min)
            cp(ap("pos"), ap("r4"))
            act(ap("r1"), ap("r0"), F.Relu, -191.0 * 4096, 4096.0)
            tt(ap("r2"), ap("r0"), ap("r1"), A.max)
            tt(ap("r3"), ap("r2"), ap("dv"), A.min)
            cp(ap("put"), ap("r3"))
            if not last:
                tt(ap("fl"), ap("r1"), up, A.min)
            n = K["vcmp"]
            cp(ind(ap("cmv"), ap("pos", s_(0, n))), ap("suf", s_(0, 16 * n)))
            if n < 48:
                act(ind(ap("cms"), ap("pos", s_(n, 48))), ap("suf", s_(16 * n, 768)), F.Silu)
                tt(ap("mrg"), ap("cmv", s_(0, 192)), ap("cms", s_(0, 192)), A.add)
                ts(ap("sv"), ap("mrg"), -64.0, A.add)
            else:
                ts(ap("sv"), ap("cmv", s_(0, 192)), -64.0, A.add)
            n = 192 // K["nren"]
            for i in range(K["nren"]):
                x = s_(16 * n * i, 16 * n * (i + 1))
                src = ind(xall, ap("sv", s_(n * i, n * (i + 1))))
                if i < K["vren"]:
                    ts(ap("gr", x), src, 0.5, A.mult, 0.375, A.add)
                else:
                    act(ap("gr", x), src, F.Identity, 0.375, 0.5)
                for j in range(16 * n * i, 16 * n * (i + 1), 768):
                    z = s_(j, min(j + 768, 16 * n * (i + 1)))
                    y = s_(0, z.stop - z.start)
                    scan(ap("mx", z), ap("rx", y), ap("gr", z), 0.0, A.mult, A.max)
                    scan(ap("mn", z), ap("rn", y), ap("gr", z), 0.0, A.add, A.min)
                o = ap("py", s_(n * i, n * (i + 1)))
                mms([(o, idb(), ap(m, s_(16 * n * i + 15, 16 * n * (i + 1), 16)), m == "mx", m == "mn") for m in ("mx", "mn")])
            ts(ap(cur, s_(0, 192)), ap("py", s_(0, 192)), 12582912.0, A.add, 12582913.0, A.subtract)
            n = K["vput"]
            win = ap(cur, s_(0, XD))
            cp(ap(new, s_(XB, XB + 16 * n)), ind(win, ap("put", s_(0, n))))
            if n < 48:
                act(ap(new, s_(XB + 16 * n, XD)), ind(win, ap("put", s_(n, 48))), F.Identity)
            if last:
                store(T.yx[:, 512:1280], ap(new, s_(XB, XD)), "o3")

        if ahead:
            return before()
        task[:] = ["clear", t]
        clear()
        tasks = {"a": first, "b": second, "m": least, "c": third, "h": spot, "d": fourth, "M": largest}
        for x in K["order"].split():
            task[0] = x
            if x[0] in tasks:
                tasks[x[0]](int(x[1]))
            elif x == "L":
                lanes()
            elif x == "N" and not last:
                threshold()
                rnd(t + 1, True)
            elif x == "R":
                step3()
        task[0] = "D"
        step4()
        task[0] = "rep"

    inputs()
    consts()
    reps(0)
    hops = []
    if r1 is None:
        hops.append((nxt, "dl1", "adl1"))
    if r2 is None:
        hops.append((nx2, "dl2", "adl2"))
    for r in sorted({x for x in (r1, r2) if x is not None}):
        hops.append((r, "rdl", "rdl"))
    snt = remote(ap("dl0"), hops, 4000)
    arrive("dl1", "adl1", prv, snt, COST["far"] + 8000)
    arrive("dl2", "adl2", pr2, snt, COST["far"] + 8000)
    rnd(0, True)
    rnd(0)
    reps(1)
    rnd(1)
    reps(2)
    rnd(2)

    if len(ops) not in PLANS:
        PLANS[len(ops)] = plan(ops)
    start = PLANS[len(ops)]
    for o, t0 in zip(ops, start):
        o["fin"] = t0 + o["cost"] + o["lat"]
    seq = sorted(range(len(ops)), key=lambda i: (start[i], i))

    queues = {"V": g.vector, "S": g.scalar, "T": g.tensor, "G": g, "Y": g.sync, "N": None}
    esem = {"V": "cv", "S": "cs", "T": "ct", "G": "cg"}
    count = {}
    known = {e: {} for e in queues}
    final = {}
    for i in seq:
        o = ops[i]
        e, q = o["eng"], queues[o["eng"]]
        if e != "N":
            for j in sorted(o["wait"], key=lambda x: -ops[x]["fin"]):
                s, v = ops[j]["done"]
                if v and known[e].get(s, 0) < v:
                    q.wait_ge(T.sem[s], v)
                    known[e][s] = v
                    for a, b in ops[j]["clk"].items():
                        known[e][a] = max(known[e].get(a, 0), b)
        ins = o["fn"](q)
        if o["sem"] is None:
            s = esem[e]
            count[s] = count.get(s, 0) + 1
            ins.then_inc(T.sem[s], 1)
            o["done"] = (s, count[s])
            final[s] = count[s]
        else:
            o["done"] = (o["sem"], o["val"])
            if o["val"]:
                if e != "N":
                    ins.then_inc(T.sem[o["sem"]], o["val"])
                final[o["sem"]] = o["val"]
        o["clk"] = dict(known[e]) if e != "N" else {}
    if loc[0]:
        final["ls"] = loc[0]
    for s in sorted(final):
        g.wait_ge(T.sem[s], final[s])
